import numpy as np
import ml_dtypes


def mxq(x, axis, fmt="e4m3"):
    dtype, down = {"e4m3": (ml_dtypes.float8_e4m3fn, 7), "e5m2": (ml_dtypes.float8_e5m2, 14)}[fmt]
    v = np.moveaxis(np.asarray(x, np.float32).astype(ml_dtypes.bfloat16).astype(np.float64), axis, -1)
    blocks = v.reshape(v.shape[:-1] + (-1, 32))
    amax = np.abs(blocks).max(-1, keepdims=True)
    byte = np.maximum(np.where(amax > 0, np.frexp(amax)[1] - 1 + 127, 0) - down, 1)
    scale = np.exp2(byte - 127.0)
    codes = (blocks / scale).astype(np.float32).astype(dtype).astype(np.float64)
    return np.moveaxis((codes * scale).reshape(v.shape), -1, axis)


WIDE = False


def mx_kscale(k):
    if not WIDE:
        return np.ones(k)
    levels = np.array([10, -10, 5, -5, 0])
    if k % 512:
        return np.exp2(np.random.permutation(np.resize(levels, k // 32))).repeat(32)
    a = np.empty((k // 512, 16))
    for p in range(k // 512):
        a[p, :8] = np.random.permutation(np.resize(levels, 8))
        for g in range(8):
            far = levels[np.abs(levels - a[p, g]) >= 10]
            a[p, g + 8] = far[np.random.randint(len(far))]
    return np.exp2(a.ravel()).repeat(32)


def f64(x):
    return np.asarray(x).astype(np.float64)


def striped(idx):
    return np.tile(idx.reshape(-1, 16).T, (8, 1)).astype(np.uint16)


def unstriped(offs):
    return offs[:16].T.reshape(-1).astype(np.int64)


E2M1 = np.array([0.0, 0.5, 1.0, 1.5, 2.0, 3.0, 4.0, 6.0, -0.0, -0.5, -1.0, -1.5, -2.0, -3.0, -4.0, -6.0])


def pack_weight(w, fmt):
    k, n = w.shape
    w = f64(np.asarray(w, np.float32).astype(ml_dtypes.bfloat16)).reshape(k // 32, 32, n)
    amax = np.abs(w).max(1)
    if fmt == "e4m3":
        byte = np.frexp(amax)[1] - 1 + 127 - 7
    else:
        mant, ex = np.frexp(amax / 6.0)
        byte = np.where(mant > 0.5, ex, ex - 1) + 127
    byte = np.clip(np.where(amax > 0, byte, 1), 1, 254)
    scaled = (w * np.exp2(127.0 - byte)[:, None, :]).reshape(k, n).astype(np.float32)
    by_word = np.ascontiguousarray(scaled.reshape(k // 512, 128, 4, n).transpose(0, 1, 3, 2))
    if fmt == "e4m3":
        words = by_word.astype(ml_dtypes.float8_e4m3fn).view(np.uint8)
    else:
        c = by_word.astype(ml_dtypes.float4_e2m1fn).view(np.uint8) & 0xF
        words = (c[..., 0::2] | (c[..., 1::2] << 4)).reshape(k // 512, 128, 2 * n)
    return np.ascontiguousarray(words), np.ascontiguousarray(byte.astype(np.uint8).reshape(k // 512, 16, n))


def unpack_weight(words, scales, fmt):
    g, _, n = scales.shape
    words = np.ascontiguousarray(words).reshape(g, 128, n, -1)
    if fmt == "e4m3":
        vals = words.view(ml_dtypes.float8_e4m3fn).astype(np.float64)
    else:
        nib = np.empty((g, 128, n, 4), np.uint8)
        nib[..., 0::2] = words & 0xF
        nib[..., 1::2] = words >> 4
        vals = E2M1[nib]
    vals = vals * np.repeat(np.exp2(scales.astype(np.float64) - 127.0), 8, axis=1)[..., None]
    return vals.transpose(0, 1, 3, 2).reshape(g * 512, n)


def gelu(v):
    return 0.5 * v * (1.0 + np.tanh(np.sqrt(2.0 / np.pi) * (v + 0.044715 * v**3)))


K, T, S, T2, H, N, P = 1024, 2048, 1024, 2048, 512, 512, 128

def setup_inputs():
    n = np.random.standard_normal
    s = mx_kscale(K)[:, None]
    u = mx_kscale(H)[:, None]
    tab_words, tab_scales = pack_weight(n((K, T)) * s, "e4m3")
    w2_words, w2_scales = pack_weight(n((K, H)) / np.sqrt(K) / s * u.T, "e2m1")
    return {
        "tab_words": tab_words, "tab_scales": tab_scales,
        "offs": striped(np.random.permutation(T)[:S]),
        "w1": (n((K, H)) / np.sqrt(K) / s * u.T).astype(np.float32),
        "w2_words": w2_words, "w2_scales": w2_scales,
        "wgs": np.exp(0.3 * n((P, S))).astype(np.float32),
        "offs2": striped(np.random.permutation(T2)[:S]),
        "old": (n((H, T2)) * u).astype(np.float32),
        "wf": (n((H, N)) / np.sqrt(H) / u).astype(np.float32),
        "bf": (0.5 * n(N)).astype(np.float32),
    }

def reference(tab_words, tab_scales, offs, w1, w2_words, w2_scales, wgs, offs2, old, wf, bf):
    v = unpack_weight(tab_words, tab_scales, "e4m3")[:, unstriped(offs)]
    w1q = mxq(f64(w1), 0, "e4m3")
    w2 = unpack_weight(w2_words, w2_scales, "e2m1")
    h = np.minimum(w1q.T @ v, w2.T @ v)
    page = np.zeros((H, T2))
    page[:, unstriped(offs2)] = np.tile(f64(wgs), (H // P, 1)) * h
    z = np.minimum(page, f64(old))
    zq = mxq(z, 0, "e4m3")
    wfq = mxq(f64(wf), 0, "e4m3")
    return np.maximum((wfq.T @ zq) + f64(bf)[:, None], 0.0)

@@ -1,0 +1,196 @@
+from contextlib import ExitStack
+
+import concourse.mybir as mybir
+
+K, T, S, T2, H, N = 1024, 2048, 1024, 2048, 512, 512
+P = 128
+PACK = 4
+PASSES = K // (P * PACK)
+BANK = 512
+HALVES = S // BANK
+CHUNKS = [256, 512, 512, 512, 256]
+
+FLOPS = 2 * (2 * K * H * S + H * N * T2)
+
+F32 = mybir.dt.float32
+BF16 = mybir.dt.bfloat16
+I32 = mybir.dt.int32
+U32 = mybir.dt.uint32
+U16 = mybir.dt.uint16
+U8 = mybir.dt.uint8
+FP8X4 = mybir.dt.float8_e4m3fn_x4
+FP4X4 = mybir.dt.float4_e2m1fn_x4
+ALU = mybir.AluOpType
+ACT = mybir.ActivationFunctionType
+
+
+def tile_list_zone_map_filter_kernel(tc, tab_words, tab_scales, offs, w1, w2_words, w2_scales, wgs, offs2, old, wf, bf, out):
+    nc = tc.nc
+    with ExitStack() as ctx:
+        keep = ctx.enter_context(tc.tile_pool(name="keep", bufs=1))
+        ring = ctx.enter_context(tc.tile_pool(name="ring", bufs=3))
+        slab = ctx.enter_context(tc.tile_pool(name="slab", bufs=4))
+        psum = ctx.enter_context(tc.psum_pool(name="psum", bufs=8))
+
+        gather_list = keep.tile([P, S // 16], U16, name="gather_list")
+        scatter_list = keep.tile([P, S // 16], U16, name="scatter_list")
+        nc.sync.dma_start(gather_list[:], offs)
+
+        tab_sc = keep.tile([P, T // 4], I32, name="tab_sc", align_bytes=64)
+        w2_sc_raw = keep.tile([P, PASSES, H // 4], I32, name="w2_sc_raw", align_bytes=64)
+        v_sc1 = keep.tile([P, S // 4], I32, name="v_sc1", align_bytes=64)
+        nc.vector.memset(tab_sc[:], 0)
+        nc.vector.memset(w2_sc_raw[:], 0)
+        nc.vector.memset(v_sc1[:], 0)
+        for q in range(4):
+            nc.sync.dma_start(tab_sc[32 * q : 32 * q + 8, :], tab_scales[:, 4 * q : 4 * q + 4, :].bitcast(I32))
+        tab_w = [keep.tile([P, T], I32, name="tab_w%d" % a, align_bytes=64) for a in range(PASSES)]
+        w1_raw = [slab.tile([P, PACK, H], F32, name="slab", align_bytes=64) for a in range(PASSES)]
+        w1_rows = [w1[a * 512 : (a + 1) * 512, :].rearrange("(p j) c -> p j c", j=PACK) for a in range(PASSES)]
+        w2_raw = keep.tile([P, PASSES, H // 2], I32, name="w2_raw", align_bytes=64)
+        bias = keep.tile([P, PACK], F32, name="bias")
+        nc.sync.dma_start(tab_w[0][:], tab_words[0].rearrange("p t i -> p (t i)").bitcast(I32))
+        nc.sync.dma_start(scatter_list[:], offs2)
+        nc.sync.dma_start(bias[:], bf.rearrange("(p m) -> p m", m=PACK))
+        nc.sync.dma_start(w2_raw[:], w2_words.rearrange("a p c -> p a c").bitcast(I32))
+        nc.sync.dma_start(w1_raw[0][:], w1_rows[0])
+        for q in range(4):
+            nc.sync.dma_start(w2_sc_raw[32 * q : 32 * q + 4, :, :],
+                              w2_scales[:, 4 * q : 4 * q + 4, :].rearrange("a r c -> r a c").bitcast(I32))
+        nc.sync.dma_start(tab_w[1][:], tab_words[1].rearrange("p t i -> p (t i)").bitcast(I32))
+        for j0 in (0, 2):
+            nc.sync.dma_start(w1_raw[1][:, j0 : j0 + 2, :], w1_rows[1][:, j0 : j0 + 2, :])
+        gains = keep.tile([P, PACK, S], F32, name="gains")
+        wgs_rows = wgs.rearrange("(m t) j -> m t j", t=PACK)
+        for t0, t1 in ((0, 1), (1, 2), (2, 4)):
+            for q in (0, 2, 1, 3):
+                nc.sync.dma_start(gains[32 * q : 32 * q + 32, t0:t1, :], wgs_rows[:, t0:t1, :])
+        wf_raw = slab.tile([P, PACK, N], F32, name="slab", align_bytes=64)
+        nc.sync.dma_start(wf_raw[:], wf.rearrange("(p j) c -> p j c", j=PACK))
+        starts = [sum(CHUNKS[:c]) for c in range(len(CHUNKS))]
+        old_planes = old.rearrange("(p t) c -> p t c", t=PACK)
+        old_sb = keep.tile([P, PACK, T2], F32, name="old_sb", align_bytes=64)
+        for c0 in range(0, T2, 512):
+            nc.sync.dma_start(old_sb[:, :, c0 : c0 + 512], old_planes[:, :, c0 : c0 + 512])
+
+        pages = [keep.tile([P, T2], F32, name="page%d" % t) for t in range(PACK)]
+        for t in range(PACK):
+            nc.vector.memset(pages[t][:], 0.0)
+
+        v_sc = keep.tile([P, S], U8, name="v_sc", align_bytes=64)
+        v_w = [keep.tile([P, S], U32, name="v_w%d" % a, align_bytes=64) for a in range(PASSES)]
+        nc.vector.tensor_copy(v_w[0][:], tab_w[0][:].bitcast(U32).indirect(gather_list[:]))
+        nc.vector.tensor_copy(v_sc[:], tab_sc[:].bitcast(U8).indirect(gather_list[:]))
+        nc.scalar.dma_start(v_sc1[0:112, :], v_sc[4:116, :].bitcast(I32))
+        nc.vector.tensor_copy(v_w[1][:], tab_w[1][:].bitcast(U32).indirect(gather_list[:]))
+
+        w2_c = keep.tile([P, PASSES, H // 2], I32, name="w2_c", align_bytes=64)
+        w2_s = keep.tile([P, PASSES, H], U8, name="w2_s", align_bytes=64)
+        nc.vector.tensor_copy(
+            w2_c[:].rearrange("p a c -> p (a c)").bitcast(U16).rearrange("p (a t m) -> p a t m", a=PASSES, t=PACK),
+            w2_raw[:].rearrange("p a c -> p (a c)").bitcast(U16).rearrange("p (a m t) -> p a t m", a=PASSES, t=PACK))
+        nc.vector.tensor_copy(
+            w2_s[:].rearrange("p a (t m) -> p a t m", t=PACK),
+            w2_sc_raw[:].rearrange("p a c -> p (a c)").bitcast(U8).rearrange("p (a m t) -> p a t m", a=PASSES, t=PACK))
+
+        def interleave(raw):
+            grouped = ring.tile([P, PACK * 512], BF16, name="z", align_bytes=64)
+            nc.scalar.copy(grouped[:].rearrange("p (t m j) -> p m j t", t=PACK, j=PACK),
+                           raw[:].rearrange("p j (m t) -> p m j t", t=PACK))
+            return grouped
+
+        def quantize(grouped, width, pool, name):
+            codes = pool.tile([P, width], U32, name=name + "_c", align_bytes=64)
+            scales = pool.tile([P, width], U8, name=name + "_s", align_bytes=64)
+            nc.vector.quantize_mx(out=codes[:].bitcast(FP8X4), scales=scales[:], in_=grouped)
+            return codes, scales
+
+        w1_c = [keep.tile([P, H], U32, name="w1_c%d" % a, align_bytes=64) for a in range(PASSES)]
+        w1_s = [keep.tile([P, H], U8, name="w1_s%d" % a, align_bytes=64) for a in range(PASSES)]
+        nc.vector.quantize_mx(out=w1_c[0][:].bitcast(FP8X4), scales=w1_s[0][:], in_=interleave(w1_raw[0])[:])
+        last = ring.tile([P, PACK * 512], BF16, name="z", align_bytes=64)
+        last_out = last[:].rearrange("p (t m j) -> p m j t", t=PACK, j=PACK)
+        last_in = w1_raw[1][:].rearrange("p j (m t) -> p m j t", t=PACK)
+        nc.scalar.copy(last_out[:, :, 0:2, :], last_in[:, :, 0:2, :])
+        nc.vector.tensor_copy(last_out[:, :, 2:4, :], last_in[:, :, 2:4, :])
+        for c0, c1 in ((0, 128), (128, 256), (256, 512)):
+            nc.vector.quantize_mx(out=w1_c[1][:, c0:c1].bitcast(FP8X4), scales=w1_s[1][:, c0:c1], in_=last[:, 4 * c0 : 4 * c1])
+
+        h_tiles = {}
+
+        def project(t, u):
+            cols = slice(u * BANK, (u + 1) * BANK)
+            rows = slice(t * P, (t + 1) * P)
+            if u == 0:
+                h_tiles[t] = ring.tile([P, S], F32, name="h")
+            acc2 = psum.tile([P, BANK], F32, name="acc")
+            for a in range(PASSES):
+                nc.tensor.matmul_mx(out=acc2[:],
+                                    lhsT=w2_c[:, a, t * 64 : (t + 1) * 64].bitcast(U8).bitcast(FP4X4),
+                                    lhsT_scale=w2_s[:, a, rows],
+                                    rhs=v_w[a][:, cols].bitcast(FP8X4),
+                                    rhs_scale=(v_sc[:], v_sc1[:].bitcast(U8))[a][:, cols],
+                                    start=(a == 0), stop=(a == PASSES - 1))
+            second = ring.tile([P, BANK], F32, name="second")
+            nc.scalar.copy(second[:], acc2[:])
+            acc1 = psum.tile([P, BANK], F32, name="acc")
+            for a in range(PASSES):
+                nc.tensor.matmul_mx(out=acc1[:],
+                                    lhsT=w1_c[a][:, rows].bitcast(FP8X4), lhsT_scale=w1_s[a][:, rows],
+                                    rhs=v_w[a][:, cols].bitcast(FP8X4), rhs_scale=v_sc[4 * a :, cols],
+                                    start=(a == 0), stop=(a == PASSES - 1))
+            nc.vector.tensor_tensor(h_tiles[t][:, cols], acc1[:], second[:], ALU.min)
+
+        page4 = keep.tile([P, PACK, T2], F32, name="page4", align_bytes=64)
+
+        def scatter(t, j0, j1):
+            nc.vector.tensor_tensor(pages[t][:].indirect(scatter_list[:, j0 // 16 : j1 // 16]),
+                                    h_tiles[t][:, j0:j1], gains[:, t, j0:j1], ALU.mult)
+
+        project(0, 0)
+        project(0, 1)
+        scatter(0, 0, BANK)
+        project(1, 0)
+        scatter(0, BANK, S)
+        nc.scalar.copy(page4[:, 0, :], pages[0][:])
+        project(1, 1)
+        for t in (1, 2):
+            project(t + 1, 0)
+            scatter(t, 0, S)
+            nc.scalar.copy(page4[:, t, :], pages[t][:])
+            project(t + 1, 1)
+        wf_q = quantize(interleave(wf_raw)[:], N, keep, "wf")
+        scatter(3, 0, S)
+
+        out_planes = out.rearrange("(p m) c -> p m c", m=PACK)
+
+        def lower(c):
+            c0, w = starts[c], CHUNKS[c]
+            nc.scalar.copy(page4[:, 3, c0 : c0 + w], pages[3][:, c0 : c0 + w])
+            z = ring.tile([P, PACK * w], BF16, name="z", align_bytes=64)
+            nc.vector.tensor_tensor(z[:].rearrange("p (c i t) -> p c t i", i=4, t=PACK),
+                                    page4[:, :, c0 : c0 + w].rearrange("p t (c i) -> p c t i", i=4),
+                                    old_sb[:, :, c0 : c0 + w].rearrange("p t (c i) -> p c t i", i=4), ALU.min)
+            return z
+
+        def test(c, z):
+            c0, w = starts[c], CHUNKS[c]
+            z_c, z_s = quantize(z[:], w, ring, "zq")
+            res = slab.tile([P, PACK, w], F32, name="slab", align_bytes=64)
+            for m in range(PACK):
+                rows = slice(m * P, (m + 1) * P)
+                acc = psum.tile([P, BANK], F32, name="acc")
+                nc.tensor.matmul_mx(out=acc[:, :w], lhsT=wf_q[0][:, rows].bitcast(FP8X4), lhsT_scale=wf_q[1][:, rows],
+                                    rhs=z_c[:].bitcast(FP8X4), rhs_scale=z_s[:], start=True, stop=True)
+                if c >= len(CHUNKS) - 2 and m % 2 == 1:
+                    nc.vector.tensor_scalar(res[:, m, :], acc[:, :w], bias[:, m : m + 1], 0.0, ALU.add, ALU.max)
+                else:
+                    nc.scalar.activation(res[:, m, :], acc[:, :w], ACT.Relu, bias=bias[:, m : m + 1])
+                if m % 2 == 1:
+                    nc.sync.dma_start(out_planes[:, m - 1 : m + 1, c0 : c0 + w], res[:, m - 1 : m + 1, :])
+
+        pending = lower(0)
+        for c in range(len(CHUNKS)):
+            following = lower(c + 1) if c + 1 < len(CHUNKS) else None
+            test(c, pending)
+            pending = following

@@ -9,6 +9,7 @@ PASSES = K // (P * PACK)
 BANK = 512
 HALVES = S // BANK
 CHUNKS = [256, 512, 512, 512, 256]
+OLD_SPLIT = 768
 
 FLOPS = 2 * (2 * K * H * S + H * N * T2)
 
@@ -29,59 +30,53 @@ def tile_list_zone_map_filter_kernel(tc, tab_words, tab_scales, offs, w1, w2_wor
     with ExitStack() as ctx:
         keep = ctx.enter_context(tc.tile_pool(name="keep", bufs=1))
         ring = ctx.enter_context(tc.tile_pool(name="ring", bufs=3))
-        slab = ctx.enter_context(tc.tile_pool(name="slab", bufs=4))
         psum = ctx.enter_context(tc.psum_pool(name="psum", bufs=8))
 
         gather_list = keep.tile([P, S // 16], U16, name="gather_list")
         scatter_list = keep.tile([P, S // 16], U16, name="scatter_list")
         nc.sync.dma_start(gather_list[:], offs)
 
-        tab_sc = keep.tile([P, T // 4], I32, name="tab_sc", align_bytes=64)
+        tab_sc = keep.tile([P, T // 4], I32, name="tab_sc", tag="slot_a", align_bytes=64)
         w2_sc_raw = keep.tile([P, PASSES, H // 4], I32, name="w2_sc_raw", align_bytes=64)
         v_sc1 = keep.tile([P, S // 4], I32, name="v_sc1", align_bytes=64)
-        nc.vector.memset(tab_sc[:], 0)
-        nc.vector.memset(w2_sc_raw[:], 0)
-        nc.vector.memset(v_sc1[:], 0)
+        nc.gpsimd.memset(tab_sc[:], 0)
         for q in range(4):
             nc.sync.dma_start(tab_sc[32 * q : 32 * q + 8, :], tab_scales[:, 4 * q : 4 * q + 4, :].bitcast(I32))
-        tab_w = [keep.tile([P, T], I32, name="tab_w%d" % a, align_bytes=64) for a in range(PASSES)]
-        w1_raw = [slab.tile([P, PACK, H], F32, name="slab", align_bytes=64) for a in range(PASSES)]
-        w1_rows = [w1[a * 512 : (a + 1) * 512, :].rearrange("(p j) c -> p j c", j=PACK) for a in range(PASSES)]
-        w2_raw = keep.tile([P, PASSES, H // 2], I32, name="w2_raw", align_bytes=64)
-        bias = keep.tile([P, PACK], F32, name="bias")
-        nc.sync.dma_start(tab_w[0][:], tab_words[0].rearrange("p t i -> p (t i)").bitcast(I32))
+        tab_w0 = keep.tile([P, T], I32, name="tab_w0", align_bytes=64)
+        nc.sync.dma_start(tab_w0[:], tab_words[0].rearrange("p t i -> p (t i)").bitcast(I32))
         nc.sync.dma_start(scatter_list[:], offs2)
-        nc.sync.dma_start(bias[:], bf.rearrange("(p m) -> p m", m=PACK))
-        nc.sync.dma_start(w2_raw[:], w2_words.rearrange("a p c -> p a c").bitcast(I32))
+        with tc.tile_pool(name="warm", bufs=1) as warm:
+            seed = warm.tile([P, 8], F32, name="seed")
+            warmed = warm.tile([P, 8], F32, name="warmed")
+            nc.gpsimd.memset(seed[:], 0.0)
+            nc.scalar.activation(warmed[:], seed[:], ACT.Relu)
+        pages = [keep.tile([P, T2], F32, name="page%d" % t) for t in range(PACK)]
+        nc.gpsimd.memset(pages[0][:], 0.0)
+        nc.gpsimd.memset(pages[1][:], 0.0)
+        nc.gpsimd.memset(w2_sc_raw[:], 0)
+        nc.gpsimd.memset(v_sc1[:], 0)
+        for t in range(2, PACK):
+            nc.gpsimd.memset(pages[t][:], 0.0)
+        late = ctx.enter_context(tc.tile_pool(name="late", bufs=1))
+        tab_w = [tab_w0, late.tile([P, T], I32, name="tab_w1", tag="slot_b", align_bytes=64)]
+        w1_raw = [late.tile([P, PACK, H], F32, name="w1_raw", tag="slot_w%d" % a, align_bytes=64) for a in range(PASSES)]
+        w1_rows = [w1[a * 512 : (a + 1) * 512, :].rearrange("(p j) c -> p j c", j=PACK) for a in range(PASSES)]
+        w2_raw = late.tile([P, PASSES, H // 2], I32, name="w2_raw", tag="slot_c", align_bytes=64)
         nc.sync.dma_start(w1_raw[0][:], w1_rows[0])
-        for q in range(4):
-            nc.sync.dma_start(w2_sc_raw[32 * q : 32 * q + 4, :, :],
-                              w2_scales[:, 4 * q : 4 * q + 4, :].rearrange("a r c -> r a c").bitcast(I32))
         nc.sync.dma_start(tab_w[1][:], tab_words[1].rearrange("p t i -> p (t i)").bitcast(I32))
+        nc.sync.dma_start(w2_raw[:], w2_words.rearrange("a p c -> p a c").bitcast(I32))
+        for q in range(4):
+            nc.scalar.dma_start(w2_sc_raw[32 * q : 32 * q + 4, :, :],
+                              w2_scales[:, 4 * q : 4 * q + 4, :].rearrange("a r c -> r a c").bitcast(I32))
         for j0 in (0, 2):
             nc.sync.dma_start(w1_raw[1][:, j0 : j0 + 2, :], w1_rows[1][:, j0 : j0 + 2, :])
-        gains = keep.tile([P, PACK, S], F32, name="gains")
-        wgs_rows = wgs.rearrange("(m t) j -> m t j", t=PACK)
-        for t0, t1 in ((0, 1), (1, 2), (2, 4)):
-            for q in (0, 2, 1, 3):
-                nc.sync.dma_start(gains[32 * q : 32 * q + 32, t0:t1, :], wgs_rows[:, t0:t1, :])
-        wf_raw = slab.tile([P, PACK, N], F32, name="slab", align_bytes=64)
-        nc.sync.dma_start(wf_raw[:], wf.rearrange("(p j) c -> p j c", j=PACK))
-        starts = [sum(CHUNKS[:c]) for c in range(len(CHUNKS))]
-        old_planes = old.rearrange("(p t) c -> p t c", t=PACK)
-        old_sb = keep.tile([P, PACK, T2], F32, name="old_sb", align_bytes=64)
-        for c0 in range(0, T2, 512):
-            nc.sync.dma_start(old_sb[:, :, c0 : c0 + 512], old_planes[:, :, c0 : c0 + 512])
 
-        pages = [keep.tile([P, T2], F32, name="page%d" % t) for t in range(PACK)]
-        for t in range(PACK):
-            nc.vector.memset(pages[t][:], 0.0)
 
         v_sc = keep.tile([P, S], U8, name="v_sc", align_bytes=64)
-        v_w = [keep.tile([P, S], U32, name="v_w%d" % a, align_bytes=64) for a in range(PASSES)]
+        v_w = [keep.tile([P, S], U32, name="v_w", tag="slot_v%d" % a, align_bytes=64) for a in range(PASSES)]
         nc.vector.tensor_copy(v_w[0][:], tab_w[0][:].bitcast(U32).indirect(gather_list[:]))
         nc.vector.tensor_copy(v_sc[:], tab_sc[:].bitcast(U8).indirect(gather_list[:]))
-        nc.scalar.dma_start(v_sc1[0:112, :], v_sc[4:116, :].bitcast(I32))
+        nc.sync.dma_start(v_sc1[0:112, :], v_sc[4:116, :].bitcast(I32))
         nc.vector.tensor_copy(v_w[1][:], tab_w[1][:].bitcast(U32).indirect(gather_list[:]))
 
         w2_c = keep.tile([P, PASSES, H // 2], I32, name="w2_c", align_bytes=64)
@@ -116,6 +111,18 @@ def tile_list_zone_map_filter_kernel(tc, tab_words, tab_scales, offs, w1, w2_wor
         for c0, c1 in ((0, 128), (128, 256), (256, 512)):
             nc.vector.quantize_mx(out=w1_c[1][:, c0:c1].bitcast(FP8X4), scales=w1_s[1][:, c0:c1], in_=last[:, 4 * c0 : 4 * c1])
 
+        gains = [keep.tile([P, 2, S], F32, name="gains_lo", tag="slot_a", align_bytes=64),
+                 late.tile([P, 2, S], F32, name="gains_hi", tag="slot_b", align_bytes=64)]
+        wgs_rows = wgs.rearrange("(m t) j -> m t j", t=PACK)
+        for t0, t1 in ((0, 1), (1, 2), (2, 4)):
+            for q in (0, 2, 1, 3):
+                nc.sync.dma_start(gains[t0 // 2][32 * q : 32 * q + 32, t0 % 2 : t0 % 2 + t1 - t0, :], wgs_rows[:, t0:t1, :])
+        wf_raw = late.tile([P, PACK, N], F32, name="wf_raw", tag="slot_w1", align_bytes=64)
+        nc.sync.dma_start(wf_raw[:], wf.rearrange("(p j) c -> p j c", j=PACK))
+        bias = late.tile([P, PACK], F32, name="bias", tag="slot_c", align_bytes=64)
+        nc.sync.dma_start(bias[:], bf.rearrange("(p m) -> p m", m=PACK))
+        starts = [sum(CHUNKS[:c]) for c in range(len(CHUNKS))]
+
         h_tiles = {}
 
         def project(t, u):
@@ -145,7 +152,7 @@ def tile_list_zone_map_filter_kernel(tc, tab_words, tab_scales, offs, w1, w2_wor
 
         def scatter(t, j0, j1):
             nc.vector.tensor_tensor(pages[t][:].indirect(scatter_list[:, j0 // 16 : j1 // 16]),
-                                    h_tiles[t][:, j0:j1], gains[:, t, j0:j1], ALU.mult)
+                                    h_tiles[t][:, j0:j1], gains[t // 2][:, t % 2, j0:j1], ALU.mult)
 
         project(0, 0)
         project(0, 1)
@@ -159,6 +166,11 @@ def tile_list_zone_map_filter_kernel(tc, tab_words, tab_scales, offs, w1, w2_wor
             scatter(t, 0, S)
             nc.scalar.copy(page4[:, t, :], pages[t][:])
             project(t + 1, 1)
+        old_planes = old.rearrange("(p t) c -> p t c", t=PACK)
+        old_sb = []
+        for a, (c0, c1) in enumerate(((0, OLD_SPLIT), (OLD_SPLIT, T2))):
+            old_sb.append(keep.tile([P, PACK, c1 - c0], F32, name="old_sb", tag="slot_v%d" % a, align_bytes=64))
+            nc.sync.dma_start(old_sb[a][:], old_planes[:, :, c0:c1])
         wf_q = quantize(interleave(wf_raw)[:], N, keep, "wf")
         scatter(3, 0, S)
 
@@ -170,13 +182,13 @@ def tile_list_zone_map_filter_kernel(tc, tab_words, tab_scales, offs, w1, w2_wor
             z = ring.tile([P, PACK * w], BF16, name="z", align_bytes=64)
             nc.vector.tensor_tensor(z[:].rearrange("p (c i t) -> p c t i", i=4, t=PACK),
                                     page4[:, :, c0 : c0 + w].rearrange("p t (c i) -> p c t i", i=4),
-                                    old_sb[:, :, c0 : c0 + w].rearrange("p t (c i) -> p c t i", i=4), ALU.min)
+                                    (old_sb[0][:, :, c0 : c0 + w] if c0 < OLD_SPLIT else old_sb[1][:, :, c0 - OLD_SPLIT : c0 - OLD_SPLIT + w]).rearrange("p t (c i) -> p c t i", i=4), ALU.min)
             return z
 
         def test(c, z):
             c0, w = starts[c], CHUNKS[c]
             z_c, z_s = quantize(z[:], w, ring, "zq")
-            res = slab.tile([P, PACK, w], F32, name="slab", align_bytes=64)
+            res = late.tile([P, PACK, w], F32, name="res", bufs=3, align_bytes=64)
             for m in range(PACK):
                 rows = slice(m * P, (m + 1) * P)
                 acc = psum.tile([P, BANK], F32, name="acc")

@@ -8,7 +8,7 @@ PACK = 4
 PASSES = K // (P * PACK)
 BANK = 512
 HALVES = S // BANK
-CHUNKS = [256, 512, 512, 512, 256]
+CHUNKS = [256, 512, 512, 256, 256, 128, 128]
 OLD_SPLIT = 768
 
 FLOPS = 2 * (2 * K * H * S + H * N * T2)
@@ -42,7 +42,7 @@ def tile_list_zone_map_filter_kernel(tc, tab_words, tab_scales, offs, w1, w2_wor
         nc.gpsimd.memset(tab_sc[:], 0)
         for q in range(4):
             nc.sync.dma_start(tab_sc[32 * q : 32 * q + 8, :], tab_scales[:, 4 * q : 4 * q + 4, :].bitcast(I32))
-        tab_w0 = keep.tile([P, T], I32, name="tab_w0", align_bytes=64)
+        tab_w0 = keep.tile([P, T], I32, name="tab_w0", tag="slot_d", align_bytes=64)
         nc.sync.dma_start(tab_w0[:], tab_words[0].rearrange("p t i -> p (t i)").bitcast(I32))
         nc.sync.dma_start(scatter_list[:], offs2)
         with tc.tile_pool(name="warm", bufs=1) as warm:
@@ -59,25 +59,24 @@ def tile_list_zone_map_filter_kernel(tc, tab_words, tab_scales, offs, w1, w2_wor
             nc.gpsimd.memset(pages[t][:], 0.0)
         late = ctx.enter_context(tc.tile_pool(name="late", bufs=1))
         tab_w = [tab_w0, late.tile([P, T], I32, name="tab_w1", tag="slot_b", align_bytes=64)]
-        w1_raw = [late.tile([P, PACK, H], F32, name="w1_raw", tag="slot_w%d" % a, align_bytes=64) for a in range(PASSES)]
+        w1_raw = [late.tile([P, PACK, H], F32, name="w1_raw0", tag="slot_w", align_bytes=64)]
         w1_rows = [w1[a * 512 : (a + 1) * 512, :].rearrange("(p j) c -> p j c", j=PACK) for a in range(PASSES)]
         w2_raw = late.tile([P, PASSES, H // 2], I32, name="w2_raw", tag="slot_c", align_bytes=64)
         nc.sync.dma_start(w1_raw[0][:], w1_rows[0])
-        nc.sync.dma_start(tab_w[1][:], tab_words[1].rearrange("p t i -> p (t i)").bitcast(I32))
         nc.sync.dma_start(w2_raw[:], w2_words.rearrange("a p c -> p a c").bitcast(I32))
+        nc.sync.dma_start(tab_w[1][:], tab_words[1].rearrange("p t i -> p (t i)").bitcast(I32))
         for q in range(4):
             nc.scalar.dma_start(w2_sc_raw[32 * q : 32 * q + 4, :, :],
-                              w2_scales[:, 4 * q : 4 * q + 4, :].rearrange("a r c -> r a c").bitcast(I32))
-        for j0 in (0, 2):
-            nc.sync.dma_start(w1_raw[1][:, j0 : j0 + 2, :], w1_rows[1][:, j0 : j0 + 2, :])
+                                w2_scales[:, 4 * q : 4 * q + 4, :].rearrange("a r c -> r a c").bitcast(I32))
 
 
         v_sc = keep.tile([P, S], U8, name="v_sc", align_bytes=64)
         v_w = [keep.tile([P, S], U32, name="v_w", tag="slot_v%d" % a, align_bytes=64) for a in range(PASSES)]
         nc.vector.tensor_copy(v_w[0][:], tab_w[0][:].bitcast(U32).indirect(gather_list[:]))
+        w1_raw.append(keep.tile([P, PACK, H], F32, name="w1_raw1", tag="slot_d", align_bytes=64))
+        for j0 in (0, 2):
+            nc.sync.dma_start(w1_raw[1][:, j0 : j0 + 2, :], w1_rows[1][:, j0 : j0 + 2, :])
         nc.vector.tensor_copy(v_sc[:], tab_sc[:].bitcast(U8).indirect(gather_list[:]))
-        nc.sync.dma_start(v_sc1[0:112, :], v_sc[4:116, :].bitcast(I32))
-        nc.vector.tensor_copy(v_w[1][:], tab_w[1][:].bitcast(U32).indirect(gather_list[:]))
 
         w2_c = keep.tile([P, PASSES, H // 2], I32, name="w2_c", align_bytes=64)
         w2_s = keep.tile([P, PASSES, H], U8, name="w2_s", align_bytes=64)
@@ -103,6 +102,8 @@ def tile_list_zone_map_filter_kernel(tc, tab_words, tab_scales, offs, w1, w2_wor
         w1_c = [keep.tile([P, H], U32, name="w1_c%d" % a, align_bytes=64) for a in range(PASSES)]
         w1_s = [keep.tile([P, H], U8, name="w1_s%d" % a, align_bytes=64) for a in range(PASSES)]
         nc.vector.quantize_mx(out=w1_c[0][:].bitcast(FP8X4), scales=w1_s[0][:], in_=interleave(w1_raw[0])[:])
+        nc.sync.dma_start(v_sc1[0:112, :], v_sc[4:116, :].bitcast(I32))
+        nc.vector.tensor_copy(v_w[1][:], tab_w[1][:].bitcast(U32).indirect(gather_list[:]))
         last = ring.tile([P, PACK * 512], BF16, name="z", align_bytes=64)
         last_out = last[:].rearrange("p (t m j) -> p m j t", t=PACK, j=PACK)
         last_in = w1_raw[1][:].rearrange("p j (m t) -> p m j t", t=PACK)
@@ -117,7 +118,7 @@ def tile_list_zone_map_filter_kernel(tc, tab_words, tab_scales, offs, w1, w2_wor
         for t0, t1 in ((0, 1), (1, 2), (2, 4)):
             for q in (0, 2, 1, 3):
                 nc.sync.dma_start(gains[t0 // 2][32 * q : 32 * q + 32, t0 % 2 : t0 % 2 + t1 - t0, :], wgs_rows[:, t0:t1, :])
-        wf_raw = late.tile([P, PACK, N], F32, name="wf_raw", tag="slot_w1", align_bytes=64)
+        wf_raw = keep.tile([P, PACK, N], F32, name="wf_raw", tag="slot_d", align_bytes=64)
         nc.sync.dma_start(wf_raw[:], wf.rearrange("(p j) c -> p j c", j=PACK))
         bias = late.tile([P, PACK], F32, name="bias", tag="slot_c", align_bytes=64)
         nc.sync.dma_start(bias[:], bf.rearrange("(p m) -> p m", m=PACK))
@@ -125,28 +126,38 @@ def tile_list_zone_map_filter_kernel(tc, tab_words, tab_scales, offs, w1, w2_wor
 
         h_tiles = {}
 
-        def project(t, u):
+        sums = {}
+
+        def multiply(t, u, a):
             cols = slice(u * BANK, (u + 1) * BANK)
             rows = slice(t * P, (t + 1) * P)
+            if a == 0:
+                sums[t, u] = (psum.tile([P, BANK], F32, name="acc"), psum.tile([P, BANK], F32, name="acc"))
+            acc1, acc2 = sums[t, u]
+            nc.tensor.matmul_mx(out=acc2[:],
+                                lhsT=w2_c[:, a, t * 64 : (t + 1) * 64].bitcast(U8).bitcast(FP4X4),
+                                lhsT_scale=w2_s[:, a, rows],
+                                rhs=v_w[a][:, cols].bitcast(FP8X4),
+                                rhs_scale=(v_sc[:], v_sc1[:].bitcast(U8))[a][:, cols],
+                                start=(a == 0), stop=(a == PASSES - 1))
+            nc.tensor.matmul_mx(out=acc1[:],
+                                lhsT=w1_c[a][:, rows].bitcast(FP8X4), lhsT_scale=w1_s[a][:, rows],
+                                rhs=v_w[a][:, cols].bitcast(FP8X4), rhs_scale=v_sc[4 * a :, cols],
+                                start=(a == 0), stop=(a == PASSES - 1))
+
+        def smaller(t, u):
+            cols = slice(u * BANK, (u + 1) * BANK)
             if u == 0:
                 h_tiles[t] = ring.tile([P, S], F32, name="h")
-            acc2 = psum.tile([P, BANK], F32, name="acc")
-            for a in range(PASSES):
-                nc.tensor.matmul_mx(out=acc2[:],
-                                    lhsT=w2_c[:, a, t * 64 : (t + 1) * 64].bitcast(U8).bitcast(FP4X4),
-                                    lhsT_scale=w2_s[:, a, rows],
-                                    rhs=v_w[a][:, cols].bitcast(FP8X4),
-                                    rhs_scale=(v_sc[:], v_sc1[:].bitcast(U8))[a][:, cols],
-                                    start=(a == 0), stop=(a == PASSES - 1))
+            acc1, acc2 = sums[t, u]
             second = ring.tile([P, BANK], F32, name="second")
             nc.scalar.copy(second[:], acc2[:])
-            acc1 = psum.tile([P, BANK], F32, name="acc")
-            for a in range(PASSES):
-                nc.tensor.matmul_mx(out=acc1[:],
-                                    lhsT=w1_c[a][:, rows].bitcast(FP8X4), lhsT_scale=w1_s[a][:, rows],
-                                    rhs=v_w[a][:, cols].bitcast(FP8X4), rhs_scale=v_sc[4 * a :, cols],
-                                    start=(a == 0), stop=(a == PASSES - 1))
             nc.vector.tensor_tensor(h_tiles[t][:, cols], acc1[:], second[:], ALU.min)
+
+        def project(t, u):
+            multiply(t, u, 0)
+            multiply(t, u, 1)
+            smaller(t, u)
 
         page4 = keep.tile([P, PACK, T2], F32, name="page4", align_bytes=64)
 
@@ -154,8 +165,12 @@ def tile_list_zone_map_filter_kernel(tc, tab_words, tab_scales, offs, w1, w2_wor
             nc.vector.tensor_tensor(pages[t][:].indirect(scatter_list[:, j0 // 16 : j1 // 16]),
                                     h_tiles[t][:, j0:j1], gains[t // 2][:, t % 2, j0:j1], ALU.mult)
 
-        project(0, 0)
-        project(0, 1)
+        multiply(0, 0, 0)
+        multiply(0, 1, 0)
+        multiply(0, 0, 1)
+        smaller(0, 0)
+        multiply(0, 1, 1)
+        smaller(0, 1)
         scatter(0, 0, BANK)
         project(1, 0)
         scatter(0, BANK, S)
@@ -176,19 +191,26 @@ def tile_list_zone_map_filter_kernel(tc, tab_words, tab_scales, offs, w1, w2_wor
 
         out_planes = out.rearrange("(p m) c -> p m c", m=PACK)
 
-        def lower(c):
+        for c0, c1 in ((0, 256), (256, OLD_SPLIT), (OLD_SPLIT, T2)):
+            nc.scalar.copy(page4[:, 3, c0:c1], pages[3][:, c0:c1])
+
+        z_tiles = {}
+
+        def lower(c, half):
             c0, w = starts[c], CHUNKS[c]
-            nc.scalar.copy(page4[:, 3, c0 : c0 + w], pages[3][:, c0 : c0 + w])
-            z = ring.tile([P, PACK * w], BF16, name="z", align_bytes=64)
-            nc.vector.tensor_tensor(z[:].rearrange("p (c i t) -> p c t i", i=4, t=PACK),
-                                    page4[:, :, c0 : c0 + w].rearrange("p t (c i) -> p c t i", i=4),
-                                    (old_sb[0][:, :, c0 : c0 + w] if c0 < OLD_SPLIT else old_sb[1][:, :, c0 - OLD_SPLIT : c0 - OLD_SPLIT + w]).rearrange("p t (c i) -> p c t i", i=4), ALU.min)
-            return z
+            if half == 0:
+                z_tiles[c] = ring.tile([P, PACK * w], BF16, name="z", align_bytes=64)
+            d0 = half * w // 2
+            cols = slice(c0 + d0, c0 + d0 + w // 2)
+            old_cols = old_sb[0][:, :, cols] if c0 < OLD_SPLIT else old_sb[1][:, :, cols.start - OLD_SPLIT : cols.stop - OLD_SPLIT]
+            nc.vector.tensor_tensor(z_tiles[c][:, PACK * d0 : PACK * (d0 + w // 2)].rearrange("p (c i t) -> p c t i", i=4, t=PACK),
+                                    page4[:, :, cols].rearrange("p t (c i) -> p c t i", i=4),
+                                    old_cols.rearrange("p t (c i) -> p c t i", i=4), ALU.min)
 
         def test(c, z):
             c0, w = starts[c], CHUNKS[c]
             z_c, z_s = quantize(z[:], w, ring, "zq")
-            res = late.tile([P, PACK, w], F32, name="res", bufs=3, align_bytes=64)
+            res = late.tile([P, PACK, w], F32, name="res", bufs=4, align_bytes=64)
             for m in range(PACK):
                 rows = slice(m * P, (m + 1) * P)
                 acc = psum.tile([P, BANK], F32, name="acc")
@@ -198,11 +220,15 @@ def tile_list_zone_map_filter_kernel(tc, tab_words, tab_scales, offs, w1, w2_wor
                     nc.vector.tensor_scalar(res[:, m, :], acc[:, :w], bias[:, m : m + 1], 0.0, ALU.add, ALU.max)
                 else:
                     nc.scalar.activation(res[:, m, :], acc[:, :w], ACT.Relu, bias=bias[:, m : m + 1])
-                if m % 2 == 1:
-                    nc.sync.dma_start(out_planes[:, m - 1 : m + 1, c0 : c0 + w], res[:, m - 1 : m + 1, :])
+                group = 2 if w == BANK else PACK
+                if (m + 1) % group == 0:
+                    nc.sync.dma_start(out_planes[:, m + 1 - group : m + 1, c0 : c0 + w], res[:, m + 1 - group : m + 1, :])
 
-        pending = lower(0)
+        lower(0, 0)
+        lower(0, 1)
         for c in range(len(CHUNKS)):
-            following = lower(c + 1) if c + 1 < len(CHUNKS) else None
-            test(c, pending)
-            pending = following
+            if c + 1 < len(CHUNKS):
+                lower(c + 1, 0)
+            test(c, z_tiles[c])
+            if c + 1 < len(CHUNKS):
+                lower(c + 1, 1)

@@ -39,7 +39,7 @@ def tile_list_zone_map_filter_kernel(tc, tab_words, tab_scales, offs, w1, w2_wor
         tab_sc = keep.tile([P, T // 4], I32, name="tab_sc", tag="slot_a", align_bytes=64)
         w2_sc_raw = keep.tile([P, PASSES, H // 4], I32, name="w2_sc_raw", align_bytes=64)
         v_sc1 = keep.tile([P, S // 4], I32, name="v_sc1", align_bytes=64)
-        nc.gpsimd.memset(tab_sc[:], 0)
+        nc.vector.memset(tab_sc[:], 0)
         for q in range(4):
             nc.sync.dma_start(tab_sc[32 * q : 32 * q + 8, :], tab_scales[:, 4 * q : 4 * q + 4, :].bitcast(I32))
         tab_w0 = keep.tile([P, T], I32, name="tab_w0", tag="slot_d", align_bytes=64)
@@ -48,15 +48,14 @@ def tile_list_zone_map_filter_kernel(tc, tab_words, tab_scales, offs, w1, w2_wor
         with tc.tile_pool(name="warm", bufs=1) as warm:
             seed = warm.tile([P, 8], F32, name="seed")
             warmed = warm.tile([P, 8], F32, name="warmed")
-            nc.gpsimd.memset(seed[:], 0.0)
+            nc.vector.memset(seed[:], 0.0)
             nc.scalar.activation(warmed[:], seed[:], ACT.Relu)
         pages = [keep.tile([P, T2], F32, name="page%d" % t) for t in range(PACK)]
-        nc.gpsimd.memset(pages[0][:], 0.0)
-        nc.gpsimd.memset(pages[1][:], 0.0)
-        nc.gpsimd.memset(w2_sc_raw[:], 0)
-        nc.gpsimd.memset(v_sc1[:], 0)
-        for t in range(2, PACK):
-            nc.gpsimd.memset(pages[t][:], 0.0)
+        nc.vector.memset(pages[0][:], 0.0)
+        nc.vector.memset(pages[1][:], 0.0)
+        nc.vector.memset(w2_sc_raw[:], 0)
+        nc.vector.memset(v_sc1[:], 0)
+        nc.vector.memset(pages[2][:], 0.0)
         late = ctx.enter_context(tc.tile_pool(name="late", bufs=1))
         tab_w = [tab_w0, late.tile([P, T], I32, name="tab_w1", tag="slot_b", align_bytes=64)]
         w1_raw = [late.tile([P, PACK, H], F32, name="w1_raw0", tag="slot_w", align_bytes=64)]
@@ -74,9 +73,9 @@ def tile_list_zone_map_filter_kernel(tc, tab_words, tab_scales, offs, w1, w2_wor
         v_w = [keep.tile([P, S], U32, name="v_w", tag="slot_v%d" % a, align_bytes=64) for a in range(PASSES)]
         nc.vector.tensor_copy(v_w[0][:], tab_w[0][:].bitcast(U32).indirect(gather_list[:]))
         w1_raw.append(keep.tile([P, PACK, H], F32, name="w1_raw1", tag="slot_d", align_bytes=64))
-        for j0 in (0, 2):
-            nc.sync.dma_start(w1_raw[1][:, j0 : j0 + 2, :], w1_rows[1][:, j0 : j0 + 2, :])
+        nc.sync.dma_start(w1_raw[1][:], w1_rows[1])
         nc.vector.tensor_copy(v_sc[:], tab_sc[:].bitcast(U8).indirect(gather_list[:]))
+        nc.vector.memset(pages[3][:], 0.0)
 
         w2_c = keep.tile([P, PASSES, H // 2], I32, name="w2_c", align_bytes=64)
         w2_s = keep.tile([P, PASSES, H], U8, name="w2_s", align_bytes=64)
@@ -89,8 +88,8 @@ def tile_list_zone_map_filter_kernel(tc, tab_words, tab_scales, offs, w1, w2_wor
 
         def interleave(raw):
             grouped = ring.tile([P, PACK * 512], BF16, name="z", align_bytes=64)
-            nc.scalar.copy(grouped[:].rearrange("p (t m j) -> p m j t", t=PACK, j=PACK),
-                           raw[:].rearrange("p j (m t) -> p m j t", t=PACK))
+            nc.scalar.copy(grouped[:].rearrange("p (t m j) -> p m t j", t=PACK, j=PACK),
+                           raw[:].rearrange("p j (m t) -> p m t j", t=PACK))
             return grouped
 
         def quantize(grouped, width, pool, name):
@@ -105,10 +104,10 @@ def tile_list_zone_map_filter_kernel(tc, tab_words, tab_scales, offs, w1, w2_wor
         nc.sync.dma_start(v_sc1[0:112, :], v_sc[4:116, :].bitcast(I32))
         nc.vector.tensor_copy(v_w[1][:], tab_w[1][:].bitcast(U32).indirect(gather_list[:]))
         last = ring.tile([P, PACK * 512], BF16, name="z", align_bytes=64)
-        last_out = last[:].rearrange("p (t m j) -> p m j t", t=PACK, j=PACK)
-        last_in = w1_raw[1][:].rearrange("p j (m t) -> p m j t", t=PACK)
-        nc.scalar.copy(last_out[:, :, 0:2, :], last_in[:, :, 0:2, :])
-        nc.vector.tensor_copy(last_out[:, :, 2:4, :], last_in[:, :, 2:4, :])
+        last_out = last[:].rearrange("p (t m j) -> p m t j", t=PACK, j=PACK)
+        last_in = w1_raw[1][:].rearrange("p j (m t) -> p m t j", t=PACK)
+        nc.scalar.copy(last_out[:, 88:], last_in[:, 88:])
+        nc.vector.tensor_copy(last_out[:, :88], last_in[:, :88])
         for c0, c1 in ((0, 128), (128, 256), (256, 512)):
             nc.vector.quantize_mx(out=w1_c[1][:, c0:c1].bitcast(FP8X4), scales=w1_s[1][:, c0:c1], in_=last[:, 4 * c0 : 4 * c1])
 
@@ -203,9 +202,9 @@ def tile_list_zone_map_filter_kernel(tc, tab_words, tab_scales, offs, w1, w2_wor
             d0 = half * w // 2
             cols = slice(c0 + d0, c0 + d0 + w // 2)
             old_cols = old_sb[0][:, :, cols] if c0 < OLD_SPLIT else old_sb[1][:, :, cols.start - OLD_SPLIT : cols.stop - OLD_SPLIT]
-            nc.vector.tensor_tensor(z_tiles[c][:, PACK * d0 : PACK * (d0 + w // 2)].rearrange("p (c i t) -> p c t i", i=4, t=PACK),
-                                    page4[:, :, cols].rearrange("p t (c i) -> p c t i", i=4),
-                                    old_cols.rearrange("p t (c i) -> p c t i", i=4), ALU.min)
+            nc.vector.tensor_tensor(z_tiles[c][:, PACK * d0 : PACK * (d0 + w // 2)].rearrange("p (c i t) -> p c t i", i=2, t=PACK),
+                                    page4[:, :, cols].rearrange("p t (c i) -> p c t i", i=2),
+                                    old_cols.rearrange("p t (c i) -> p c t i", i=2), ALU.min)
 
         def test(c, z):
             c0, w = starts[c], CHUNKS[c]

@@ -30,54 +30,65 @@ def tile_list_zone_map_filter_kernel(tc, tab_words, tab_scales, offs, w1, w2_wor
     with ExitStack() as ctx:
         keep = ctx.enter_context(tc.tile_pool(name="keep", bufs=1))
         ring = ctx.enter_context(tc.tile_pool(name="ring", bufs=3))
-        psum = ctx.enter_context(tc.psum_pool(name="psum", bufs=8))
+        psum = ctx.enter_context(tc.psum_pool(name="psum", bufs=4))
 
         gather_list = keep.tile([P, S // 16], U16, name="gather_list")
         scatter_list = keep.tile([P, S // 16], U16, name="scatter_list")
         nc.sync.dma_start(gather_list[:], offs)
-
-        tab_sc = keep.tile([P, T // 4], I32, name="tab_sc", tag="slot_a", align_bytes=64)
-        w2_sc_raw = keep.tile([P, PASSES, H // 4], I32, name="w2_sc_raw", align_bytes=64)
-        v_sc1 = keep.tile([P, S // 4], I32, name="v_sc1", align_bytes=64)
-        nc.vector.memset(tab_sc[:], 0)
-        for q in range(4):
-            nc.sync.dma_start(tab_sc[32 * q : 32 * q + 8, :], tab_scales[:, 4 * q : 4 * q + 4, :].bitcast(I32))
-        tab_w0 = keep.tile([P, T], I32, name="tab_w0", tag="slot_d", align_bytes=64)
+        tab_w0 = keep.tile([P, T], I32, name="tab_w0", tag="slot_a", align_bytes=64)
         nc.sync.dma_start(tab_w0[:], tab_words[0].rearrange("p t i -> p (t i)").bitcast(I32))
         nc.sync.dma_start(scatter_list[:], offs2)
+
+        tab_sc = keep.tile([P, T // 4], I32, name="tab_sc", tag="slot_e", align_bytes=64)
+        nc.vector.memset(tab_sc[:], 0)
+        nc.sync.dma_start(tab_sc[8:24, :], tab_scales[1].bitcast(I32))
+        for q in range(4):
+            nc.sync.dma_start(tab_sc[32 * q : 32 * q + 4, :], tab_scales[0, 4 * q : 4 * q + 4, :].bitcast(I32))
         with tc.tile_pool(name="warm", bufs=1) as warm:
             seed = warm.tile([P, 8], F32, name="seed")
             warmed = warm.tile([P, 8], F32, name="warmed")
             nc.vector.memset(seed[:], 0.0)
             nc.scalar.activation(warmed[:], seed[:], ACT.Relu)
-        pages = [keep.tile([P, T2], F32, name="page%d" % t) for t in range(PACK)]
+        late = ctx.enter_context(tc.tile_pool(name="late", bufs=1))
+        w2_sc_raw = late.tile([P, PASSES, H // 4], I32, name="w2_sc_raw", align_bytes=64)
+        nc.vector.memset(w2_sc_raw[:], 0)
+        v_sc1 = keep.tile([P, S // 4], I32, name="v_sc1", align_bytes=64)
+        nc.vector.memset(v_sc1[:], 0)
+        pages = [keep.tile([P, T2], F32, name="page%d" % t) for t in range(2)]
         nc.vector.memset(pages[0][:], 0.0)
         nc.vector.memset(pages[1][:], 0.0)
-        nc.vector.memset(w2_sc_raw[:], 0)
-        nc.vector.memset(v_sc1[:], 0)
-        nc.vector.memset(pages[2][:], 0.0)
-        late = ctx.enter_context(tc.tile_pool(name="late", bufs=1))
-        tab_w = [tab_w0, late.tile([P, T], I32, name="tab_w1", tag="slot_b", align_bytes=64)]
-        w1_raw = [late.tile([P, PACK, H], F32, name="w1_raw0", tag="slot_w", align_bytes=64)]
+
         w1_rows = [w1[a * 512 : (a + 1) * 512, :].rearrange("(p j) c -> p j c", j=PACK) for a in range(PASSES)]
-        w2_raw = late.tile([P, PASSES, H // 2], I32, name="w2_raw", tag="slot_c", align_bytes=64)
-        nc.sync.dma_start(w1_raw[0][:], w1_rows[0])
+        w1_raw0 = late.tile([P, PACK, H], F32, name="w1_raw0", tag="slot_c", align_bytes=64)
+        w2_raw = late.tile([P, PASSES, H // 2], I32, name="w2_raw", align_bytes=64)
+        tab_w1 = late.tile([P, T], I32, name="tab_w1", tag="slot_b", align_bytes=64)
+        nc.sync.dma_start(w1_raw0[:], w1_rows[0])
         nc.sync.dma_start(w2_raw[:], w2_words.rearrange("a p c -> p a c").bitcast(I32))
-        nc.sync.dma_start(tab_w[1][:], tab_words[1].rearrange("p t i -> p (t i)").bitcast(I32))
+        nc.sync.dma_start(tab_w1[:], tab_words[1].rearrange("p t i -> p (t i)").bitcast(I32))
         for q in range(4):
-            nc.scalar.dma_start(w2_sc_raw[32 * q : 32 * q + 4, :, :],
-                                w2_scales[:, 4 * q : 4 * q + 4, :].rearrange("a r c -> r a c").bitcast(I32))
+            nc.sync.dma_start(w2_sc_raw[32 * q : 32 * q + 4, :, :],
+                              w2_scales[:, 4 * q : 4 * q + 4, :].rearrange("a r c -> r a c").bitcast(I32))
 
+        v_sc0 = keep.tile([P, S], U8, name="v_sc0", align_bytes=64)
+        v_w0 = keep.tile([P, S], U32, name="v_w0", tag="slot_v", align_bytes=64)
+        nc.vector.tensor_copy(v_w0[:], tab_w0[:].bitcast(U32).indirect(gather_list[:]))
+        w1_raw1 = keep.tile([P, PACK, H], F32, name="w1_raw1", tag="slot_a", align_bytes=64)
+        nc.sync.dma_start(w1_raw1[:], w1_rows[1])
+        nc.vector.tensor_copy(v_sc0[:], tab_sc[:].bitcast(U8).indirect(gather_list[:]))
+        for q in range(4):
+            nc.sync.dma_start(v_sc1[32 * q : 32 * q + 4, :], v_sc0[8 + 4 * q : 12 + 4 * q, :].bitcast(I32))
+        v_sc = [v_sc0[:], v_sc1[:].bitcast(U8)]
 
-        v_sc = keep.tile([P, S], U8, name="v_sc", align_bytes=64)
-        v_w = [keep.tile([P, S], U32, name="v_w", tag="slot_v%d" % a, align_bytes=64) for a in range(PASSES)]
-        nc.vector.tensor_copy(v_w[0][:], tab_w[0][:].bitcast(U32).indirect(gather_list[:]))
-        w1_raw.append(keep.tile([P, PACK, H], F32, name="w1_raw1", tag="slot_d", align_bytes=64))
-        nc.sync.dma_start(w1_raw[1][:], w1_rows[1])
-        nc.vector.tensor_copy(v_sc[:], tab_sc[:].bitcast(U8).indirect(gather_list[:]))
-        nc.vector.memset(pages[3][:], 0.0)
+        wgs_rows = wgs.rearrange("(m t) j -> m t j", t=PACK)
 
-        w2_c = keep.tile([P, PASSES, H // 2], I32, name="w2_c", align_bytes=64)
+        def load_gains(tile_view, t0, t1, j0, j1):
+            for q in (0, 2, 1, 3):
+                nc.sync.dma_start(tile_view[32 * q : 32 * q + 32], wgs_rows[:, t0:t1, j0:j1])
+
+        gains_first = keep.tile([P, 1, BANK], F32, name="gains_first", tag="slot_e", align_bytes=64)
+        load_gains(gains_first, 0, 1, 0, BANK)
+
+        w2_c = keep.tile([P, PASSES, H // 2], I32, name="w2_c", tag="slot_w", align_bytes=64)
         w2_s = keep.tile([P, PASSES, H], U8, name="w2_s", align_bytes=64)
         nc.vector.tensor_copy(
             w2_c[:].rearrange("p a c -> p (a c)").bitcast(U16).rearrange("p (a t m) -> p a t m", a=PASSES, t=PACK),
@@ -86,11 +97,9 @@ def tile_list_zone_map_filter_kernel(tc, tab_words, tab_scales, offs, w1, w2_wor
             w2_s[:].rearrange("p a (t m) -> p a t m", t=PACK),
             w2_sc_raw[:].rearrange("p a c -> p (a c)").bitcast(U8).rearrange("p (a m t) -> p a t m", a=PASSES, t=PACK))
 
-        def interleave(raw):
-            grouped = ring.tile([P, PACK * 512], BF16, name="z", align_bytes=64)
-            nc.scalar.copy(grouped[:].rearrange("p (t m j) -> p m t j", t=PACK, j=PACK),
-                           raw[:].rearrange("p j (m t) -> p m t j", t=PACK))
-            return grouped
+        def interleave(copy, grouped, raw, t0, t1):
+            copy(grouped[:].rearrange("p (t m j) -> p m t j", t=t1 - t0, j=PACK),
+                 raw[:].rearrange("p j (m t) -> p m t j", t=PACK)[:, :, t0:t1, :])
 
         def quantize(grouped, width, pool, name):
             codes = pool.tile([P, width], U32, name=name + "_c", align_bytes=64)
@@ -98,95 +107,106 @@ def tile_list_zone_map_filter_kernel(tc, tab_words, tab_scales, offs, w1, w2_wor
             nc.vector.quantize_mx(out=codes[:].bitcast(FP8X4), scales=scales[:], in_=grouped)
             return codes, scales
 
-        w1_c = [keep.tile([P, H], U32, name="w1_c%d" % a, align_bytes=64) for a in range(PASSES)]
-        w1_s = [keep.tile([P, H], U8, name="w1_s%d" % a, align_bytes=64) for a in range(PASSES)]
-        nc.vector.quantize_mx(out=w1_c[0][:].bitcast(FP8X4), scales=w1_s[0][:], in_=interleave(w1_raw[0])[:])
-        nc.sync.dma_start(v_sc1[0:112, :], v_sc[4:116, :].bitcast(I32))
-        nc.vector.tensor_copy(v_w[1][:], tab_w[1][:].bitcast(U32).indirect(gather_list[:]))
-        last = ring.tile([P, PACK * 512], BF16, name="z", align_bytes=64)
-        last_out = last[:].rearrange("p (t m j) -> p m t j", t=PACK, j=PACK)
-        last_in = w1_raw[1][:].rearrange("p j (m t) -> p m t j", t=PACK)
-        nc.scalar.copy(last_out[:, 88:], last_in[:, 88:])
-        nc.vector.tensor_copy(last_out[:, :88], last_in[:, :88])
-        for c0, c1 in ((0, 128), (128, 256), (256, 512)):
-            nc.vector.quantize_mx(out=w1_c[1][:, c0:c1].bitcast(FP8X4), scales=w1_s[1][:, c0:c1], in_=last[:, 4 * c0 : 4 * c1])
+        w1_g0 = keep.tile([P, PACK * H], BF16, name="w1_g0", align_bytes=64)
+        interleave(nc.scalar.copy, w1_g0, w1_raw0, 0, PACK)
+        w1_q0 = quantize(w1_g0[:], H, keep, "w1_q0")
+        gains_rest = late.tile([P, 3, BANK], F32, name="gains_rest", tag="slot_c", align_bytes=64)
+        load_gains(gains_rest[:, 0:1, :], 0, 1, BANK, S)
+        load_gains(gains_rest[:, 1:3, :].rearrange("p (t a) b -> p t (a b)", t=1), 1, 2, 0, S)
 
-        gains = [keep.tile([P, 2, S], F32, name="gains_lo", tag="slot_a", align_bytes=64),
-                 late.tile([P, 2, S], F32, name="gains_hi", tag="slot_b", align_bytes=64)]
-        wgs_rows = wgs.rearrange("(m t) j -> m t j", t=PACK)
-        for t0, t1 in ((0, 1), (1, 2), (2, 4)):
-            for q in (0, 2, 1, 3):
-                nc.sync.dma_start(gains[t0 // 2][32 * q : 32 * q + 32, t0 % 2 : t0 % 2 + t1 - t0, :], wgs_rows[:, t0:t1, :])
-        wf_raw = keep.tile([P, PACK, N], F32, name="wf_raw", tag="slot_d", align_bytes=64)
-        nc.sync.dma_start(wf_raw[:], wf.rearrange("(p j) c -> p j c", j=PACK))
-        bias = late.tile([P, PACK], F32, name="bias", tag="slot_c", align_bytes=64)
-        nc.sync.dma_start(bias[:], bf.rearrange("(p m) -> p m", m=PACK))
-        starts = [sum(CHUNKS[:c]) for c in range(len(CHUNKS))]
+        v_w1 = [keep.tile([P, BANK], U32, name="v_w1_lo", tag="slot_l", align_bytes=64)]
+        nc.vector.tensor_copy(v_w1[0][:], tab_w1[:].bitcast(U32).indirect(gather_list[:, : BANK // 16]))
 
         h_tiles = {}
-
         sums = {}
+        w1_q1 = []
 
-        def multiply(t, u, a):
+        def moving(u, a):
             cols = slice(u * BANK, (u + 1) * BANK)
-            rows = slice(t * P, (t + 1) * P)
-            if a == 0:
-                sums[t, u] = (psum.tile([P, BANK], F32, name="acc"), psum.tile([P, BANK], F32, name="acc"))
-            acc1, acc2 = sums[t, u]
-            nc.tensor.matmul_mx(out=acc2[:],
-                                lhsT=w2_c[:, a, t * 64 : (t + 1) * 64].bitcast(U8).bitcast(FP4X4),
-                                lhsT_scale=w2_s[:, a, rows],
-                                rhs=v_w[a][:, cols].bitcast(FP8X4),
-                                rhs_scale=(v_sc[:], v_sc1[:].bitcast(U8))[a][:, cols],
-                                start=(a == 0), stop=(a == PASSES - 1))
-            nc.tensor.matmul_mx(out=acc1[:],
-                                lhsT=w1_c[a][:, rows].bitcast(FP8X4), lhsT_scale=w1_s[a][:, rows],
-                                rhs=v_w[a][:, cols].bitcast(FP8X4), rhs_scale=v_sc[4 * a :, cols],
-                                start=(a == 0), stop=(a == PASSES - 1))
+            words = v_w0[:, cols] if a == 0 else v_w1[u][:]
+            return dict(rhs=words.bitcast(FP8X4), rhs_scale=v_sc[a][:, cols], start=(a == 0), stop=(a == PASSES - 1))
+
+        def multiply_w2(t, u):
+            acc = psum.tile([P, BANK], F32, name="acc_w2", tag="bank_w2", bufs=1)
+            for a in range(PASSES):
+                nc.tensor.matmul_mx(out=acc[:], lhsT=w2_c[:, a, t * 64 : (t + 1) * 64].bitcast(U8).bitcast(FP4X4),
+                                    lhsT_scale=w2_s[:, a, t * P : (t + 1) * P], **moving(u, a))
+            second = ring.tile([P, BANK], F32, name="second")
+            nc.scalar.copy(second[:], acc[:])
+            sums[t, u] = second
+
+        def multiply_w1(t, u):
+            acc = psum.tile([P, BANK], F32, name="acc_w1", tag="bank_w1", bufs=3)
+            for a in range(PASSES):
+                codes, scales = w1_q0 if a == 0 else w1_q1[t // 2]
+                m0 = (t if a == 0 else t % 2) * P
+                nc.tensor.matmul_mx(out=acc[:], lhsT=codes[:, m0 : m0 + P].bitcast(FP8X4), lhsT_scale=scales[:, m0 : m0 + P],
+                                    **moving(u, a))
+            sums[t, u] = (acc, sums[t, u])
 
         def smaller(t, u):
-            cols = slice(u * BANK, (u + 1) * BANK)
             if u == 0:
-                h_tiles[t] = ring.tile([P, S], F32, name="h")
-            acc1, acc2 = sums[t, u]
-            second = ring.tile([P, BANK], F32, name="second")
-            nc.scalar.copy(second[:], acc2[:])
-            nc.vector.tensor_tensor(h_tiles[t][:, cols], acc1[:], second[:], ALU.min)
+                h_tiles[t] = ring.tile([P, S], F32, name="h", bufs=2)
+            acc, second = sums[t, u]
+            nc.vector.tensor_tensor(h_tiles[t][:, u * BANK : (u + 1) * BANK], acc[:], second[:], ALU.min)
 
         def project(t, u):
-            multiply(t, u, 0)
-            multiply(t, u, 1)
+            multiply_w2(t, u)
+            multiply_w1(t, u)
             smaller(t, u)
 
-        page4 = keep.tile([P, PACK, T2], F32, name="page4", align_bytes=64)
-
-        def scatter(t, j0, j1):
-            nc.vector.tensor_tensor(pages[t][:].indirect(scatter_list[:, j0 // 16 : j1 // 16]),
-                                    h_tiles[t][:, j0:j1], gains[t // 2][:, t % 2, j0:j1], ALU.mult)
-
-        multiply(0, 0, 0)
-        multiply(0, 1, 0)
-        multiply(0, 0, 1)
+        multiply_w2(0, 0)
+        w1_g1 = [keep.tile([P, 2 * H], BF16, name="w1_g1_lo", tag="slot_o", align_bytes=64),
+                 keep.tile([P, 2 * H], BF16, name="w1_g1_hi", tag="slot_p", align_bytes=64)]
+        interleave(nc.vector.tensor_copy, w1_g1[0], w1_raw1, 0, 2)
+        interleave(nc.scalar.copy, w1_g1[1], w1_raw1, 2, 4)
+        w1_q1.append(quantize(w1_g1[0][:], H // 2, keep, "w1_q1_lo"))
+        multiply_w1(0, 0)
+        v_w1.append(keep.tile([P, BANK], U32, name="v_w1_hi", tag="slot_o", align_bytes=64))
+        nc.vector.tensor_copy(v_w1[1][:], tab_w1[:].bitcast(U32).indirect(gather_list[:, BANK // 16 :]))
         smaller(0, 0)
-        multiply(0, 1, 1)
-        smaller(0, 1)
-        scatter(0, 0, BANK)
+        w1_q1.append(quantize(w1_g1[1][:], H // 2, keep, "w1_q1_hi"))
+        pages.append(keep.tile([P, T2], F32, name="page2", tag="slot_p", align_bytes=64))
+        nc.gpsimd.memset(pages[2][:], 0.0)
+
+        gains_hi = late.tile([P, 2, S], F32, name="gains_hi", tag="slot_b", align_bytes=64)
+        load_gains(gains_hi, 2, 4, 0, S)
+        wf_raw = keep.tile([P, PACK, N], F32, name="wf_raw", tag="slot_a", align_bytes=64)
+        nc.sync.dma_start(wf_raw[:], wf.rearrange("(p j) c -> p j c", j=PACK))
+        starts = [sum(CHUNKS[:c]) for c in range(len(CHUNKS))]
+
+
+        def scatter(t, j0, j1, gains):
+            nc.vector.tensor_tensor(pages[t][:].indirect(scatter_list[:, j0 // 16 : j1 // 16]),
+                                    h_tiles[t][:, j0:j1], gains, ALU.mult)
+
+        scatter(0, 0, BANK, gains_first[:, 0, :])
+        old_sb = keep.tile([P, PACK, T2], F32, name="old_sb", tag="slot_e", align_bytes=64)
+        nc.sync.dma_start(old_sb[:], old.rearrange("(p t) c -> p t c", t=PACK))
+        project(0, 1)
         project(1, 0)
-        scatter(0, BANK, S)
-        nc.scalar.copy(page4[:, 0, :], pages[0][:])
+        scatter(0, BANK, S, gains_rest[:, 0, :])
         project(1, 1)
-        for t in (1, 2):
-            project(t + 1, 0)
-            scatter(t, 0, S)
+        project(2, 0)
+        scatter(1, 0, S, gains_rest[:, 1:3, :].rearrange("p a b -> p (a b)"))
+        project(2, 1)
+        project(3, 0)
+        project(3, 1)
+        pages.append(keep.tile([P, T2], F32, name="page3", tag="slot_v", align_bytes=64))
+        nc.gpsimd.memset(pages[3][:], 0.0)
+        bias = keep.tile([P, PACK], F32, name="bias", tag="slot_o", align_bytes=64)
+        nc.sync.dma_start(bias[:], bf.rearrange("(p m) -> p m", m=PACK))
+        scatter(2, 0, S, gains_hi[:, 0, :])
+        wf_g = keep.tile([P, PACK * N], BF16, name="wf_g", tag="slot_l", align_bytes=64)
+        interleave(nc.scalar.copy, wf_g, wf_raw, 0, PACK)
+        page4 = keep.tile([P, PACK, T2], F32, name="page4", tag="slot_w", align_bytes=64)
+        for t in range(PACK - 1):
             nc.scalar.copy(page4[:, t, :], pages[t][:])
-            project(t + 1, 1)
-        old_planes = old.rearrange("(p t) c -> p t c", t=PACK)
-        old_sb = []
-        for a, (c0, c1) in enumerate(((0, OLD_SPLIT), (OLD_SPLIT, T2))):
-            old_sb.append(keep.tile([P, PACK, c1 - c0], F32, name="old_sb", tag="slot_v%d" % a, align_bytes=64))
-            nc.sync.dma_start(old_sb[a][:], old_planes[:, :, c0:c1])
-        wf_q = quantize(interleave(wf_raw)[:], N, keep, "wf")
-        scatter(3, 0, S)
+        scatter(3, 0, S, gains_hi[:, 1, :])
+        wf_c = late.tile([P, N], U32, name="wf_c", tag="slot_b", align_bytes=64)
+        wf_s = keep.tile([P, N], U8, name="wf_s", align_bytes=64)
+        nc.vector.quantize_mx(out=wf_c[:].bitcast(FP8X4), scales=wf_s[:], in_=wf_g[:])
+        wf_q = (wf_c, wf_s)
 
         out_planes = out.rearrange("(p m) c -> p m c", m=PACK)
 
@@ -201,7 +221,7 @@ def tile_list_zone_map_filter_kernel(tc, tab_words, tab_scales, offs, w1, w2_wor
                 z_tiles[c] = ring.tile([P, PACK * w], BF16, name="z", align_bytes=64)
             d0 = half * w // 2
             cols = slice(c0 + d0, c0 + d0 + w // 2)
-            old_cols = old_sb[0][:, :, cols] if c0 < OLD_SPLIT else old_sb[1][:, :, cols.start - OLD_SPLIT : cols.stop - OLD_SPLIT]
+            old_cols = old_sb[:, :, cols]
             nc.vector.tensor_tensor(z_tiles[c][:, PACK * d0 : PACK * (d0 + w // 2)].rearrange("p (c i t) -> p c t i", i=2, t=PACK),
                                     page4[:, :, cols].rearrange("p t (c i) -> p c t i", i=2),
                                     old_cols.rearrange("p t (c i) -> p c t i", i=2), ALU.min)
@@ -212,7 +232,8 @@ def tile_list_zone_map_filter_kernel(tc, tab_words, tab_scales, offs, w1, w2_wor
             res = late.tile([P, PACK, w], F32, name="res", bufs=4, align_bytes=64)
             for m in range(PACK):
                 rows = slice(m * P, (m + 1) * P)
-                acc = psum.tile([P, BANK], F32, name="acc")
+                tag, bufs = ("bank_out", 4) if c % 2 == 0 else ("bank_w1", 3) if m < 3 else ("bank_w2", 1)
+                acc = psum.tile([P, BANK], F32, name="acc", tag=tag, bufs=bufs)
                 nc.tensor.matmul_mx(out=acc[:, :w], lhsT=wf_q[0][:, rows].bitcast(FP8X4), lhsT_scale=wf_q[1][:, rows],
                                     rhs=z_c[:].bitcast(FP8X4), rhs_scale=z_s[:], start=True, stop=True)
                 if c >= len(CHUNKS) - 2 and m % 2 == 1:

@@ -30,7 +30,7 @@ def tile_list_zone_map_filter_kernel(tc, tab_words, tab_scales, offs, w1, w2_wor
     with ExitStack() as ctx:
         keep = ctx.enter_context(tc.tile_pool(name="keep", bufs=1))
         ring = ctx.enter_context(tc.tile_pool(name="ring", bufs=3))
-        psum = ctx.enter_context(tc.psum_pool(name="psum", bufs=4))
+        psum = ctx.enter_context(tc.psum_pool(name="psum", bufs=1))
 
         gather_list = keep.tile([P, S // 16], U16, name="gather_list")
         scatter_list = keep.tile([P, S // 16], U16, name="scatter_list")
@@ -55,8 +55,8 @@ def tile_list_zone_map_filter_kernel(tc, tab_words, tab_scales, offs, w1, w2_wor
         v_sc1 = keep.tile([P, S // 4], I32, name="v_sc1", align_bytes=64)
         nc.vector.memset(v_sc1[:], 0)
         pages = [keep.tile([P, T2], F32, name="page%d" % t) for t in range(2)]
-        nc.vector.memset(pages[0][:], 0.0)
-        nc.vector.memset(pages[1][:], 0.0)
+        for page in pages:
+            nc.vector.memset(page[:], 0.0)
 
         w1_rows = [w1[a * 512 : (a + 1) * 512, :].rearrange("(p j) c -> p j c", j=PACK) for a in range(PASSES)]
         w1_raw0 = late.tile([P, PACK, H], F32, name="w1_raw0", tag="slot_c", align_bytes=64)
@@ -70,7 +70,7 @@ def tile_list_zone_map_filter_kernel(tc, tab_words, tab_scales, offs, w1, w2_wor
                               w2_scales[:, 4 * q : 4 * q + 4, :].rearrange("a r c -> r a c").bitcast(I32))
 
         v_sc0 = keep.tile([P, S], U8, name="v_sc0", align_bytes=64)
-        v_w0 = keep.tile([P, S], U32, name="v_w0", tag="slot_v", align_bytes=64)
+        v_w0 = keep.tile([P, S], U32, name="v_w0", align_bytes=64)
         nc.vector.tensor_copy(v_w0[:], tab_w0[:].bitcast(U32).indirect(gather_list[:]))
         w1_raw1 = keep.tile([P, PACK, H], F32, name="w1_raw1", tag="slot_a", align_bytes=64)
         nc.sync.dma_start(w1_raw1[:], w1_rows[1])
@@ -88,7 +88,7 @@ def tile_list_zone_map_filter_kernel(tc, tab_words, tab_scales, offs, w1, w2_wor
         gains_first = keep.tile([P, 1, BANK], F32, name="gains_first", tag="slot_e", align_bytes=64)
         load_gains(gains_first, 0, 1, 0, BANK)
 
-        w2_c = keep.tile([P, PASSES, H // 2], I32, name="w2_c", tag="slot_w", align_bytes=64)
+        w2_c = keep.tile([P, PASSES, H // 2], I32, name="w2_c", align_bytes=64)
         w2_s = keep.tile([P, PASSES, H], U8, name="w2_s", align_bytes=64)
         nc.vector.tensor_copy(
             w2_c[:].rearrange("p a c -> p (a c)").bitcast(U16).rearrange("p (a t m) -> p a t m", a=PASSES, t=PACK),
@@ -127,16 +127,16 @@ def tile_list_zone_map_filter_kernel(tc, tab_words, tab_scales, offs, w1, w2_wor
             return dict(rhs=words.bitcast(FP8X4), rhs_scale=v_sc[a][:, cols], start=(a == 0), stop=(a == PASSES - 1))
 
         def multiply_w2(t, u):
-            acc = psum.tile([P, BANK], F32, name="acc_w2", tag="bank_w2", bufs=1)
+            acc = psum.tile([P, BANK], F32, name="acc_w2", tag="bank_w2_%d" % u)
             for a in range(PASSES):
                 nc.tensor.matmul_mx(out=acc[:], lhsT=w2_c[:, a, t * 64 : (t + 1) * 64].bitcast(U8).bitcast(FP4X4),
                                     lhsT_scale=w2_s[:, a, t * P : (t + 1) * P], **moving(u, a))
-            second = ring.tile([P, BANK], F32, name="second")
+            second = keep.tile([P, BANK], F32, name="second", tag="second_%d" % ((2 * t + u) % 4))
             nc.scalar.copy(second[:], acc[:])
             sums[t, u] = second
 
         def multiply_w1(t, u):
-            acc = psum.tile([P, BANK], F32, name="acc_w1", tag="bank_w1", bufs=3)
+            acc = psum.tile([P, BANK], F32, name="acc_w1", tag="bank_w1_%d" % ((2 * t + u) % 4))
             for a in range(PASSES):
                 codes, scales = w1_q0 if a == 0 else w1_q1[t // 2]
                 m0 = (t if a == 0 else t % 2) * P
@@ -157,7 +157,7 @@ def tile_list_zone_map_filter_kernel(tc, tab_words, tab_scales, offs, w1, w2_wor
 
         multiply_w2(0, 0)
         w1_g1 = [keep.tile([P, 2 * H], BF16, name="w1_g1_lo", tag="slot_o", align_bytes=64),
-                 keep.tile([P, 2 * H], BF16, name="w1_g1_hi", tag="slot_p", align_bytes=64)]
+                 keep.tile([P, 2 * H], BF16, name="w1_g1_hi", align_bytes=64)]
         interleave(nc.vector.tensor_copy, w1_g1[0], w1_raw1, 0, 2)
         interleave(nc.scalar.copy, w1_g1[1], w1_raw1, 2, 4)
         w1_q1.append(quantize(w1_g1[0][:], H // 2, keep, "w1_q1_lo"))
@@ -166,8 +166,6 @@ def tile_list_zone_map_filter_kernel(tc, tab_words, tab_scales, offs, w1, w2_wor
         nc.vector.tensor_copy(v_w1[1][:], tab_w1[:].bitcast(U32).indirect(gather_list[:, BANK // 16 :]))
         smaller(0, 0)
         w1_q1.append(quantize(w1_g1[1][:], H // 2, keep, "w1_q1_hi"))
-        pages.append(keep.tile([P, T2], F32, name="page2", tag="slot_p", align_bytes=64))
-        nc.gpsimd.memset(pages[2][:], 0.0)
 
         gains_hi = late.tile([P, 2, S], F32, name="gains_hi", tag="slot_b", align_bytes=64)
         load_gains(gains_hi, 2, 4, 0, S)
@@ -177,7 +175,7 @@ def tile_list_zone_map_filter_kernel(tc, tab_words, tab_scales, offs, w1, w2_wor
 
 
         def scatter(t, j0, j1, gains):
-            nc.vector.tensor_tensor(pages[t][:].indirect(scatter_list[:, j0 // 16 : j1 // 16]),
+            nc.vector.tensor_tensor(pages[t % 2][:].indirect(scatter_list[:, j0 // 16 : j1 // 16]),
                                     h_tiles[t][:, j0:j1], gains, ALU.mult)
 
         scatter(0, 0, BANK, gains_first[:, 0, :])
@@ -192,17 +190,16 @@ def tile_list_zone_map_filter_kernel(tc, tab_words, tab_scales, offs, w1, w2_wor
         project(2, 1)
         project(3, 0)
         project(3, 1)
-        pages.append(keep.tile([P, T2], F32, name="page3", tag="slot_v", align_bytes=64))
-        nc.gpsimd.memset(pages[3][:], 0.0)
         bias = keep.tile([P, PACK], F32, name="bias", tag="slot_o", align_bytes=64)
         nc.sync.dma_start(bias[:], bf.rearrange("(p m) -> p m", m=PACK))
+        page4 = keep.tile([P, PACK, T2], F32, name="page4", tag="second_1")
+        nc.scalar.copy(page4[:, 0, :], pages[0][:])
         scatter(2, 0, S, gains_hi[:, 0, :])
+        nc.scalar.copy(page4[:, 1, :], pages[1][:])
         wf_g = keep.tile([P, PACK * N], BF16, name="wf_g", tag="slot_l", align_bytes=64)
         interleave(nc.scalar.copy, wf_g, wf_raw, 0, PACK)
-        page4 = keep.tile([P, PACK, T2], F32, name="page4", tag="slot_w", align_bytes=64)
-        for t in range(PACK - 1):
-            nc.scalar.copy(page4[:, t, :], pages[t][:])
         scatter(3, 0, S, gains_hi[:, 1, :])
+        nc.scalar.copy(page4[:, 2, :], pages[0][:])
         wf_c = late.tile([P, N], U32, name="wf_c", tag="slot_b", align_bytes=64)
         wf_s = keep.tile([P, N], U8, name="wf_s", align_bytes=64)
         nc.vector.quantize_mx(out=wf_c[:].bitcast(FP8X4), scales=wf_s[:], in_=wf_g[:])
@@ -211,7 +208,7 @@ def tile_list_zone_map_filter_kernel(tc, tab_words, tab_scales, offs, w1, w2_wor
         out_planes = out.rearrange("(p m) c -> p m c", m=PACK)
 
         for c0, c1 in ((0, 256), (256, OLD_SPLIT), (OLD_SPLIT, T2)):
-            nc.scalar.copy(page4[:, 3, c0:c1], pages[3][:, c0:c1])
+            nc.scalar.copy(page4[:, 3, c0:c1], pages[1][:, c0:c1])
 
         z_tiles = {}
 
@@ -232,8 +229,8 @@ def tile_list_zone_map_filter_kernel(tc, tab_words, tab_scales, offs, w1, w2_wor
             res = late.tile([P, PACK, w], F32, name="res", bufs=4, align_bytes=64)
             for m in range(PACK):
                 rows = slice(m * P, (m + 1) * P)
-                tag, bufs = ("bank_out", 4) if c % 2 == 0 else ("bank_w1", 3) if m < 3 else ("bank_w2", 1)
-                acc = psum.tile([P, BANK], F32, name="acc", tag=tag, bufs=bufs)
+                tag = "bank_w1_%d" % m if c % 2 == 1 else "bank_out_%d" % m if m < 2 else "bank_w2_%d" % (m - 2)
+                acc = psum.tile([P, BANK], F32, name="acc", tag=tag)
                 nc.tensor.matmul_mx(out=acc[:, :w], lhsT=wf_q[0][:, rows].bitcast(FP8X4), lhsT_scale=wf_q[1][:, rows],
                                     rhs=z_c[:].bitcast(FP8X4), rhs_scale=z_s[:], start=True, stop=True)
                 if c >= len(CHUNKS) - 2 and m % 2 == 1:

@@ -8,7 +8,7 @@ PACK = 4
 PASSES = K // (P * PACK)
 BANK = 512
 HALVES = S // BANK
-CHUNKS = [256, 512, 512, 256, 256, 128, 128]
+CHUNKS = [128, 128] + [256] * 6 + [128, 128]
 OLD_SPLIT = 768
 
 FLOPS = 2 * (2 * K * H * S + H * N * T2)
@@ -167,10 +167,11 @@ def tile_list_zone_map_filter_kernel(tc, tab_words, tab_scales, offs, w1, w2_wor
         smaller(0, 0)
         w1_q1.append(quantize(w1_g1[1][:], H // 2, keep, "w1_q1_hi"))
 
-        gains_hi = late.tile([P, 2, S], F32, name="gains_hi", tag="slot_b", align_bytes=64)
-        load_gains(gains_hi, 2, 4, 0, S)
         wf_raw = keep.tile([P, PACK, N], F32, name="wf_raw", tag="slot_a", align_bytes=64)
         nc.sync.dma_start(wf_raw[:], wf.rearrange("(p j) c -> p j c", j=PACK))
+        gains_hi = late.tile([P, 2, S], F32, name="gains_hi", tag="slot_b", align_bytes=64)
+        load_gains(gains_hi[:, 0:1, :], 2, 3, 0, S)
+        load_gains(gains_hi[:, 1:2, :], 3, 4, 0, S)
         starts = [sum(CHUNKS[:c]) for c in range(len(CHUNKS))]
 
 
@@ -192,12 +193,12 @@ def tile_list_zone_map_filter_kernel(tc, tab_words, tab_scales, offs, w1, w2_wor
         project(3, 1)
         bias = keep.tile([P, PACK], F32, name="bias", tag="slot_o", align_bytes=64)
         nc.sync.dma_start(bias[:], bf.rearrange("(p m) -> p m", m=PACK))
-        page4 = keep.tile([P, PACK, T2], F32, name="page4", tag="second_1")
+        wf_g = keep.tile([P, PACK * N], BF16, name="wf_g", tag="slot_l", align_bytes=64)
+        interleave(nc.scalar.copy, wf_g, wf_raw, 0, PACK)
+        page4 = keep.tile([P, PACK, T2], F32, name="page4", tag="slot_a", align_bytes=64)
         nc.scalar.copy(page4[:, 0, :], pages[0][:])
         scatter(2, 0, S, gains_hi[:, 0, :])
         nc.scalar.copy(page4[:, 1, :], pages[1][:])
-        wf_g = keep.tile([P, PACK * N], BF16, name="wf_g", tag="slot_l", align_bytes=64)
-        interleave(nc.scalar.copy, wf_g, wf_raw, 0, PACK)
         scatter(3, 0, S, gains_hi[:, 1, :])
         nc.scalar.copy(page4[:, 2, :], pages[0][:])
         wf_c = late.tile([P, N], U32, name="wf_c", tag="slot_b", align_bytes=64)
@@ -207,21 +208,21 @@ def tile_list_zone_map_filter_kernel(tc, tab_words, tab_scales, offs, w1, w2_wor
 
         out_planes = out.rearrange("(p m) c -> p m c", m=PACK)
 
-        for c0, c1 in ((0, 256), (256, OLD_SPLIT), (OLD_SPLIT, T2)):
+        nc.sync.dma_start(page4[:, 3, 1024:], pages[1][:, 1024:])
+        for c0, c1 in ((0, 128), (128, 256), (256, 512), (512, 1024)):
             nc.scalar.copy(page4[:, 3, c0:c1], pages[1][:, c0:c1])
 
         z_tiles = {}
 
-        def lower(c, half):
+        def lower(c, part, parts):
             c0, w = starts[c], CHUNKS[c]
-            if half == 0:
+            if part == 0:
                 z_tiles[c] = ring.tile([P, PACK * w], BF16, name="z", align_bytes=64)
-            d0 = half * w // 2
-            cols = slice(c0 + d0, c0 + d0 + w // 2)
-            old_cols = old_sb[:, :, cols]
-            nc.vector.tensor_tensor(z_tiles[c][:, PACK * d0 : PACK * (d0 + w // 2)].rearrange("p (c i t) -> p c t i", i=2, t=PACK),
+            d0, d1 = part * w // parts, (part + 1) * w // parts
+            cols = slice(c0 + d0, c0 + d1)
+            nc.vector.tensor_tensor(z_tiles[c][:, PACK * d0 : PACK * d1].rearrange("p (c i t) -> p c t i", i=2, t=PACK),
                                     page4[:, :, cols].rearrange("p t (c i) -> p c t i", i=2),
-                                    old_cols.rearrange("p t (c i) -> p c t i", i=2), ALU.min)
+                                    old_sb[:, :, cols].rearrange("p t (c i) -> p c t i", i=2), ALU.min)
 
         def test(c, z):
             c0, w = starts[c], CHUNKS[c]
@@ -233,7 +234,7 @@ def tile_list_zone_map_filter_kernel(tc, tab_words, tab_scales, offs, w1, w2_wor
                 acc = psum.tile([P, BANK], F32, name="acc", tag=tag)
                 nc.tensor.matmul_mx(out=acc[:, :w], lhsT=wf_q[0][:, rows].bitcast(FP8X4), lhsT_scale=wf_q[1][:, rows],
                                     rhs=z_c[:].bitcast(FP8X4), rhs_scale=z_s[:], start=True, stop=True)
-                if c >= len(CHUNKS) - 2 and m % 2 == 1:
+                if c == len(CHUNKS) - 1 and m % 2 == 1:
                     nc.vector.tensor_scalar(res[:, m, :], acc[:, :w], bias[:, m : m + 1], 0.0, ALU.add, ALU.max)
                 else:
                     nc.scalar.activation(res[:, m, :], acc[:, :w], ACT.Relu, bias=bias[:, m : m + 1])
@@ -241,11 +242,8 @@ def tile_list_zone_map_filter_kernel(tc, tab_words, tab_scales, offs, w1, w2_wor
                 if (m + 1) % group == 0:
                     nc.sync.dma_start(out_planes[:, m + 1 - group : m + 1, c0 : c0 + w], res[:, m + 1 - group : m + 1, :])
 
-        lower(0, 0)
-        lower(0, 1)
+        lower(0, 0, 1)
         for c in range(len(CHUNKS)):
             if c + 1 < len(CHUNKS):
-                lower(c + 1, 0)
+                lower(c + 1, 0, 1)
             test(c, z_tiles[c])
-            if c + 1 < len(CHUNKS):
-                lower(c + 1, 1)

@@ -44,11 +44,6 @@ def tile_list_zone_map_filter_kernel(tc, tab_words, tab_scales, offs, w1, w2_wor
         nc.sync.dma_start(tab_sc[8:24, :], tab_scales[1].bitcast(I32))
         for q in range(4):
             nc.sync.dma_start(tab_sc[32 * q : 32 * q + 4, :], tab_scales[0, 4 * q : 4 * q + 4, :].bitcast(I32))
-        with tc.tile_pool(name="warm", bufs=1) as warm:
-            seed = warm.tile([P, 8], F32, name="seed")
-            warmed = warm.tile([P, 8], F32, name="warmed")
-            nc.vector.memset(seed[:], 0.0)
-            nc.scalar.activation(warmed[:], seed[:], ACT.Relu)
         late = ctx.enter_context(tc.tile_pool(name="late", bufs=1))
         w2_sc_raw = late.tile([P, PASSES, H // 4], I32, name="w2_sc_raw", align_bytes=64)
         nc.vector.memset(w2_sc_raw[:], 0)

@@ -7,9 +7,12 @@ P = 128
 PACK = 4
 PASSES = K // (P * PACK)
 BANK = 512
-HALVES = S // BANK
+QUAD = 32
+SCALE_ROWS = 4
+PARKED = 8
+AHEAD = 4
 CHUNKS = [128, 128] + [256] * 6 + [128, 128]
-OLD_SPLIT = 768
+LAST_PLANE_CUTS = [0, 128, 256, 512, 1024]
 
 FLOPS = 2 * (2 * K * H * S + H * N * T2)
 
@@ -41,9 +44,10 @@ def tile_list_zone_map_filter_kernel(tc, tab_words, tab_scales, offs, w1, w2_wor
 
         tab_sc = keep.tile([P, T // 4], I32, name="tab_sc", tag="slot_e", align_bytes=64)
         nc.vector.memset(tab_sc[:], 0)
-        nc.sync.dma_start(tab_sc[8:24, :], tab_scales[1].bitcast(I32))
+        nc.scalar.dma_start(tab_sc[PARKED : PARKED + 16, :], tab_scales[1].bitcast(I32))
         for q in range(4):
-            nc.sync.dma_start(tab_sc[32 * q : 32 * q + 4, :], tab_scales[0, 4 * q : 4 * q + 4, :].bitcast(I32))
+            nc.scalar.dma_start(tab_sc[QUAD * q : QUAD * q + SCALE_ROWS, :],
+                                tab_scales[0, SCALE_ROWS * q : SCALE_ROWS * (q + 1), :].bitcast(I32))
         late = ctx.enter_context(tc.tile_pool(name="late", bufs=1))
         w2_sc_raw = late.tile([P, PASSES, H // 4], I32, name="w2_sc_raw", align_bytes=64)
         nc.vector.memset(w2_sc_raw[:], 0)
@@ -53,7 +57,7 @@ def tile_list_zone_map_filter_kernel(tc, tab_words, tab_scales, offs, w1, w2_wor
         for page in pages:
             nc.vector.memset(page[:], 0.0)
 
-        w1_rows = [w1[a * 512 : (a + 1) * 512, :].rearrange("(p j) c -> p j c", j=PACK) for a in range(PASSES)]
+        w1_rows = [w1[a * P * PACK : (a + 1) * P * PACK, :].rearrange("(p j) c -> p j c", j=PACK) for a in range(PASSES)]
         w1_raw0 = late.tile([P, PACK, H], F32, name="w1_raw0", tag="slot_c", align_bytes=64)
         w2_raw = late.tile([P, PASSES, H // 2], I32, name="w2_raw", align_bytes=64)
         tab_w1 = late.tile([P, T], I32, name="tab_w1", tag="slot_b", align_bytes=64)
@@ -61,8 +65,8 @@ def tile_list_zone_map_filter_kernel(tc, tab_words, tab_scales, offs, w1, w2_wor
         nc.sync.dma_start(w2_raw[:], w2_words.rearrange("a p c -> p a c").bitcast(I32))
         nc.sync.dma_start(tab_w1[:], tab_words[1].rearrange("p t i -> p (t i)").bitcast(I32))
         for q in range(4):
-            nc.sync.dma_start(w2_sc_raw[32 * q : 32 * q + 4, :, :],
-                              w2_scales[:, 4 * q : 4 * q + 4, :].rearrange("a r c -> r a c").bitcast(I32))
+            nc.sync.dma_start(w2_sc_raw[QUAD * q : QUAD * q + SCALE_ROWS, :, :],
+                              w2_scales[:, SCALE_ROWS * q : SCALE_ROWS * (q + 1), :].rearrange("a r c -> r a c").bitcast(I32))
 
         v_sc0 = keep.tile([P, S], U8, name="v_sc0", align_bytes=64)
         v_w0 = keep.tile([P, S], U32, name="v_w0", align_bytes=64)
@@ -71,17 +75,18 @@ def tile_list_zone_map_filter_kernel(tc, tab_words, tab_scales, offs, w1, w2_wor
         nc.sync.dma_start(w1_raw1[:], w1_rows[1])
         nc.vector.tensor_copy(v_sc0[:], tab_sc[:].bitcast(U8).indirect(gather_list[:]))
         for q in range(4):
-            nc.sync.dma_start(v_sc1[32 * q : 32 * q + 4, :], v_sc0[8 + 4 * q : 12 + 4 * q, :].bitcast(I32))
+            parked = PARKED + SCALE_ROWS * q
+            nc.sync.dma_start(v_sc1[QUAD * q : QUAD * q + SCALE_ROWS, :], v_sc0[parked : parked + SCALE_ROWS, :].bitcast(I32))
         v_sc = [v_sc0[:], v_sc1[:].bitcast(U8)]
 
         wgs_rows = wgs.rearrange("(m t) j -> m t j", t=PACK)
 
-        def load_gains(tile_view, t0, t1, j0, j1):
+        def load_gains(gains, t, j0, j1):
             for q in (0, 2, 1, 3):
-                nc.sync.dma_start(tile_view[32 * q : 32 * q + 32], wgs_rows[:, t0:t1, j0:j1])
+                nc.sync.dma_start(gains[QUAD * q : QUAD * (q + 1)], wgs_rows[:, t : t + 1, j0:j1])
 
         gains_first = keep.tile([P, 1, BANK], F32, name="gains_first", tag="slot_e", align_bytes=64)
-        load_gains(gains_first, 0, 1, 0, BANK)
+        load_gains(gains_first, 0, 0, BANK)
 
         w2_c = keep.tile([P, PASSES, H // 2], I32, name="w2_c", align_bytes=64)
         w2_s = keep.tile([P, PASSES, H], U8, name="w2_s", align_bytes=64)
@@ -106,14 +111,15 @@ def tile_list_zone_map_filter_kernel(tc, tab_words, tab_scales, offs, w1, w2_wor
         interleave(nc.scalar.copy, w1_g0, w1_raw0, 0, PACK)
         w1_q0 = quantize(w1_g0[:], H, keep, "w1_q0")
         gains_rest = late.tile([P, 3, BANK], F32, name="gains_rest", tag="slot_c", align_bytes=64)
-        load_gains(gains_rest[:, 0:1, :], 0, 1, BANK, S)
-        load_gains(gains_rest[:, 1:3, :].rearrange("p (t a) b -> p t (a b)", t=1), 1, 2, 0, S)
+        load_gains(gains_rest[:, 0:1, :], 0, BANK, S)
+        load_gains(gains_rest[:, 1:3, :].rearrange("p (t a) b -> p t (a b)", t=1), 1, 0, S)
 
         v_w1 = [keep.tile([P, BANK], U32, name="v_w1_lo", tag="slot_l", align_bytes=64)]
         nc.vector.tensor_copy(v_w1[0][:], tab_w1[:].bitcast(U32).indirect(gather_list[:, : BANK // 16]))
 
         h_tiles = {}
-        sums = {}
+        w1_sums = {}
+        w2_sums = {}
         w1_q1 = []
 
         def moving(u, a):
@@ -124,26 +130,25 @@ def tile_list_zone_map_filter_kernel(tc, tab_words, tab_scales, offs, w1, w2_wor
         def multiply_w2(t, u):
             acc = psum.tile([P, BANK], F32, name="acc_w2", tag="bank_w2_%d" % u)
             for a in range(PASSES):
-                nc.tensor.matmul_mx(out=acc[:], lhsT=w2_c[:, a, t * 64 : (t + 1) * 64].bitcast(U8).bitcast(FP4X4),
+                nc.tensor.matmul_mx(out=acc[:], lhsT=w2_c[:, a, t * P // 2 : (t + 1) * P // 2].bitcast(U8).bitcast(FP4X4),
                                     lhsT_scale=w2_s[:, a, t * P : (t + 1) * P], **moving(u, a))
-            second = keep.tile([P, BANK], F32, name="second", tag="second_%d" % ((2 * t + u) % 4))
+            second = keep.tile([P, BANK], F32, name="second", tag="second_%d" % ((2 * t + u) % AHEAD))
             nc.scalar.copy(second[:], acc[:])
-            sums[t, u] = second
+            w2_sums[t, u] = second
 
         def multiply_w1(t, u):
-            acc = psum.tile([P, BANK], F32, name="acc_w1", tag="bank_w1_%d" % ((2 * t + u) % 4))
+            acc = psum.tile([P, BANK], F32, name="acc_w1", tag="bank_w1_%d" % ((2 * t + u) % AHEAD))
             for a in range(PASSES):
                 codes, scales = w1_q0 if a == 0 else w1_q1[t // 2]
                 m0 = (t if a == 0 else t % 2) * P
                 nc.tensor.matmul_mx(out=acc[:], lhsT=codes[:, m0 : m0 + P].bitcast(FP8X4), lhsT_scale=scales[:, m0 : m0 + P],
                                     **moving(u, a))
-            sums[t, u] = (acc, sums[t, u])
+            w1_sums[t, u] = acc
 
         def smaller(t, u):
             if u == 0:
                 h_tiles[t] = ring.tile([P, S], F32, name="h", bufs=2)
-            acc, second = sums[t, u]
-            nc.vector.tensor_tensor(h_tiles[t][:, u * BANK : (u + 1) * BANK], acc[:], second[:], ALU.min)
+            nc.vector.tensor_tensor(h_tiles[t][:, u * BANK : (u + 1) * BANK], w1_sums[t, u][:], w2_sums[t, u][:], ALU.min)
 
         def project(t, u):
             multiply_w2(t, u)
@@ -165,10 +170,8 @@ def tile_list_zone_map_filter_kernel(tc, tab_words, tab_scales, offs, w1, w2_wor
         wf_raw = keep.tile([P, PACK, N], F32, name="wf_raw", tag="slot_a", align_bytes=64)
         nc.sync.dma_start(wf_raw[:], wf.rearrange("(p j) c -> p j c", j=PACK))
         gains_hi = late.tile([P, 2, S], F32, name="gains_hi", tag="slot_b", align_bytes=64)
-        load_gains(gains_hi[:, 0:1, :], 2, 3, 0, S)
-        load_gains(gains_hi[:, 1:2, :], 3, 4, 0, S)
-        starts = [sum(CHUNKS[:c]) for c in range(len(CHUNKS))]
-
+        load_gains(gains_hi[:, 0:1, :], 2, 0, S)
+        load_gains(gains_hi[:, 1:2, :], 3, 0, S)
 
         def scatter(t, j0, j1, gains):
             nc.vector.tensor_tensor(pages[t % 2][:].indirect(scatter_list[:, j0 // 16 : j1 // 16]),
@@ -199,46 +202,41 @@ def tile_list_zone_map_filter_kernel(tc, tab_words, tab_scales, offs, w1, w2_wor
         wf_c = late.tile([P, N], U32, name="wf_c", tag="slot_b", align_bytes=64)
         wf_s = keep.tile([P, N], U8, name="wf_s", align_bytes=64)
         nc.vector.quantize_mx(out=wf_c[:].bitcast(FP8X4), scales=wf_s[:], in_=wf_g[:])
-        wf_q = (wf_c, wf_s)
 
-        out_planes = out.rearrange("(p m) c -> p m c", m=PACK)
+        nc.sync.dma_start(page4[:, PACK - 1, LAST_PLANE_CUTS[-1] :], pages[1][:, LAST_PLANE_CUTS[-1] :])
+        for c0, c1 in zip(LAST_PLANE_CUTS, LAST_PLANE_CUTS[1:]):
+            nc.scalar.copy(page4[:, PACK - 1, c0:c1], pages[1][:, c0:c1])
 
-        nc.sync.dma_start(page4[:, 3, 1024:], pages[1][:, 1024:])
-        for c0, c1 in ((0, 128), (128, 256), (256, 512), (512, 1024)):
-            nc.scalar.copy(page4[:, 3, c0:c1], pages[1][:, c0:c1])
+        out_rows = out.rearrange("(p m) c -> p m c", m=PACK)
+        chunk_cols = [slice(sum(CHUNKS[:c]), sum(CHUNKS[: c + 1])) for c in range(len(CHUNKS))]
 
-        z_tiles = {}
+        def lower(c):
+            z = ring.tile([P, PACK * CHUNKS[c]], BF16, name="z", align_bytes=64)
+            nc.vector.tensor_tensor(z[:].rearrange("p (c i t) -> p c t i", i=2, t=PACK),
+                                    page4[:, :, chunk_cols[c]].rearrange("p t (c i) -> p c t i", i=2),
+                                    old_sb[:, :, chunk_cols[c]].rearrange("p t (c i) -> p c t i", i=2), ALU.min)
+            return z
 
-        def lower(c, part, parts):
-            c0, w = starts[c], CHUNKS[c]
-            if part == 0:
-                z_tiles[c] = ring.tile([P, PACK * w], BF16, name="z", align_bytes=64)
-            d0, d1 = part * w // parts, (part + 1) * w // parts
-            cols = slice(c0 + d0, c0 + d1)
-            nc.vector.tensor_tensor(z_tiles[c][:, PACK * d0 : PACK * d1].rearrange("p (c i t) -> p c t i", i=2, t=PACK),
-                                    page4[:, :, cols].rearrange("p t (c i) -> p c t i", i=2),
-                                    old_sb[:, :, cols].rearrange("p t (c i) -> p c t i", i=2), ALU.min)
+        bank_tags = [["bank_out_0", "bank_out_1", "bank_w2_0", "bank_w2_1"], ["bank_w1_%d" % m for m in range(AHEAD)]]
 
-        def test(c, z):
-            c0, w = starts[c], CHUNKS[c]
+        def apply_filters(c, z):
+            w = CHUNKS[c]
             z_c, z_s = quantize(z[:], w, ring, "zq")
             res = late.tile([P, PACK, w], F32, name="res", bufs=4, align_bytes=64)
             for m in range(PACK):
                 rows = slice(m * P, (m + 1) * P)
-                tag = "bank_w1_%d" % m if c % 2 == 1 else "bank_out_%d" % m if m < 2 else "bank_w2_%d" % (m - 2)
-                acc = psum.tile([P, BANK], F32, name="acc", tag=tag)
-                nc.tensor.matmul_mx(out=acc[:, :w], lhsT=wf_q[0][:, rows].bitcast(FP8X4), lhsT_scale=wf_q[1][:, rows],
+                acc = psum.tile([P, BANK], F32, name="acc", tag=bank_tags[c % 2][m])
+                nc.tensor.matmul_mx(out=acc[:, :w], lhsT=wf_c[:, rows].bitcast(FP8X4), lhsT_scale=wf_s[:, rows],
                                     rhs=z_c[:].bitcast(FP8X4), rhs_scale=z_s[:], start=True, stop=True)
                 if c == len(CHUNKS) - 1 and m % 2 == 1:
                     nc.vector.tensor_scalar(res[:, m, :], acc[:, :w], bias[:, m : m + 1], 0.0, ALU.add, ALU.max)
                 else:
                     nc.scalar.activation(res[:, m, :], acc[:, :w], ACT.Relu, bias=bias[:, m : m + 1])
-                group = 2 if w == BANK else PACK
-                if (m + 1) % group == 0:
-                    nc.sync.dma_start(out_planes[:, m + 1 - group : m + 1, c0 : c0 + w], res[:, m + 1 - group : m + 1, :])
+            nc.sync.dma_start(out_rows[:, :, chunk_cols[c]], res[:])
 
-        lower(0, 0, 1)
+        z_next = lower(0)
         for c in range(len(CHUNKS)):
+            z_now = z_next
             if c + 1 < len(CHUNKS):
-                lower(c + 1, 0, 1)
-            test(c, z_tiles[c])
+                z_next = lower(c + 1)
+            apply_filters(c, z_now)

@@ -9,7 +9,9 @@ PASSES = K // (P * PACK)
 BANK = 512
 QUAD = 32
 SCALE_ROWS = 4
-PARKED = 8
+OLD_AT = 1024
+W2_REST_AT = OLD_AT + PACK * T2 * 4
+PLANE_GROUPS = [(0, 1), (1, 2), (2, 4)]
 AHEAD = 4
 CHUNKS = [128, 128] + [256] * 6 + [128, 128]
 LAST_PLANE_CUTS = [0, 128, 256, 512, 1024]
@@ -38,68 +40,79 @@ def tile_list_zone_map_filter_kernel(tc, tab_words, tab_scales, offs, w1, w2_wor
         gather_list = keep.tile([P, S // 16], U16, name="gather_list")
         scatter_list = keep.tile([P, S // 16], U16, name="scatter_list")
         nc.sync.dma_start(gather_list[:], offs)
-        tab_w0 = keep.tile([P, T], I32, name="tab_w0", tag="slot_a", align_bytes=64)
-        nc.sync.dma_start(tab_w0[:], tab_words[0].rearrange("p t i -> p (t i)").bitcast(I32))
         nc.sync.dma_start(scatter_list[:], offs2)
-
-        tab_sc = keep.tile([P, T // 4], I32, name="tab_sc", tag="slot_e", align_bytes=64)
-        nc.vector.memset(tab_sc[:], 0)
-        nc.scalar.dma_start(tab_sc[PARKED : PARKED + 16, :], tab_scales[1].bitcast(I32))
-        for q in range(4):
-            nc.scalar.dma_start(tab_sc[QUAD * q : QUAD * q + SCALE_ROWS, :],
-                                tab_scales[0, SCALE_ROWS * q : SCALE_ROWS * (q + 1), :].bitcast(I32))
         late = ctx.enter_context(tc.tile_pool(name="late", bufs=1))
-        w2_sc_raw = late.tile([P, PASSES, H // 4], I32, name="w2_sc_raw", align_bytes=64)
-        nc.vector.memset(w2_sc_raw[:], 0)
-        v_sc1 = keep.tile([P, S // 4], I32, name="v_sc1", align_bytes=64)
-        nc.vector.memset(v_sc1[:], 0)
+        tab_w0 = keep.tile([P, T], I32, name="tab_w0", tag="slot_a", align_bytes=64)
+        placed = ctx.enter_context(tc.tile_pool(name="placed", bufs=1))
+        tab_w1 = placed.tile([P, T], I32, name="tab_w1", offset=0, align_bytes=64)
+        w2_raw = late.tile([P, PASSES, H // 2], I32, name="w2_raw", align_bytes=64)
+        tab_sc = late.tile([P, T // 4], I32, name="tab_sc", tag="slot_c", align_bytes=64)
+        nc.sync.dma_start(tab_sc[:QUAD, :], tab_scales.rearrange("a q t -> q a t").bitcast(I32))
+        nc.vector.memset(tab_sc[QUAD : 2 * QUAD, :], 0)
+        nc.vector.memset(tab_sc[2 * QUAD :, :], 0)
+        nc.sync.dma_start(tab_w0[:], tab_words[0].rearrange("p t i -> p (t i)").bitcast(I32))
+        nc.sync.dma_start(tab_w1[:], tab_words[1].rearrange("p t i -> p (t i)").bitcast(I32))
+        nc.sync.dma_start(w2_raw[:], w2_words.rearrange("a p c -> p a c").bitcast(I32))
+
+        w2_sc_raw = keep.tile([P, PASSES, H // 4], I32, name="w2_sc_raw", align_bytes=64)
+        nc.gpsimd.memset(w2_sc_raw[:], 0)
+        for q in range(4):
+            nc.scalar.dma_start(w2_sc_raw[QUAD * q : QUAD * q + SCALE_ROWS, :, :],
+                                w2_scales[:, SCALE_ROWS * q : SCALE_ROWS * (q + 1), :].rearrange("a r c -> r a c").bitcast(I32))
+        v_sc_moved = keep.tile([P, PASSES, S // 4], I32, name="v_sc_moved", align_bytes=64)
+        nc.gpsimd.memset(v_sc_moved[:], 0)
         pages = [keep.tile([P, T2], F32, name="page%d" % t) for t in range(2)]
         for page in pages:
-            nc.vector.memset(page[:], 0.0)
-
-        w1_rows = [w1[a * P * PACK : (a + 1) * P * PACK, :].rearrange("(p j) c -> p j c", j=PACK) for a in range(PASSES)]
-        w1_raw0 = late.tile([P, PACK, H], F32, name="w1_raw0", tag="slot_c", align_bytes=64)
-        w2_raw = late.tile([P, PASSES, H // 2], I32, name="w2_raw", align_bytes=64)
-        tab_w1 = late.tile([P, T], I32, name="tab_w1", tag="slot_b", align_bytes=64)
-        nc.sync.dma_start(w1_raw0[:], w1_rows[0])
-        nc.sync.dma_start(w2_raw[:], w2_words.rearrange("a p c -> p a c").bitcast(I32))
-        nc.sync.dma_start(tab_w1[:], tab_words[1].rearrange("p t i -> p (t i)").bitcast(I32))
-        for q in range(4):
-            nc.sync.dma_start(w2_sc_raw[QUAD * q : QUAD * q + SCALE_ROWS, :, :],
-                              w2_scales[:, SCALE_ROWS * q : SCALE_ROWS * (q + 1), :].rearrange("a r c -> r a c").bitcast(I32))
+            nc.gpsimd.memset(page[:], 0.0)
 
         v_sc0 = keep.tile([P, S], U8, name="v_sc0", align_bytes=64)
-        v_w0 = keep.tile([P, S], U32, name="v_w0", align_bytes=64)
-        nc.vector.tensor_copy(v_w0[:], tab_w0[:].bitcast(U32).indirect(gather_list[:]))
+        nc.vector.tensor_copy(v_sc0[:], tab_sc[:].bitcast(U8).indirect(gather_list[:]))
+        w1_rows = [w1[a * P * PACK : (a + 1) * P * PACK, :].rearrange("(p j) c -> p j c", j=PACK) for a in range(PASSES)]
+        w1_raw0 = late.tile([P, PACK, H], F32, name="w1_raw0", tag="slot_c", align_bytes=64)
+        nc.sync.dma_start(w1_raw0[:], w1_rows[0])
+        for q in range(4):
+            rows = PASSES * SCALE_ROWS
+            nc.sync.dma_start(v_sc_moved[QUAD * q : QUAD * q + SCALE_ROWS, :, :], v_sc0[rows * q : rows * (q + 1), :].bitcast(I32))
+        v_sc = [v_sc_moved[:, a, :].bitcast(U8) for a in range(PASSES)]
+        v_w = [keep.tile([P, S], U32, name="v_w%d" % a, align_bytes=64) for a in range(PASSES)]
+        nc.vector.tensor_copy(v_w[0][:], tab_w0[:].bitcast(U32).indirect(gather_list[:]))
         w1_raw1 = keep.tile([P, PACK, H], F32, name="w1_raw1", tag="slot_a", align_bytes=64)
         nc.sync.dma_start(w1_raw1[:], w1_rows[1])
-        nc.vector.tensor_copy(v_sc0[:], tab_sc[:].bitcast(U8).indirect(gather_list[:]))
-        for q in range(4):
-            parked = PARKED + SCALE_ROWS * q
-            nc.sync.dma_start(v_sc1[QUAD * q : QUAD * q + SCALE_ROWS, :], v_sc0[parked : parked + SCALE_ROWS, :].bitcast(I32))
-        v_sc = [v_sc0[:], v_sc1[:].bitcast(U8)]
+        nc.vector.tensor_copy(v_w[1][:], tab_w1[:].bitcast(U32).indirect(gather_list[:]))
 
-        wgs_rows = wgs.rearrange("(m t) j -> m t j", t=PACK)
+        w2_q = {}
+
+        def prepare_w2(t0, t1, offset):
+            n = t1 - t0
+            codes = placed.tile([P, PASSES, n * P // 2], I32, name="w2_c%d" % t0, offset=offset, align_bytes=64)
+            scales = placed.tile([P, PASSES, n * P // 4], I32, name="w2_s%d" % t0, offset=offset + PASSES * n * P * 2, align_bytes=64)
+            for dst, src, dtype, run in ((codes, w2_raw, U32, 4), (scales, w2_sc_raw, U16, 8)):
+                nc.vector.tensor_copy(
+                    dst[:].rearrange("p a c -> p (a c)").bitcast(dtype).rearrange("p (a t g i) -> p a g t i", a=PASSES, t=n, i=run),
+                    src[:].rearrange("p a c -> p (a c)").bitcast(dtype).rearrange("p (a g i t) -> p a g t i", a=PASSES, t=PACK, i=run)[:, :, :, t0:t1, :])
+            for t in range(t0, t1):
+                w2_q[t] = (codes, scales, t - t0)
+
+        prepare_w2(0, 1, 0)
+
+        def planes(rows):
+            return rows.rearrange("(g t e) c -> t g e c", t=PACK, e=2)
 
         def load_gains(gains, t, j0, j1):
             for q in (0, 2, 1, 3):
-                nc.sync.dma_start(gains[QUAD * q : QUAD * (q + 1)], wgs_rows[:, t : t + 1, j0:j1])
+                nc.sync.dma_start(gains[QUAD * q : QUAD * (q + 1), :], planes(wgs)[t][:, :, j0:j1])
 
-        gains_first = keep.tile([P, 1, BANK], F32, name="gains_first", tag="slot_e", align_bytes=64)
-        load_gains(gains_first, 0, 0, BANK)
+        gains_first = placed.tile([P, BANK], F32, name="gains_first", offset=OLD_AT, align_bytes=64)
+        load_gains(gains_first[:], 0, 0, BANK)
 
-        w2_c = keep.tile([P, PASSES, H // 2], I32, name="w2_c", align_bytes=64)
-        w2_s = keep.tile([P, PASSES, H], U8, name="w2_s", align_bytes=64)
-        nc.vector.tensor_copy(
-            w2_c[:].rearrange("p a c -> p (a c)").bitcast(U16).rearrange("p (a t m) -> p a t m", a=PASSES, t=PACK),
-            w2_raw[:].rearrange("p a c -> p (a c)").bitcast(U16).rearrange("p (a m t) -> p a t m", a=PASSES, t=PACK))
-        nc.vector.tensor_copy(
-            w2_s[:].rearrange("p a (t m) -> p a t m", t=PACK),
-            w2_sc_raw[:].rearrange("p a c -> p (a c)").bitcast(U8).rearrange("p (a m t) -> p a t m", a=PASSES, t=PACK))
-
-        def interleave(copy, grouped, raw, t0, t1):
-            copy(grouped[:].rearrange("p (t m j) -> p m t j", t=t1 - t0, j=PACK),
-                 raw[:].rearrange("p j (m t) -> p m t j", t=PACK)[:, :, t0:t1, :])
+        def interleave(copy, raw, t0, t1, name, tag):
+            if name == "w1_1_0_g":
+                grouped = placed.tile([P, (t1 - t0) * H], BF16, name=name, offset=W2_REST_AT + 1024, align_bytes=64)
+            else:
+                grouped = keep.tile([P, (t1 - t0) * H], BF16, name=name, tag=tag, align_bytes=64)
+            copy(grouped[:].rearrange("p (t g e j) -> p g t j e", t=t1 - t0, e=2, j=PACK),
+                 raw[:].rearrange("p j (g t e) -> p g t j e", t=PACK, e=2)[:, :, t0:t1, :, :])
+            return grouped
 
         def quantize(grouped, width, pool, name):
             codes = pool.tile([P, width], U32, name=name + "_c", align_bytes=64)
@@ -107,42 +120,47 @@ def tile_list_zone_map_filter_kernel(tc, tab_words, tab_scales, offs, w1, w2_wor
             nc.vector.quantize_mx(out=codes[:].bitcast(FP8X4), scales=scales[:], in_=grouped)
             return codes, scales
 
-        w1_g0 = keep.tile([P, PACK * H], BF16, name="w1_g0", align_bytes=64)
-        interleave(nc.scalar.copy, w1_g0, w1_raw0, 0, PACK)
-        w1_q0 = quantize(w1_g0[:], H, keep, "w1_q0")
-        gains_rest = late.tile([P, 3, BANK], F32, name="gains_rest", tag="slot_c", align_bytes=64)
-        load_gains(gains_rest[:, 0:1, :], 0, BANK, S)
-        load_gains(gains_rest[:, 1:3, :].rearrange("p (t a) b -> p t (a b)", t=1), 1, 0, S)
+        w1_q = {}
 
-        v_w1 = [keep.tile([P, BANK], U32, name="v_w1_lo", tag="slot_l", align_bytes=64)]
-        nc.vector.tensor_copy(v_w1[0][:], tab_w1[:].bitcast(U32).indirect(gather_list[:, : BANK // 16]))
+        def prepare_w1(copy, raw, a, t0, t1):
+            name = "w1_%d_%d" % (a, t0)
+            grouped = interleave(copy, raw, t0, t1, name + "_g", name + "_g")
+            codes, scales = quantize(grouped[:], (t1 - t0) * P, keep, name)
+            for t in range(t0, t1):
+                w1_q[a, t] = (codes, scales, (t - t0) * P)
+
+        prepare_w1(nc.vector.tensor_copy, w1_raw0, 0, 0, 2)
+        prepare_w1(nc.scalar.copy, w1_raw0, 0, 2, 4)
+        gains_rest = late.tile([P, 3 * BANK], F32, name="gains_rest", tag="slot_c", align_bytes=64)
+        load_gains(gains_rest[:, :BANK], 0, BANK, S)
+        load_gains(gains_rest[:, BANK:], 1, 0, S)
 
         h_tiles = {}
         w1_sums = {}
         w2_sums = {}
-        w1_q1 = []
 
-        def moving(u, a):
+        def moving(u, a, first):
             cols = slice(u * BANK, (u + 1) * BANK)
-            words = v_w0[:, cols] if a == 0 else v_w1[u][:]
-            return dict(rhs=words.bitcast(FP8X4), rhs_scale=v_sc[a][:, cols], start=(a == 0), stop=(a == PASSES - 1))
+            words = v_w[a][:, cols]
+            return dict(rhs=words.bitcast(FP8X4), rhs_scale=v_sc[a][:, cols], start=(a == first), stop=(a != first))
 
         def multiply_w2(t, u):
             acc = psum.tile([P, BANK], F32, name="acc_w2", tag="bank_w2_%d" % u)
+            codes, scales, i = w2_q[t]
             for a in range(PASSES):
-                nc.tensor.matmul_mx(out=acc[:], lhsT=w2_c[:, a, t * P // 2 : (t + 1) * P // 2].bitcast(U8).bitcast(FP4X4),
-                                    lhsT_scale=w2_s[:, a, t * P : (t + 1) * P], **moving(u, a))
+                nc.tensor.matmul_mx(out=acc[:], lhsT=codes[:, a, i * P // 2 : (i + 1) * P // 2].bitcast(U8).bitcast(FP4X4),
+                                    lhsT_scale=scales[:, a, i * P // 4 : (i + 1) * P // 4].bitcast(U8), **moving(u, a, 0))
             second = keep.tile([P, BANK], F32, name="second", tag="second_%d" % ((2 * t + u) % AHEAD))
             nc.scalar.copy(second[:], acc[:])
             w2_sums[t, u] = second
 
         def multiply_w1(t, u):
             acc = psum.tile([P, BANK], F32, name="acc_w1", tag="bank_w1_%d" % ((2 * t + u) % AHEAD))
-            for a in range(PASSES):
-                codes, scales = w1_q0 if a == 0 else w1_q1[t // 2]
-                m0 = (t if a == 0 else t % 2) * P
+            first = 0 if (t, u) == (0, 0) else 1
+            for a in (first, 1 - first):
+                codes, scales, m0 = w1_q[a, t]
                 nc.tensor.matmul_mx(out=acc[:], lhsT=codes[:, m0 : m0 + P].bitcast(FP8X4), lhsT_scale=scales[:, m0 : m0 + P],
-                                    **moving(u, a))
+                                    **moving(u, a, first))
             w1_sums[t, u] = acc
 
         def smaller(t, u):
@@ -156,50 +174,51 @@ def tile_list_zone_map_filter_kernel(tc, tab_words, tab_scales, offs, w1, w2_wor
             smaller(t, u)
 
         multiply_w2(0, 0)
-        w1_g1 = [keep.tile([P, 2 * H], BF16, name="w1_g1_lo", tag="slot_o", align_bytes=64),
-                 keep.tile([P, 2 * H], BF16, name="w1_g1_hi", align_bytes=64)]
-        interleave(nc.vector.tensor_copy, w1_g1[0], w1_raw1, 0, 2)
-        interleave(nc.scalar.copy, w1_g1[1], w1_raw1, 2, 4)
-        w1_q1.append(quantize(w1_g1[0][:], H // 2, keep, "w1_q1_lo"))
+        prepare_w1(nc.vector.tensor_copy, w1_raw1, 1, *PLANE_GROUPS[0])
         multiply_w1(0, 0)
-        v_w1.append(keep.tile([P, BANK], U32, name="v_w1_hi", tag="slot_o", align_bytes=64))
-        nc.vector.tensor_copy(v_w1[1][:], tab_w1[:].bitcast(U32).indirect(gather_list[:, BANK // 16 :]))
         smaller(0, 0)
-        w1_q1.append(quantize(w1_g1[1][:], H // 2, keep, "w1_q1_hi"))
+        prepare_w2(1, PACK, W2_REST_AT)
+        prepare_w1(nc.vector.tensor_copy, w1_raw1, 1, *PLANE_GROUPS[1])
+        prepare_w1(nc.scalar.copy, w1_raw1, 1, *PLANE_GROUPS[2])
 
         wf_raw = keep.tile([P, PACK, N], F32, name="wf_raw", tag="slot_a", align_bytes=64)
-        nc.sync.dma_start(wf_raw[:], wf.rearrange("(p j) c -> p j c", j=PACK))
-        gains_hi = late.tile([P, 2, S], F32, name="gains_hi", tag="slot_b", align_bytes=64)
-        load_gains(gains_hi[:, 0:1, :], 2, 0, S)
-        load_gains(gains_hi[:, 1:2, :], 3, 0, S)
+        for t in range(PACK):
+            nc.sync.dma_start(wf_raw[:, t, :], planes(wf)[t])
+        gains_hi = keep.tile([P, 2, S], F32, name="gains_hi", tag="w1_1_2_g", align_bytes=64)
+        load_gains(gains_hi[:, 0, :], 2, 0, S)
+        load_gains(gains_hi[:, 1, :], 3, 0, S)
 
         def scatter(t, j0, j1, gains):
             nc.vector.tensor_tensor(pages[t % 2][:].indirect(scatter_list[:, j0 // 16 : j1 // 16]),
                                     h_tiles[t][:, j0:j1], gains, ALU.mult)
 
-        scatter(0, 0, BANK, gains_first[:, 0, :])
-        old_sb = keep.tile([P, PACK, T2], F32, name="old_sb", tag="slot_e", align_bytes=64)
-        nc.sync.dma_start(old_sb[:], old.rearrange("(p t) c -> p t c", t=PACK))
+        scatter(0, 0, BANK, gains_first[:])
+        old_sb = placed.tile([P, PACK, T2], F32, name="old_sb", offset=OLD_AT, align_bytes=64)
+        for t in range(PACK):
+            nc.sync.dma_start(old_sb[:, t, :], planes(old)[t])
         project(0, 1)
         project(1, 0)
-        scatter(0, BANK, S, gains_rest[:, 0, :])
+        scatter(0, BANK, S, gains_rest[:, :BANK])
         project(1, 1)
         project(2, 0)
-        scatter(1, 0, S, gains_rest[:, 1:3, :].rearrange("p a b -> p (a b)"))
+        scatter(1, 0, S, gains_rest[:, BANK:])
         project(2, 1)
         project(3, 0)
         project(3, 1)
-        bias = keep.tile([P, PACK], F32, name="bias", tag="slot_o", align_bytes=64)
+        bias = keep.tile([P, PACK], F32, name="bias", tag="w1_1_1_g", align_bytes=64)
         nc.sync.dma_start(bias[:], bf.rearrange("(p m) -> p m", m=PACK))
-        wf_g = keep.tile([P, PACK * N], BF16, name="wf_g", tag="slot_l", align_bytes=64)
-        interleave(nc.scalar.copy, wf_g, wf_raw, 0, PACK)
+        wf_g = keep.tile([P, PACK * N], BF16, name="wf_g", align_bytes=64)
+        for q in range(4):
+            cols = slice(QUAD * q, QUAD * (q + 1))
+            nc.scalar.copy(wf_g[:].rearrange("p (m c j) -> p c m j", m=PACK, j=PACK)[:, cols],
+                           wf_raw[:].rearrange("p j (c m) -> p c m j", m=PACK)[:, cols])
         page4 = keep.tile([P, PACK, T2], F32, name="page4", tag="slot_a", align_bytes=64)
         nc.scalar.copy(page4[:, 0, :], pages[0][:])
         scatter(2, 0, S, gains_hi[:, 0, :])
         nc.scalar.copy(page4[:, 1, :], pages[1][:])
         scatter(3, 0, S, gains_hi[:, 1, :])
         nc.scalar.copy(page4[:, 2, :], pages[0][:])
-        wf_c = late.tile([P, N], U32, name="wf_c", tag="slot_b", align_bytes=64)
+        wf_c = keep.tile([P, N], U32, name="wf_c", tag="w1_1_2_g", align_bytes=64)
         wf_s = keep.tile([P, N], U8, name="wf_s", align_bytes=64)
         nc.vector.quantize_mx(out=wf_c[:].bitcast(FP8X4), scales=wf_s[:], in_=wf_g[:])
 

@@ -9,7 +9,9 @@ PASSES = K // (P * PACK)
 BANK = 512
 QUAD = 32
 SCALE_ROWS = 4
-OLD_AT = 1024
+W2_FIRST_AT = T2 * 4
+TAB_AT = W2_FIRST_AT - 64
+OLD_AT = W2_FIRST_AT + 1024
 W2_REST_AT = OLD_AT + PACK * T2 * 4
 PLANE_GROUPS = [(0, 1), (1, 2), (2, 4)]
 AHEAD = 4
@@ -44,7 +46,7 @@ def tile_list_zone_map_filter_kernel(tc, tab_words, tab_scales, offs, w1, w2_wor
         late = ctx.enter_context(tc.tile_pool(name="late", bufs=1))
         tab_w0 = keep.tile([P, T], I32, name="tab_w0", tag="slot_a", align_bytes=64)
         placed = ctx.enter_context(tc.tile_pool(name="placed", bufs=1))
-        tab_w1 = placed.tile([P, T], I32, name="tab_w1", offset=0, align_bytes=64)
+        tab_w1 = placed.tile([P, T], I32, name="tab_w1", offset=TAB_AT, align_bytes=64)
         w2_raw = late.tile([P, PASSES, H // 2], I32, name="w2_raw", align_bytes=64)
         tab_sc = late.tile([P, T // 4], I32, name="tab_sc", tag="slot_c", align_bytes=64)
         nc.sync.dma_start(tab_sc[:QUAD, :], tab_scales.rearrange("a q t -> q a t").bitcast(I32))
@@ -55,15 +57,14 @@ def tile_list_zone_map_filter_kernel(tc, tab_words, tab_scales, offs, w1, w2_wor
         nc.sync.dma_start(w2_raw[:], w2_words.rearrange("a p c -> p a c").bitcast(I32))
 
         w2_sc_raw = keep.tile([P, PASSES, H // 4], I32, name="w2_sc_raw", align_bytes=64)
-        nc.gpsimd.memset(w2_sc_raw[:], 0)
+        nc.vector.memset(w2_sc_raw[:], 0)
         for q in range(4):
             nc.scalar.dma_start(w2_sc_raw[QUAD * q : QUAD * q + SCALE_ROWS, :, :],
                                 w2_scales[:, SCALE_ROWS * q : SCALE_ROWS * (q + 1), :].rearrange("a r c -> r a c").bitcast(I32))
         v_sc_moved = keep.tile([P, PASSES, S // 4], I32, name="v_sc_moved", align_bytes=64)
-        nc.gpsimd.memset(v_sc_moved[:], 0)
-        pages = [keep.tile([P, T2], F32, name="page%d" % t) for t in range(2)]
-        for page in pages:
-            nc.gpsimd.memset(page[:], 0.0)
+        nc.vector.memset(v_sc_moved[:], 0)
+        pages = [keep.tile([P, T2], F32, name="page0")]
+        nc.vector.memset(pages[0][:], 0.0)
 
         v_sc0 = keep.tile([P, S], U8, name="v_sc0", align_bytes=64)
         nc.vector.tensor_copy(v_sc0[:], tab_sc[:].bitcast(U8).indirect(gather_list[:]))
@@ -93,7 +94,7 @@ def tile_list_zone_map_filter_kernel(tc, tab_words, tab_scales, offs, w1, w2_wor
             for t in range(t0, t1):
                 w2_q[t] = (codes, scales, t - t0)
 
-        prepare_w2(0, 1, 0)
+        prepare_w2(0, 1, W2_FIRST_AT)
 
         def planes(rows):
             return rows.rearrange("(g t e) c -> t g e c", t=PACK, e=2)
@@ -131,6 +132,8 @@ def tile_list_zone_map_filter_kernel(tc, tab_words, tab_scales, offs, w1, w2_wor
 
         prepare_w1(nc.vector.tensor_copy, w1_raw0, 0, 0, 2)
         prepare_w1(nc.scalar.copy, w1_raw0, 0, 2, 4)
+        pages.append(placed.tile([P, T2], F32, name="page1", offset=0, align_bytes=64))
+        nc.vector.memset(pages[1][:], 0.0)
         gains_rest = late.tile([P, 3 * BANK], F32, name="gains_rest", tag="slot_c", align_bytes=64)
         load_gains(gains_rest[:, :BANK], 0, BANK, S)
         load_gains(gains_rest[:, BANK:], 1, 0, S)

@@ -130,7 +130,7 @@ def tile_list_zone_map_filter_kernel(tc, tab_words, tab_scales, offs, w1, w2_wor
             for t in range(t0, t1):
                 w1_q[a, t] = (codes, scales, (t - t0) * P)
 
-        prepare_w1(nc.vector.tensor_copy, w1_raw0, 0, 0, 2)
+        prepare_w1(nc.scalar.copy, w1_raw0, 0, 0, 2)
         prepare_w1(nc.scalar.copy, w1_raw0, 0, 2, 4)
         pages.append(placed.tile([P, T2], F32, name="page1", offset=0, align_bytes=64))
         nc.vector.memset(pages[1][:], 0.0)
@@ -181,7 +181,7 @@ def tile_list_zone_map_filter_kernel(tc, tab_words, tab_scales, offs, w1, w2_wor
         multiply_w1(0, 0)
         smaller(0, 0)
         prepare_w2(1, PACK, W2_REST_AT)
-        prepare_w1(nc.vector.tensor_copy, w1_raw1, 1, *PLANE_GROUPS[1])
+        prepare_w1(nc.scalar.copy, w1_raw1, 1, *PLANE_GROUPS[1])
         prepare_w1(nc.scalar.copy, w1_raw1, 1, *PLANE_GROUPS[2])
 
         wf_raw = keep.tile([P, PACK, N], F32, name="wf_raw", tag="slot_a", align_bytes=64)

@@ -9,12 +9,12 @@ PASSES = K // (P * PACK)
 BANK = 512
 QUAD = 32
 SCALE_ROWS = 4
+AHEAD = 4
 W2_FIRST_AT = T2 * 4
 TAB_AT = W2_FIRST_AT - 64
 OLD_AT = W2_FIRST_AT + 1024
 W2_REST_AT = OLD_AT + PACK * T2 * 4
-PLANE_GROUPS = [(0, 1), (1, 2), (2, 4)]
-AHEAD = 4
+W1_URGENT_AT = W2_REST_AT + 1024
 CHUNKS = [128, 128] + [256] * 6 + [128, 128]
 LAST_PLANE_CUTS = [0, 128, 256, 512, 1024]
 
@@ -66,14 +66,14 @@ def tile_list_zone_map_filter_kernel(tc, tab_words, tab_scales, offs, w1, w2_wor
         pages = [keep.tile([P, T2], F32, name="page0")]
         nc.vector.memset(pages[0][:], 0.0)
 
-        v_sc0 = keep.tile([P, S], U8, name="v_sc0", align_bytes=64)
-        nc.vector.tensor_copy(v_sc0[:], tab_sc[:].bitcast(U8).indirect(gather_list[:]))
+        v_sc_rows = keep.tile([P, S], U8, name="v_sc_rows", align_bytes=64)
+        nc.vector.tensor_copy(v_sc_rows[:], tab_sc[:].bitcast(U8).indirect(gather_list[:]))
         w1_rows = [w1[a * P * PACK : (a + 1) * P * PACK, :].rearrange("(p j) c -> p j c", j=PACK) for a in range(PASSES)]
         w1_raw0 = late.tile([P, PACK, H], F32, name="w1_raw0", tag="slot_c", align_bytes=64)
         nc.sync.dma_start(w1_raw0[:], w1_rows[0])
         for q in range(4):
             rows = PASSES * SCALE_ROWS
-            nc.sync.dma_start(v_sc_moved[QUAD * q : QUAD * q + SCALE_ROWS, :, :], v_sc0[rows * q : rows * (q + 1), :].bitcast(I32))
+            nc.sync.dma_start(v_sc_moved[QUAD * q : QUAD * q + SCALE_ROWS, :, :], v_sc_rows[rows * q : rows * (q + 1), :].bitcast(I32))
         v_sc = [v_sc_moved[:, a, :].bitcast(U8) for a in range(PASSES)]
         v_w = [keep.tile([P, S], U32, name="v_w%d" % a, align_bytes=64) for a in range(PASSES)]
         nc.vector.tensor_copy(v_w[0][:], tab_w0[:].bitcast(U32).indirect(gather_list[:]))
@@ -106,15 +106,6 @@ def tile_list_zone_map_filter_kernel(tc, tab_words, tab_scales, offs, w1, w2_wor
         gains_first = placed.tile([P, BANK], F32, name="gains_first", offset=OLD_AT, align_bytes=64)
         load_gains(gains_first[:], 0, 0, BANK)
 
-        def interleave(copy, raw, t0, t1, name, tag):
-            if name == "w1_1_0_g":
-                grouped = placed.tile([P, (t1 - t0) * H], BF16, name=name, offset=W2_REST_AT + 1024, align_bytes=64)
-            else:
-                grouped = keep.tile([P, (t1 - t0) * H], BF16, name=name, tag=tag, align_bytes=64)
-            copy(grouped[:].rearrange("p (t g e j) -> p g t j e", t=t1 - t0, e=2, j=PACK),
-                 raw[:].rearrange("p j (g t e) -> p g t j e", t=PACK, e=2)[:, :, t0:t1, :, :])
-            return grouped
-
         def quantize(grouped, width, pool, name):
             codes = pool.tile([P, width], U32, name=name + "_c", align_bytes=64)
             scales = pool.tile([P, width], U8, name=name + "_s", align_bytes=64)
@@ -123,15 +114,17 @@ def tile_list_zone_map_filter_kernel(tc, tab_words, tab_scales, offs, w1, w2_wor
 
         w1_q = {}
 
-        def prepare_w1(copy, raw, a, t0, t1):
+        def prepare_w1(copy, raw, a, t0, t1, pool, **where):
             name = "w1_%d_%d" % (a, t0)
-            grouped = interleave(copy, raw, t0, t1, name + "_g", name + "_g")
+            grouped = pool.tile([P, (t1 - t0) * H], BF16, name=name + "_g", align_bytes=64, **where)
+            copy(grouped[:].rearrange("p (t g e j) -> p g t j e", t=t1 - t0, e=2, j=PACK),
+                 raw[:].rearrange("p j (g t e) -> p g t j e", t=PACK, e=2)[:, :, t0:t1, :, :])
             codes, scales = quantize(grouped[:], (t1 - t0) * P, keep, name)
             for t in range(t0, t1):
                 w1_q[a, t] = (codes, scales, (t - t0) * P)
 
-        prepare_w1(nc.scalar.copy, w1_raw0, 0, 0, 2)
-        prepare_w1(nc.scalar.copy, w1_raw0, 0, 2, 4)
+        prepare_w1(nc.scalar.copy, w1_raw0, 0, 0, 2, keep)
+        prepare_w1(nc.scalar.copy, w1_raw0, 0, 2, 4, keep)
         pages.append(placed.tile([P, T2], F32, name="page1", offset=0, align_bytes=64))
         nc.vector.memset(pages[1][:], 0.0)
         gains_rest = late.tile([P, 3 * BANK], F32, name="gains_rest", tag="slot_c", align_bytes=64)
@@ -144,8 +137,7 @@ def tile_list_zone_map_filter_kernel(tc, tab_words, tab_scales, offs, w1, w2_wor
 
         def moving(u, a, first):
             cols = slice(u * BANK, (u + 1) * BANK)
-            words = v_w[a][:, cols]
-            return dict(rhs=words.bitcast(FP8X4), rhs_scale=v_sc[a][:, cols], start=(a == first), stop=(a != first))
+            return dict(rhs=v_w[a][:, cols].bitcast(FP8X4), rhs_scale=v_sc[a][:, cols], start=(a == first), stop=(a != first))
 
         def multiply_w2(t, u):
             acc = psum.tile([P, BANK], F32, name="acc_w2", tag="bank_w2_%d" % u)
@@ -177,17 +169,17 @@ def tile_list_zone_map_filter_kernel(tc, tab_words, tab_scales, offs, w1, w2_wor
             smaller(t, u)
 
         multiply_w2(0, 0)
-        prepare_w1(nc.vector.tensor_copy, w1_raw1, 1, *PLANE_GROUPS[0])
+        prepare_w1(nc.vector.tensor_copy, w1_raw1, 1, 0, 1, placed, offset=W1_URGENT_AT)
         multiply_w1(0, 0)
         smaller(0, 0)
         prepare_w2(1, PACK, W2_REST_AT)
-        prepare_w1(nc.scalar.copy, w1_raw1, 1, *PLANE_GROUPS[1])
-        prepare_w1(nc.scalar.copy, w1_raw1, 1, *PLANE_GROUPS[2])
+        prepare_w1(nc.scalar.copy, w1_raw1, 1, 1, 2, keep, tag="slot_bias")
+        prepare_w1(nc.scalar.copy, w1_raw1, 1, 2, 4, keep, tag="slot_g")
 
         wf_raw = keep.tile([P, PACK, N], F32, name="wf_raw", tag="slot_a", align_bytes=64)
         for t in range(PACK):
             nc.sync.dma_start(wf_raw[:, t, :], planes(wf)[t])
-        gains_hi = keep.tile([P, 2, S], F32, name="gains_hi", tag="w1_1_2_g", align_bytes=64)
+        gains_hi = keep.tile([P, 2, S], F32, name="gains_hi", tag="slot_g", align_bytes=64)
         load_gains(gains_hi[:, 0, :], 2, 0, S)
         load_gains(gains_hi[:, 1, :], 3, 0, S)
 
@@ -208,7 +200,7 @@ def tile_list_zone_map_filter_kernel(tc, tab_words, tab_scales, offs, w1, w2_wor
         project(2, 1)
         project(3, 0)
         project(3, 1)
-        bias = keep.tile([P, PACK], F32, name="bias", tag="w1_1_1_g", align_bytes=64)
+        bias = keep.tile([P, PACK], F32, name="bias", tag="slot_bias", align_bytes=64)
         nc.sync.dma_start(bias[:], bf.rearrange("(p m) -> p m", m=PACK))
         wf_g = keep.tile([P, PACK * N], BF16, name="wf_g", align_bytes=64)
         for q in range(4):
@@ -221,7 +213,7 @@ def tile_list_zone_map_filter_kernel(tc, tab_words, tab_scales, offs, w1, w2_wor
         nc.scalar.copy(page4[:, 1, :], pages[1][:])
         scatter(3, 0, S, gains_hi[:, 1, :])
         nc.scalar.copy(page4[:, 2, :], pages[0][:])
-        wf_c = keep.tile([P, N], U32, name="wf_c", tag="w1_1_2_g", align_bytes=64)
+        wf_c = keep.tile([P, N], U32, name="wf_c", tag="slot_g", align_bytes=64)
         wf_s = keep.tile([P, N], U8, name="wf_s", align_bytes=64)
         nc.vector.quantize_mx(out=wf_c[:].bitcast(FP8X4), scales=wf_s[:], in_=wf_g[:])
 
@@ -244,7 +236,7 @@ def tile_list_zone_map_filter_kernel(tc, tab_words, tab_scales, offs, w1, w2_wor
         def apply_filters(c, z):
             w = CHUNKS[c]
             z_c, z_s = quantize(z[:], w, ring, "zq")
-            res = late.tile([P, PACK, w], F32, name="res", bufs=4, align_bytes=64)
+            res = late.tile([P, PACK, w], F32, name="res", bufs=8, align_bytes=64)
             for m in range(PACK):
                 rows = slice(m * P, (m + 1) * P)
                 acc = psum.tile([P, BANK], F32, name="acc", tag=bank_tags[c % 2][m])
@@ -254,7 +246,8 @@ def tile_list_zone_map_filter_kernel(tc, tab_words, tab_scales, offs, w1, w2_wor
                     nc.vector.tensor_scalar(res[:, m, :], acc[:, :w], bias[:, m : m + 1], 0.0, ALU.add, ALU.max)
                 else:
                     nc.scalar.activation(res[:, m, :], acc[:, :w], ACT.Relu, bias=bias[:, m : m + 1])
-            nc.sync.dma_start(out_rows[:, :, chunk_cols[c]], res[:])
+                if m % 2 == 1:
+                    nc.sync.dma_start(out_rows[:, m - 1 : m + 1, chunk_cols[c]], res[:, m - 1 : m + 1, :])
 
         z_next = lower(0)
         for c in range(len(CHUNKS)):

@@ -184,8 +184,10 @@ def tile_list_zone_map_filter_kernel(tc, tab_words, tab_scales, offs, w1, w2_wor
         load_gains(gains_hi[:, 1, :], 3, 0, S)
 
         def scatter(t, j0, j1, gains):
-            nc.vector.tensor_tensor(pages[t % 2][:].indirect(scatter_list[:, j0 // 16 : j1 // 16]),
-                                    h_tiles[t][:, j0:j1], gains, ALU.mult)
+            scaled = ring.tile([P, j1 - j0], F32, name="scaled", bufs=2)
+            for c0 in range(0, j1 - j0, BANK):
+                nc.gpsimd.tensor_tensor(scaled[:, c0 : c0 + BANK], h_tiles[t][:, j0 + c0 : j0 + c0 + BANK], gains[:, c0 : c0 + BANK], ALU.mult)
+            nc.vector.tensor_copy(pages[t % 2][:].indirect(scatter_list[:, j0 // 16 : j1 // 16]), scaled[:])
 
         scatter(0, 0, BANK, gains_first[:])
         old_sb = placed.tile([P, PACK, T2], F32, name="old_sb", offset=OLD_AT, align_bytes=64)

@@ -184,6 +184,9 @@ def tile_list_zone_map_filter_kernel(tc, tab_words, tab_scales, offs, w1, w2_wor
         load_gains(gains_hi[:, 1, :], 3, 0, S)
 
         def scatter(t, j0, j1, gains):
+            if (t, j0) == (0, 0):
+                nc.vector.tensor_tensor(pages[0][:].indirect(scatter_list[:, j0 // 16 : j1 // 16]), h_tiles[t][:, j0:j1], gains, ALU.mult)
+                return
             scaled = ring.tile([P, j1 - j0], F32, name="scaled", bufs=2)
             for c0 in range(0, j1 - j0, BANK):
                 nc.gpsimd.tensor_tensor(scaled[:, c0 : c0 + BANK], h_tiles[t][:, j0 + c0 : j0 + c0 + BANK], gains[:, c0 : c0 + BANK], ALU.mult)
@@ -191,8 +194,9 @@ def tile_list_zone_map_filter_kernel(tc, tab_words, tab_scales, offs, w1, w2_wor
 
         scatter(0, 0, BANK, gains_first[:])
         old_sb = placed.tile([P, PACK, T2], F32, name="old_sb", offset=OLD_AT, align_bytes=64)
-        for t in range(PACK):
-            nc.sync.dma_start(old_sb[:, t, :], planes(old)[t])
+        for cols in (slice(0, T2 // 2), slice(T2 // 2, T2)):
+            for t in range(PACK):
+                nc.sync.dma_start(old_sb[:, t, cols], planes(old)[t][:, :, cols])
         project(0, 1)
         project(1, 0)
         scatter(0, BANK, S, gains_rest[:, :BANK])

@@ -50,30 +50,41 @@ def tile_list_zone_map_filter_kernel(tc, tab_words, tab_scales, offs, w1, w2_wor
         w2_raw = late.tile([P, PASSES, H // 2], I32, name="w2_raw", align_bytes=64)
         tab_sc = late.tile([P, T // 4], I32, name="tab_sc", tag="slot_c", align_bytes=64)
         nc.sync.dma_start(tab_sc[:QUAD, :], tab_scales.rearrange("a q t -> q a t").bitcast(I32))
+        w2_sc_rows = late.tile([P, H // 4], I32, name="w2_sc_rows", align_bytes=64)
+        nc.sync.dma_start(w2_sc_rows[:QUAD, :], w2_scales.rearrange("a q c -> q a c").bitcast(I32))
         nc.vector.memset(tab_sc[QUAD : 2 * QUAD, :], 0)
         nc.vector.memset(tab_sc[2 * QUAD :, :], 0)
         nc.sync.dma_start(tab_w0[:], tab_words[0].rearrange("p t i -> p (t i)").bitcast(I32))
         nc.sync.dma_start(tab_w1[:], tab_words[1].rearrange("p t i -> p (t i)").bitcast(I32))
         nc.sync.dma_start(w2_raw[:], w2_words.rearrange("a p c -> p a c").bitcast(I32))
 
-        w2_sc_raw = keep.tile([P, PASSES, H // 4], I32, name="w2_sc_raw", align_bytes=64)
-        nc.vector.memset(w2_sc_raw[:], 0)
-        for q in range(4):
-            nc.scalar.dma_start(w2_sc_raw[QUAD * q : QUAD * q + SCALE_ROWS, :, :],
-                                w2_scales[:, SCALE_ROWS * q : SCALE_ROWS * (q + 1), :].rearrange("a r c -> r a c").bitcast(I32))
+        w2_sc = [keep.tile([P, PASSES, n * P // 4], I32, name="w2_sc%d" % n, align_bytes=64) for n in (1, PACK - 1)]
+        for tile in w2_sc:
+            nc.vector.memset(tile[:], 0)
         v_sc_moved = keep.tile([P, PASSES, S // 4], I32, name="v_sc_moved", align_bytes=64)
         nc.vector.memset(v_sc_moved[:], 0)
         pages = [keep.tile([P, T2], F32, name="page0")]
         nc.vector.memset(pages[0][:], 0.0)
+
+        def move_rows(dst, src):
+            rows = PASSES * SCALE_ROWS
+            for q in (0, 2, 1, 3):
+                nc.sync.dma_start(dst[QUAD * q : QUAD * q + SCALE_ROWS, :, :], src[rows * q : rows * (q + 1), :])
+
+        def stage_w2_scales(t0, t1, dst, pool, **where):
+            staged = pool.tile([P, (t1 - t0) * P // 4], I32, name="w2_staged%d" % t0, align_bytes=64, **where)
+            nc.vector.tensor_copy(staged[:QUAD, :].bitcast(U16).rearrange("p (t g i) -> p g t i", t=t1 - t0, i=8),
+                                  w2_sc_rows[:QUAD, :].bitcast(U16).rearrange("p (g i t) -> p g t i", t=PACK, i=8)[:, :, t0:t1, :])
+            move_rows(dst, staged)
+
+        stage_w2_scales(0, 1, w2_sc[0], keep)
 
         v_sc_rows = keep.tile([P, S], U8, name="v_sc_rows", align_bytes=64)
         nc.vector.tensor_copy(v_sc_rows[:], tab_sc[:].bitcast(U8).indirect(gather_list[:]))
         w1_rows = [w1[a * P * PACK : (a + 1) * P * PACK, :].rearrange("(p j) c -> p j c", j=PACK) for a in range(PASSES)]
         w1_raw0 = late.tile([P, PACK, H], F32, name="w1_raw0", tag="slot_c", align_bytes=64)
         nc.sync.dma_start(w1_raw0[:], w1_rows[0])
-        for q in range(4):
-            rows = PASSES * SCALE_ROWS
-            nc.sync.dma_start(v_sc_moved[QUAD * q : QUAD * q + SCALE_ROWS, :, :], v_sc_rows[rows * q : rows * (q + 1), :].bitcast(I32))
+        move_rows(v_sc_moved, v_sc_rows[:].bitcast(I32))
         v_sc = [v_sc_moved[:, a, :].bitcast(U8) for a in range(PASSES)]
         v_w = [keep.tile([P, S], U32, name="v_w%d" % a, align_bytes=64) for a in range(PASSES)]
         nc.vector.tensor_copy(v_w[0][:], tab_w0[:].bitcast(U32).indirect(gather_list[:]))
@@ -86,11 +97,10 @@ def tile_list_zone_map_filter_kernel(tc, tab_words, tab_scales, offs, w1, w2_wor
         def prepare_w2(t0, t1, offset):
             n = t1 - t0
             codes = placed.tile([P, PASSES, n * P // 2], I32, name="w2_c%d" % t0, offset=offset, align_bytes=64)
-            scales = placed.tile([P, PASSES, n * P // 4], I32, name="w2_s%d" % t0, offset=offset + PASSES * n * P * 2, align_bytes=64)
-            for dst, src, dtype, run in ((codes, w2_raw, U32, 4), (scales, w2_sc_raw, U16, 8)):
-                nc.vector.tensor_copy(
-                    dst[:].rearrange("p a c -> p (a c)").bitcast(dtype).rearrange("p (a t g i) -> p a g t i", a=PASSES, t=n, i=run),
-                    src[:].rearrange("p a c -> p (a c)").bitcast(dtype).rearrange("p (a g i t) -> p a g t i", a=PASSES, t=PACK, i=run)[:, :, :, t0:t1, :])
+            scales = w2_sc[min(t0, 1)]
+            nc.vector.tensor_copy(
+                codes[:].rearrange("p a c -> p (a c)").bitcast(U32).rearrange("p (a t g i) -> p a g t i", a=PASSES, t=n, i=4),
+                w2_raw[:].rearrange("p a c -> p (a c)").bitcast(U32).rearrange("p (a g i t) -> p a g t i", a=PASSES, t=PACK, i=4)[:, :, :, t0:t1, :])
             for t in range(t0, t1):
                 w2_q[t] = (codes, scales, t - t0)
 
@@ -105,6 +115,7 @@ def tile_list_zone_map_filter_kernel(tc, tab_words, tab_scales, offs, w1, w2_wor
 
         gains_first = placed.tile([P, BANK], F32, name="gains_first", offset=OLD_AT, align_bytes=64)
         load_gains(gains_first[:], 0, 0, BANK)
+        stage_w2_scales(1, PACK, w2_sc[1], placed, offset=W2_FIRST_AT + 512)
 
         def quantize(grouped, width, pool, name):
             codes = pool.tile([P, width], U32, name=name + "_c", align_bytes=64)

@@ -12,9 +12,11 @@ SCALE_ROWS = 4
 AHEAD = 4
 W2_FIRST_AT = T2 * 4
 TAB_AT = W2_FIRST_AT - 64
-OLD_AT = W2_FIRST_AT + 1024
+W2_LATE_AT = W2_FIRST_AT + 512
+OLD_AT = W2_LATE_AT + 768
 W2_REST_AT = OLD_AT + PACK * T2 * 4
 W1_URGENT_AT = W2_REST_AT + 1024
+W2_ZERO_AT = W2_REST_AT + 2048
 CHUNKS = [128, 128] + [256] * 6 + [128, 128]
 LAST_PLANE_CUTS = [0, 128, 256, 512, 1024]
 
@@ -42,25 +44,24 @@ def tile_list_zone_map_filter_kernel(tc, tab_words, tab_scales, offs, w1, w2_wor
         gather_list = keep.tile([P, S // 16], U16, name="gather_list")
         scatter_list = keep.tile([P, S // 16], U16, name="scatter_list")
         nc.sync.dma_start(gather_list[:], offs)
-        nc.sync.dma_start(scatter_list[:], offs2)
         late = ctx.enter_context(tc.tile_pool(name="late", bufs=1))
         tab_w0 = keep.tile([P, T], I32, name="tab_w0", tag="slot_a", align_bytes=64)
         placed = ctx.enter_context(tc.tile_pool(name="placed", bufs=1))
         tab_w1 = placed.tile([P, T], I32, name="tab_w1", offset=TAB_AT, align_bytes=64)
         w2_raw = late.tile([P, PASSES, H // 2], I32, name="w2_raw", align_bytes=64)
         tab_sc = late.tile([P, T // 4], I32, name="tab_sc", tag="slot_c", align_bytes=64)
-        nc.sync.dma_start(tab_sc[:QUAD, :], tab_scales.rearrange("a q t -> q a t").bitcast(I32))
         w2_sc_rows = late.tile([P, H // 4], I32, name="w2_sc_rows", align_bytes=64)
         nc.sync.dma_start(w2_sc_rows[:QUAD, :], w2_scales.rearrange("a q c -> q a c").bitcast(I32))
+        nc.sync.dma_start(tab_sc[:QUAD, :], tab_scales.rearrange("a q t -> q a t").bitcast(I32))
         nc.vector.memset(tab_sc[QUAD : 2 * QUAD, :], 0)
         nc.vector.memset(tab_sc[2 * QUAD :, :], 0)
+        nc.sync.dma_start(scatter_list[:], offs2)
         nc.sync.dma_start(tab_w0[:], tab_words[0].rearrange("p t i -> p (t i)").bitcast(I32))
-        nc.sync.dma_start(tab_w1[:], tab_words[1].rearrange("p t i -> p (t i)").bitcast(I32))
         nc.sync.dma_start(w2_raw[:], w2_words.rearrange("a p c -> p a c").bitcast(I32))
+        nc.sync.dma_start(tab_w1[:], tab_words[1].rearrange("p t i -> p (t i)").bitcast(I32))
 
-        w2_sc = [keep.tile([P, PASSES, n * P // 4], I32, name="w2_sc%d" % n, align_bytes=64) for n in (1, PACK - 1)]
-        for tile in w2_sc:
-            nc.vector.memset(tile[:], 0)
+        w2_sc = [keep.tile([P, PASSES, P // 4], I32, name="w2_sc0", align_bytes=64)]
+        nc.vector.memset(w2_sc[0][:], 0)
         v_sc_moved = keep.tile([P, PASSES, S // 4], I32, name="v_sc_moved", align_bytes=64)
         nc.vector.memset(v_sc_moved[:], 0)
         pages = [keep.tile([P, T2], F32, name="page0")]
@@ -71,27 +72,25 @@ def tile_list_zone_map_filter_kernel(tc, tab_words, tab_scales, offs, w1, w2_wor
             for q in (0, 2, 1, 3):
                 nc.sync.dma_start(dst[QUAD * q : QUAD * q + SCALE_ROWS, :, :], src[rows * q : rows * (q + 1), :])
 
-        def stage_w2_scales(t0, t1, dst, pool, **where):
-            staged = pool.tile([P, (t1 - t0) * P // 4], I32, name="w2_staged%d" % t0, align_bytes=64, **where)
-            nc.vector.tensor_copy(staged[:QUAD, :].bitcast(U16).rearrange("p (t g i) -> p g t i", t=t1 - t0, i=8),
-                                  w2_sc_rows[:QUAD, :].bitcast(U16).rearrange("p (g i t) -> p g t i", t=PACK, i=8)[:, :, t0:t1, :])
-            move_rows(dst, staged)
-
-        stage_w2_scales(0, 1, w2_sc[0], keep)
+        staged = keep.tile([P, H // 4], I32, name="w2_staged", align_bytes=64)
+        nc.vector.tensor_copy(staged[:QUAD, :].bitcast(U16).rearrange("p (t g i) -> p g t i", t=PACK, i=8),
+                              w2_sc_rows[:QUAD, :].bitcast(U16).rearrange("p (g i t) -> p g t i", t=PACK, i=8))
+        move_rows(w2_sc[0], staged[:, : P // 4])
 
         v_sc_rows = keep.tile([P, S], U8, name="v_sc_rows", align_bytes=64)
         nc.vector.tensor_copy(v_sc_rows[:], tab_sc[:].bitcast(U8).indirect(gather_list[:]))
         w1_rows = [w1[a * P * PACK : (a + 1) * P * PACK, :].rearrange("(p j) c -> p j c", j=PACK) for a in range(PASSES)]
         w1_raw0 = late.tile([P, PACK, H], F32, name="w1_raw0", tag="slot_c", align_bytes=64)
-        nc.sync.dma_start(w1_raw0[:], w1_rows[0])
-        move_rows(v_sc_moved, v_sc_rows[:].bitcast(I32))
+        for r in range(SCALE_ROWS):
+            for a in range(PASSES):
+                nc.sync.dma_start(v_sc_moved[r:P:QUAD, a, :], v_sc_rows[PASSES * r + a : QUAD : PASSES * SCALE_ROWS, :].bitcast(I32))
+            if r == 0:
+                nc.sync.dma_start(w1_raw0[:], w1_rows[0])
         v_sc = [v_sc_moved[:, a, :].bitcast(U8) for a in range(PASSES)]
         v_w = [keep.tile([P, S], U32, name="v_w%d" % a, align_bytes=64) for a in range(PASSES)]
         nc.vector.tensor_copy(v_w[0][:], tab_w0[:].bitcast(U32).indirect(gather_list[:]))
         w1_raw1 = keep.tile([P, PACK, H], F32, name="w1_raw1", tag="slot_a", align_bytes=64)
         nc.sync.dma_start(w1_raw1[:], w1_rows[1])
-        nc.vector.tensor_copy(v_w[1][:], tab_w1[:].bitcast(U32).indirect(gather_list[:]))
-
         w2_q = {}
 
         def prepare_w2(t0, t1, offset):
@@ -104,7 +103,9 @@ def tile_list_zone_map_filter_kernel(tc, tab_words, tab_scales, offs, w1, w2_wor
             for t in range(t0, t1):
                 w2_q[t] = (codes, scales, t - t0)
 
-        prepare_w2(0, 1, W2_FIRST_AT)
+        prepare_w2(0, 1, W2_ZERO_AT)
+
+        nc.vector.tensor_copy(v_w[1][:], tab_w1[:].bitcast(U32).indirect(gather_list[:]))
 
         def planes(rows):
             return rows.rearrange("(g t e) c -> t g e c", t=PACK, e=2)
@@ -115,7 +116,9 @@ def tile_list_zone_map_filter_kernel(tc, tab_words, tab_scales, offs, w1, w2_wor
 
         gains_first = placed.tile([P, BANK], F32, name="gains_first", offset=OLD_AT, align_bytes=64)
         load_gains(gains_first[:], 0, 0, BANK)
-        stage_w2_scales(1, PACK, w2_sc[1], placed, offset=W2_FIRST_AT + 512)
+        w2_sc.append(placed.tile([P, PASSES, (PACK - 1) * P // 4], I32, name="w2_sc1", offset=W2_LATE_AT, align_bytes=64))
+        nc.vector.memset(w2_sc[1][:], 0)
+        move_rows(w2_sc[1], staged[:, P // 4 :])
 
         def quantize(grouped, width, pool, name):
             codes = pool.tile([P, width], U32, name=name + "_c", align_bytes=64)
@@ -135,9 +138,7 @@ def tile_list_zone_map_filter_kernel(tc, tab_words, tab_scales, offs, w1, w2_wor
                 w1_q[a, t] = (codes, scales, (t - t0) * P)
 
         prepare_w1(nc.scalar.copy, w1_raw0, 0, 0, 2, keep)
-        prepare_w1(nc.scalar.copy, w1_raw0, 0, 2, 4, keep)
-        pages.append(placed.tile([P, T2], F32, name="page1", offset=0, align_bytes=64))
-        nc.vector.memset(pages[1][:], 0.0)
+        prepare_w1(nc.scalar.copy, w1_raw0, 0, 2, 4, keep, tag="slot_bias")
         gains_rest = late.tile([P, 3 * BANK], F32, name="gains_rest", tag="slot_c", align_bytes=64)
         load_gains(gains_rest[:, :BANK], 0, BANK, S)
         load_gains(gains_rest[:, BANK:], 1, 0, S)
@@ -156,7 +157,10 @@ def tile_list_zone_map_filter_kernel(tc, tab_words, tab_scales, offs, w1, w2_wor
             for a in range(PASSES):
                 nc.tensor.matmul_mx(out=acc[:], lhsT=codes[:, a, i * P // 2 : (i + 1) * P // 2].bitcast(U8).bitcast(FP4X4),
                                     lhsT_scale=scales[:, a, i * P // 4 : (i + 1) * P // 4].bitcast(U8), **moving(u, a, 0))
-            second = keep.tile([P, BANK], F32, name="second", tag="second_%d" % ((2 * t + u) % AHEAD))
+            if (t, u) == (0, 1):
+                second = placed.tile([P, BANK], F32, name="second_half", offset=0, align_bytes=64)
+            else:
+                second = keep.tile([P, BANK], F32, name="second", tag="second_%d" % ((2 * t + u) % AHEAD))
             nc.scalar.copy(second[:], acc[:])
             w2_sums[t, u] = second
 
@@ -184,8 +188,8 @@ def tile_list_zone_map_filter_kernel(tc, tab_words, tab_scales, offs, w1, w2_wor
         multiply_w1(0, 0)
         smaller(0, 0)
         prepare_w2(1, PACK, W2_REST_AT)
-        prepare_w1(nc.scalar.copy, w1_raw1, 1, 1, 2, keep, tag="slot_bias")
-        prepare_w1(nc.scalar.copy, w1_raw1, 1, 2, 4, keep, tag="slot_g")
+        prepare_w1(nc.scalar.copy, w1_raw1, 1, 1, 2, keep, tag="slot_g")
+        prepare_w1(nc.scalar.copy, w1_raw1, 1, 2, 4, placed, offset=BANK * 4)
 
         wf_raw = keep.tile([P, PACK, N], F32, name="wf_raw", tag="slot_a", align_bytes=64)
         for t in range(PACK):
@@ -211,6 +215,8 @@ def tile_list_zone_map_filter_kernel(tc, tab_words, tab_scales, offs, w1, w2_wor
         project(0, 1)
         project(1, 0)
         scatter(0, BANK, S, gains_rest[:, :BANK])
+        pages.append(placed.tile([P, T2], F32, name="page1", offset=0, align_bytes=64))
+        nc.gpsimd.memset(pages[1][:], 0.0)
         project(1, 1)
         project(2, 0)
         scatter(1, 0, S, gains_rest[:, BANK:])

@@ -17,8 +17,9 @@ OLD_AT = W2_LATE_AT + 768
 W2_REST_AT = OLD_AT + PACK * T2 * 4
 W1_URGENT_AT = W2_REST_AT + 1024
 W2_ZERO_AT = W2_REST_AT + 2048
-CHUNKS = [128, 128] + [256] * 6 + [128, 128]
-LAST_PLANE_CUTS = [0, 128, 256, 512, 1024]
+CHUNK = 256
+LEAD = 64
+LAST_PLANE_CUTS = [0, 256, 512, 1024]
 
 FLOPS = 2 * (2 * K * H * S + H * N * T2)
 
@@ -245,36 +246,39 @@ def tile_list_zone_map_filter_kernel(tc, tab_words, tab_scales, offs, w1, w2_wor
             nc.scalar.copy(page4[:, PACK - 1, c0:c1], pages[1][:, c0:c1])
 
         out_rows = out.rearrange("(p m) c -> p m c", m=PACK)
-        chunk_cols = [slice(sum(CHUNKS[:c]), sum(CHUNKS[: c + 1])) for c in range(len(CHUNKS))]
+        chunks = T2 // CHUNK
+        z_tiles = {}
 
-        def lower(c):
-            z = ring.tile([P, PACK * CHUNKS[c]], BF16, name="z", align_bytes=64)
-            nc.vector.tensor_tensor(z[:].rearrange("p (c i t) -> p c t i", i=2, t=PACK),
-                                    page4[:, :, chunk_cols[c]].rearrange("p t (c i) -> p c t i", i=2),
-                                    old_sb[:, :, chunk_cols[c]].rearrange("p t (c i) -> p c t i", i=2), ALU.min)
-            return z
+        def lower(c, c0, c1):
+            if c0 == 0:
+                z_tiles[c] = ring.tile([P, PACK * CHUNK], BF16, name="z", align_bytes=64)
+            cols = slice(c * CHUNK + c0, c * CHUNK + c1)
+            nc.vector.tensor_tensor(z_tiles[c][:, PACK * c0 : PACK * c1].rearrange("p (c i t) -> p c t i", i=2, t=PACK),
+                                    page4[:, :, cols].rearrange("p t (c i) -> p c t i", i=2),
+                                    old_sb[:, :, cols].rearrange("p t (c i) -> p c t i", i=2), ALU.min)
 
         bank_tags = [["bank_out_0", "bank_out_1", "bank_w2_0", "bank_w2_1"], ["bank_w1_%d" % m for m in range(AHEAD)]]
 
-        def apply_filters(c, z):
-            w = CHUNKS[c]
-            z_c, z_s = quantize(z[:], w, ring, "zq")
-            res = late.tile([P, PACK, w], F32, name="res", bufs=8, align_bytes=64)
+        def apply_filters(c):
+            cols = slice(c * CHUNK, (c + 1) * CHUNK)
+            z_c, z_s = quantize(z_tiles[c][:], CHUNK, ring, "zq")
+            res = late.tile([P, PACK, CHUNK], F32, name="res", bufs=8, align_bytes=64)
             for m in range(PACK):
                 rows = slice(m * P, (m + 1) * P)
                 acc = psum.tile([P, BANK], F32, name="acc", tag=bank_tags[c % 2][m])
-                nc.tensor.matmul_mx(out=acc[:, :w], lhsT=wf_c[:, rows].bitcast(FP8X4), lhsT_scale=wf_s[:, rows],
+                nc.tensor.matmul_mx(out=acc[:, :CHUNK], lhsT=wf_c[:, rows].bitcast(FP8X4), lhsT_scale=wf_s[:, rows],
                                     rhs=z_c[:].bitcast(FP8X4), rhs_scale=z_s[:], start=True, stop=True)
-                if c == len(CHUNKS) - 1 and m % 2 == 1:
-                    nc.vector.tensor_scalar(res[:, m, :], acc[:, :w], bias[:, m : m + 1], 0.0, ALU.add, ALU.max)
+                if c == chunks - 1 and m % 2 == 1:
+                    nc.vector.tensor_scalar(res[:, m, :], acc[:, :CHUNK], bias[:, m : m + 1], 0.0, ALU.add, ALU.max)
                 else:
-                    nc.scalar.activation(res[:, m, :], acc[:, :w], ACT.Relu, bias=bias[:, m : m + 1])
+                    nc.scalar.activation(res[:, m, :], acc[:, :CHUNK], ACT.Relu, bias=bias[:, m : m + 1])
                 if m % 2 == 1:
-                    nc.sync.dma_start(out_rows[:, m - 1 : m + 1, chunk_cols[c]], res[:, m - 1 : m + 1, :])
+                    nc.sync.dma_start(out_rows[:, m - 1 : m + 1, cols], res[:, m - 1 : m + 1, :])
 
-        z_next = lower(0)
-        for c in range(len(CHUNKS)):
-            z_now = z_next
-            if c + 1 < len(CHUNKS):
-                z_next = lower(c + 1)
-            apply_filters(c, z_now)
+        lower(0, 0, CHUNK)
+        for c in range(chunks):
+            if c + 1 < chunks:
+                lower(c + 1, 0, LEAD)
+            apply_filters(c)
+            if c + 1 < chunks:
+                lower(c + 1, LEAD, CHUNK)

@@ -18,7 +18,7 @@ W2_REST_AT = OLD_AT + PACK * T2 * 4
 W1_URGENT_AT = W2_REST_AT + 1024
 W2_ZERO_AT = W2_REST_AT + 2048
 CHUNK = 256
-LEAD = 64
+LEAD = 96
 LAST_PLANE_CUTS = [0, 256, 512, 1024]
 
 FLOPS = 2 * (2 * K * H * S + H * N * T2)
@@ -272,7 +272,9 @@ def tile_list_zone_map_filter_kernel(tc, tab_words, tab_scales, offs, w1, w2_wor
                     nc.vector.tensor_scalar(res[:, m, :], acc[:, :CHUNK], bias[:, m : m + 1], 0.0, ALU.add, ALU.max)
                 else:
                     nc.scalar.activation(res[:, m, :], acc[:, :CHUNK], ACT.Relu, bias=bias[:, m : m + 1])
-                if m % 2 == 1:
+                if c < chunks - 1:
+                    nc.sync.dma_start(out_rows[:, m, cols], res[:, m, :])
+                elif m % 2 == 1:
                     nc.sync.dma_start(out_rows[:, m - 1 : m + 1, cols], res[:, m - 1 : m + 1, :])
 
         lower(0, 0, CHUNK)

@@ -51,9 +51,9 @@ def tile_list_zone_map_filter_kernel(tc, tab_words, tab_scales, offs, w1, w2_wor
         tab_w1 = placed.tile([P, T], I32, name="tab_w1", offset=TAB_AT, align_bytes=64)
         w2_raw = late.tile([P, PASSES, H // 2], I32, name="w2_raw", align_bytes=64)
         tab_sc = late.tile([P, T // 4], I32, name="tab_sc", tag="slot_c", align_bytes=64)
-        w2_sc_rows = late.tile([P, H // 4], I32, name="w2_sc_rows", align_bytes=64)
-        nc.sync.dma_start(w2_sc_rows[:QUAD, :], w2_scales.rearrange("a q c -> q a c").bitcast(I32))
+        w2_sc_rows = late.tile([P, H // 4], I32, name="w2_sc_rows", tag="slot_page", align_bytes=64)
         nc.sync.dma_start(tab_sc[:QUAD, :], tab_scales.rearrange("a q t -> q a t").bitcast(I32))
+        nc.sync.dma_start(w2_sc_rows[:QUAD, :], w2_scales.rearrange("a q c -> q a c").bitcast(I32))
         nc.vector.memset(tab_sc[QUAD : 2 * QUAD, :], 0)
         nc.vector.memset(tab_sc[2 * QUAD :, :], 0)
         nc.sync.dma_start(scatter_list[:], offs2)
@@ -65,8 +65,6 @@ def tile_list_zone_map_filter_kernel(tc, tab_words, tab_scales, offs, w1, w2_wor
         nc.vector.memset(w2_sc[0][:], 0)
         v_sc_moved = keep.tile([P, PASSES, S // 4], I32, name="v_sc_moved", align_bytes=64)
         nc.vector.memset(v_sc_moved[:], 0)
-        pages = [keep.tile([P, T2], F32, name="page0")]
-        nc.vector.memset(pages[0][:], 0.0)
 
         def move_rows(dst, src):
             rows = PASSES * SCALE_ROWS
@@ -74,9 +72,11 @@ def tile_list_zone_map_filter_kernel(tc, tab_words, tab_scales, offs, w1, w2_wor
                 nc.sync.dma_start(dst[QUAD * q : QUAD * q + SCALE_ROWS, :, :], src[rows * q : rows * (q + 1), :])
 
         staged = keep.tile([P, H // 4], I32, name="w2_staged", align_bytes=64)
-        nc.vector.tensor_copy(staged[:QUAD, :].bitcast(U16).rearrange("p (t g i) -> p g t i", t=PACK, i=8),
-                              w2_sc_rows[:QUAD, :].bitcast(U16).rearrange("p (g i t) -> p g t i", t=PACK, i=8))
+        nc.scalar.copy(staged[:QUAD, :].bitcast(U16).rearrange("p (t g) -> p t g", t=PACK),
+                       w2_sc_rows[:QUAD, :].bitcast(U16).rearrange("p (g t) -> p t g", t=PACK))
         move_rows(w2_sc[0], staged[:, : P // 4])
+        pages = [late.tile([P, T2], F32, name="page0", tag="slot_page", align_bytes=64)]
+        nc.gpsimd.memset(pages[0][:], 0.0)
 
         v_sc_rows = keep.tile([P, S], U8, name="v_sc_rows", align_bytes=64)
         nc.vector.tensor_copy(v_sc_rows[:], tab_sc[:].bitcast(U8).indirect(gather_list[:]))
@@ -94,17 +94,17 @@ def tile_list_zone_map_filter_kernel(tc, tab_words, tab_scales, offs, w1, w2_wor
         nc.sync.dma_start(w1_raw1[:], w1_rows[1])
         w2_q = {}
 
-        def prepare_w2(t0, t1, offset):
+        def prepare_w2(copy, t0, t1, offset):
             n = t1 - t0
             codes = placed.tile([P, PASSES, n * P // 2], I32, name="w2_c%d" % t0, offset=offset, align_bytes=64)
             scales = w2_sc[min(t0, 1)]
-            nc.vector.tensor_copy(
+            copy(
                 codes[:].rearrange("p a c -> p (a c)").bitcast(U32).rearrange("p (a t g i) -> p a g t i", a=PASSES, t=n, i=4),
                 w2_raw[:].rearrange("p a c -> p (a c)").bitcast(U32).rearrange("p (a g i t) -> p a g t i", a=PASSES, t=PACK, i=4)[:, :, :, t0:t1, :])
             for t in range(t0, t1):
                 w2_q[t] = (codes, scales, t - t0)
 
-        prepare_w2(0, 1, W2_ZERO_AT)
+        prepare_w2(nc.scalar.copy, 0, 1, W2_ZERO_AT)
 
         nc.vector.tensor_copy(v_w[1][:], tab_w1[:].bitcast(U32).indirect(gather_list[:]))
 
@@ -188,7 +188,7 @@ def tile_list_zone_map_filter_kernel(tc, tab_words, tab_scales, offs, w1, w2_wor
         prepare_w1(nc.vector.tensor_copy, w1_raw1, 1, 0, 1, placed, offset=W1_URGENT_AT)
         multiply_w1(0, 0)
         smaller(0, 0)
-        prepare_w2(1, PACK, W2_REST_AT)
+        prepare_w2(nc.vector.tensor_copy, 1, PACK, W2_REST_AT)
         prepare_w1(nc.scalar.copy, w1_raw1, 1, 1, 2, keep, tag="slot_g")
         prepare_w1(nc.scalar.copy, w1_raw1, 1, 2, 4, placed, offset=BANK * 4)
 

@@ -17,9 +17,9 @@ OLD_AT = W2_LATE_AT + 768
 W2_REST_AT = OLD_AT + PACK * T2 * 4
 W1_URGENT_AT = W2_REST_AT + 1024
 W2_ZERO_AT = W2_REST_AT + 2048
-CHUNK = 256
-LEAD = 96
-LAST_PLANE_CUTS = [0, 256, 512, 1024]
+CHUNKS = [128, 128] + [256] * 7
+LEAD = 128
+LAST_PLANE_CUTS = [0, 128, 256, 512, 1024]
 
 FLOPS = 2 * (2 * K * H * S + H * N * T2)
 
@@ -246,41 +246,45 @@ def tile_list_zone_map_filter_kernel(tc, tab_words, tab_scales, offs, w1, w2_wor
             nc.scalar.copy(page4[:, PACK - 1, c0:c1], pages[1][:, c0:c1])
 
         out_rows = out.rearrange("(p m) c -> p m c", m=PACK)
-        chunks = T2 // CHUNK
+        chunks = len(CHUNKS)
+        starts = [sum(CHUNKS[:c]) for c in range(chunks + 1)]
         z_tiles = {}
 
         def lower(c, c0, c1):
             if c0 == 0:
-                z_tiles[c] = ring.tile([P, PACK * CHUNK], BF16, name="z", align_bytes=64)
-            cols = slice(c * CHUNK + c0, c * CHUNK + c1)
+                z_tiles[c] = ring.tile([P, PACK * CHUNKS[c]], BF16, name="z", align_bytes=64)
+            cols = slice(starts[c] + c0, starts[c] + c1)
             nc.vector.tensor_tensor(z_tiles[c][:, PACK * c0 : PACK * c1].rearrange("p (c i t) -> p c t i", i=2, t=PACK),
                                     page4[:, :, cols].rearrange("p t (c i) -> p c t i", i=2),
                                     old_sb[:, :, cols].rearrange("p t (c i) -> p c t i", i=2), ALU.min)
 
         bank_tags = [["bank_out_0", "bank_out_1", "bank_w2_0", "bank_w2_1"], ["bank_w1_%d" % m for m in range(AHEAD)]]
+        res = [late.tile([P, 2, T2], F32, name="res%d" % h, align_bytes=64) for h in range(2)]
+        stored = [0, 0]
 
         def apply_filters(c):
-            cols = slice(c * CHUNK, (c + 1) * CHUNK)
-            z_c, z_s = quantize(z_tiles[c][:], CHUNK, ring, "zq")
-            res = late.tile([P, PACK, CHUNK], F32, name="res", bufs=8, align_bytes=64)
+            w = CHUNKS[c]
+            cols = slice(starts[c], starts[c + 1])
+            z_c, z_s = quantize(z_tiles[c][:], w, ring, "zq")
             for m in range(PACK):
                 rows = slice(m * P, (m + 1) * P)
+                h = m // 2
                 acc = psum.tile([P, BANK], F32, name="acc", tag=bank_tags[c % 2][m])
-                nc.tensor.matmul_mx(out=acc[:, :CHUNK], lhsT=wf_c[:, rows].bitcast(FP8X4), lhsT_scale=wf_s[:, rows],
+                nc.tensor.matmul_mx(out=acc[:, :w], lhsT=wf_c[:, rows].bitcast(FP8X4), lhsT_scale=wf_s[:, rows],
                                     rhs=z_c[:].bitcast(FP8X4), rhs_scale=z_s[:], start=True, stop=True)
                 if c == chunks - 1 and m % 2 == 1:
-                    nc.vector.tensor_scalar(res[:, m, :], acc[:, :CHUNK], bias[:, m : m + 1], 0.0, ALU.add, ALU.max)
+                    nc.vector.tensor_scalar(res[h][:, m % 2, cols], acc[:, :w], bias[:, m : m + 1], 0.0, ALU.add, ALU.max)
                 else:
-                    nc.scalar.activation(res[:, m, :], acc[:, :CHUNK], ACT.Relu, bias=bias[:, m : m + 1])
-                if c < chunks - 1:
-                    nc.sync.dma_start(out_rows[:, m, cols], res[:, m, :])
-                elif m % 2 == 1:
-                    nc.sync.dma_start(out_rows[:, m - 1 : m + 1, cols], res[:, m - 1 : m + 1, :])
+                    nc.scalar.activation(res[h][:, m % 2, cols], acc[:, :w], ACT.Relu, bias=bias[:, m : m + 1])
+                if m % 2 == 1 and (c % 2 == h or c >= chunks - 3):
+                    span = slice(stored[h], starts[c + 1])
+                    nc.sync.dma_start(out_rows[:, m - 1 : m + 1, span], res[h][:, :, span])
+                    stored[h] = starts[c + 1]
 
-        lower(0, 0, CHUNK)
+        lower(0, 0, CHUNKS[0])
         for c in range(chunks):
             if c + 1 < chunks:
-                lower(c + 1, 0, LEAD)
+                lower(c + 1, 0, min(LEAD, CHUNKS[c + 1]))
             apply_filters(c)
-            if c + 1 < chunks:
-                lower(c + 1, LEAD, CHUNK)
+            if c + 1 < chunks and LEAD < CHUNKS[c + 1]:
+                lower(c + 1, LEAD, CHUNKS[c + 1])

@@ -17,7 +17,7 @@ OLD_AT = W2_LATE_AT + 768
 W2_REST_AT = OLD_AT + PACK * T2 * 4
 W1_URGENT_AT = W2_REST_AT + 1024
 W2_ZERO_AT = W2_REST_AT + 2048
-CHUNKS = [128, 128] + [256] * 7
+CHUNKS = [128, 128] + [256] * 6 + [128, 128]
 LEAD = 128
 LAST_PLANE_CUTS = [0, 128, 256, 512, 1024]
 
@@ -259,27 +259,23 @@ def tile_list_zone_map_filter_kernel(tc, tab_words, tab_scales, offs, w1, w2_wor
                                     old_sb[:, :, cols].rearrange("p t (c i) -> p c t i", i=2), ALU.min)
 
         bank_tags = [["bank_out_0", "bank_out_1", "bank_w2_0", "bank_w2_1"], ["bank_w1_%d" % m for m in range(AHEAD)]]
-        res = [late.tile([P, 2, T2], F32, name="res%d" % h, align_bytes=64) for h in range(2)]
-        stored = [0, 0]
 
         def apply_filters(c):
             w = CHUNKS[c]
             cols = slice(starts[c], starts[c + 1])
             z_c, z_s = quantize(z_tiles[c][:], w, ring, "zq")
+            res = late.tile([P, PACK, w], F32, name="res", bufs=8, align_bytes=64)
             for m in range(PACK):
                 rows = slice(m * P, (m + 1) * P)
-                h = m // 2
                 acc = psum.tile([P, BANK], F32, name="acc", tag=bank_tags[c % 2][m])
                 nc.tensor.matmul_mx(out=acc[:, :w], lhsT=wf_c[:, rows].bitcast(FP8X4), lhsT_scale=wf_s[:, rows],
                                     rhs=z_c[:].bitcast(FP8X4), rhs_scale=z_s[:], start=True, stop=True)
                 if c == chunks - 1 and m % 2 == 1:
-                    nc.vector.tensor_scalar(res[h][:, m % 2, cols], acc[:, :w], bias[:, m : m + 1], 0.0, ALU.add, ALU.max)
+                    nc.vector.tensor_scalar(res[:, m, :], acc[:, :w], bias[:, m : m + 1], 0.0, ALU.add, ALU.max)
                 else:
-                    nc.scalar.activation(res[h][:, m % 2, cols], acc[:, :w], ACT.Relu, bias=bias[:, m : m + 1])
-                if m % 2 == 1 and (c % 2 == h or c >= chunks - 3):
-                    span = slice(stored[h], starts[c + 1])
-                    nc.sync.dma_start(out_rows[:, m - 1 : m + 1, span], res[h][:, :, span])
-                    stored[h] = starts[c + 1]
+                    nc.scalar.activation(res[:, m, :], acc[:, :w], ACT.Relu, bias=bias[:, m : m + 1])
+                if m % 2 == 1:
+                    nc.sync.dma_start(out_rows[:, m - 1 : m + 1, cols], res[:, m - 1 : m + 1, :])
 
         lower(0, 0, CHUNKS[0])
         for c in range(chunks):

from contextlib import ExitStack

import concourse.mybir as mybir

K, T, S, T2, H, N = 1024, 2048, 1024, 2048, 512, 512
P = 128
PACK = 4
PASSES = K // (P * PACK)
BANK = 512
QUAD = 32
SCALE_ROWS = 4
AHEAD = 4
W2_FIRST_AT = T2 * 4
TAB_AT = W2_FIRST_AT - 64
W2_LATE_AT = W2_FIRST_AT + 512
OLD_AT = W2_LATE_AT + 768
W2_REST_AT = OLD_AT + PACK * T2 * 4
W1_URGENT_AT = W2_REST_AT + 1024
W2_ZERO_AT = W2_REST_AT + 2048
CHUNKS = [128, 128] + [256] * 6 + [128, 128]
LEAD = 128
LAST_PLANE_CUTS = [0, 128, 256, 512, 1024]

FLOPS = 2 * (2 * K * H * S + H * N * T2)

F32 = mybir.dt.float32
BF16 = mybir.dt.bfloat16
I32 = mybir.dt.int32
U32 = mybir.dt.uint32
U16 = mybir.dt.uint16
U8 = mybir.dt.uint8
FP8X4 = mybir.dt.float8_e4m3fn_x4
FP4X4 = mybir.dt.float4_e2m1fn_x4
ALU = mybir.AluOpType
ACT = mybir.ActivationFunctionType


def tile_list_zone_map_filter_kernel(tc, tab_words, tab_scales, offs, w1, w2_words, w2_scales, wgs, offs2, old, wf, bf, out):
    nc = tc.nc
    with ExitStack() as ctx:
        keep = ctx.enter_context(tc.tile_pool(name="keep", bufs=1))
        ring = ctx.enter_context(tc.tile_pool(name="ring", bufs=3))
        psum = ctx.enter_context(tc.psum_pool(name="psum", bufs=1))

        gather_list = keep.tile([P, S // 16], U16, name="gather_list")
        scatter_list = keep.tile([P, S // 16], U16, name="scatter_list")
        nc.sync.dma_start(gather_list[:], offs)
        late = ctx.enter_context(tc.tile_pool(name="late", bufs=1))
        tab_w0 = keep.tile([P, T], I32, name="tab_w0", tag="slot_a", align_bytes=64)
        placed = ctx.enter_context(tc.tile_pool(name="placed", bufs=1))
        tab_w1 = placed.tile([P, T], I32, name="tab_w1", offset=TAB_AT, align_bytes=64)
        w2_raw = late.tile([P, PASSES, H // 2], I32, name="w2_raw", align_bytes=64)
        tab_sc = late.tile([P, T // 4], I32, name="tab_sc", tag="slot_c", align_bytes=64)
        w2_sc_rows = late.tile([P, H // 4], I32, name="w2_sc_rows", tag="slot_page", align_bytes=64)
        nc.sync.dma_start(tab_sc[:QUAD, :], tab_scales.rearrange("a q t -> q a t").bitcast(I32))
        nc.sync.dma_start(w2_sc_rows[:QUAD, :], w2_scales.rearrange("a q c -> q a c").bitcast(I32))
        nc.vector.memset(tab_sc[QUAD : 2 * QUAD, :], 0)
        nc.vector.memset(tab_sc[2 * QUAD :, :], 0)
        nc.sync.dma_start(scatter_list[:], offs2)
        nc.sync.dma_start(tab_w0[:], tab_words[0].rearrange("p t i -> p (t i)").bitcast(I32))
        nc.sync.dma_start(w2_raw[:], w2_words.rearrange("a p c -> p a c").bitcast(I32))
        nc.sync.dma_start(tab_w1[:], tab_words[1].rearrange("p t i -> p (t i)").bitcast(I32))

        w2_sc = [keep.tile([P, PASSES, P // 4], I32, name="w2_sc0", align_bytes=64)]
        nc.vector.memset(w2_sc[0][:], 0)
        v_sc_moved = keep.tile([P, PASSES, S // 4], I32, name="v_sc_moved", align_bytes=64)
        nc.vector.memset(v_sc_moved[:], 0)

        def move_rows(dst, src):
            rows = PASSES * SCALE_ROWS
            for q in (0, 2, 1, 3):
                nc.sync.dma_start(dst[QUAD * q : QUAD * q + SCALE_ROWS, :, :], src[rows * q : rows * (q + 1), :])

        staged = keep.tile([P, H // 4], I32, name="w2_staged", align_bytes=64)
        nc.scalar.copy(staged[:QUAD, :].bitcast(U16).rearrange("p (t g) -> p t g", t=PACK),
                       w2_sc_rows[:QUAD, :].bitcast(U16).rearrange("p (g t) -> p t g", t=PACK))
        move_rows(w2_sc[0], staged[:, : P // 4])
        pages = [late.tile([P, T2], F32, name="page0", tag="slot_page", align_bytes=64)]
        nc.gpsimd.memset(pages[0][:], 0.0)

        v_sc_rows = keep.tile([P, S], U8, name="v_sc_rows", align_bytes=64)
        nc.vector.tensor_copy(v_sc_rows[:], tab_sc[:].bitcast(U8).indirect(gather_list[:]))
        w1_rows = [w1[a * P * PACK : (a + 1) * P * PACK, :].rearrange("(p j) c -> p j c", j=PACK) for a in range(PASSES)]
        w1_raw0 = late.tile([P, PACK, H], F32, name="w1_raw0", tag="slot_c", align_bytes=64)
        for r in range(SCALE_ROWS):
            for a in range(PASSES):
                nc.sync.dma_start(v_sc_moved[r:P:QUAD, a, :], v_sc_rows[PASSES * r + a : QUAD : PASSES * SCALE_ROWS, :].bitcast(I32))
            if r == 0:
                nc.sync.dma_start(w1_raw0[:], w1_rows[0])
        v_sc = [v_sc_moved[:, a, :].bitcast(U8) for a in range(PASSES)]
        v_w = [keep.tile([P, S], U32, name="v_w%d" % a, align_bytes=64) for a in range(PASSES)]
        nc.vector.tensor_copy(v_w[0][:], tab_w0[:].bitcast(U32).indirect(gather_list[:]))
        w1_raw1 = keep.tile([P, PACK, H], F32, name="w1_raw1", tag="slot_a", align_bytes=64)
        nc.sync.dma_start(w1_raw1[:], w1_rows[1])
        w2_q = {}

        def prepare_w2(copy, t0, t1, offset):
            n = t1 - t0
            codes = placed.tile([P, PASSES, n * P // 2], I32, name="w2_c%d" % t0, offset=offset, align_bytes=64)
            scales = w2_sc[min(t0, 1)]
            copy(
                codes[:].rearrange("p a c -> p (a c)").bitcast(U32).rearrange("p (a t g i) -> p a g t i", a=PASSES, t=n, i=4),
                w2_raw[:].rearrange("p a c -> p (a c)").bitcast(U32).rearrange("p (a g i t) -> p a g t i", a=PASSES, t=PACK, i=4)[:, :, :, t0:t1, :])
            for t in range(t0, t1):
                w2_q[t] = (codes, scales, t - t0)

        prepare_w2(nc.scalar.copy, 0, 1, W2_ZERO_AT)

        nc.vector.tensor_copy(v_w[1][:], tab_w1[:].bitcast(U32).indirect(gather_list[:]))

        def planes(rows):
            return rows.rearrange("(g t e) c -> t g e c", t=PACK, e=2)

        def load_gains(gains, t, j0, j1):
            for q in (0, 2, 1, 3):
                nc.sync.dma_start(gains[QUAD * q : QUAD * (q + 1), :], planes(wgs)[t][:, :, j0:j1])

        gains_first = placed.tile([P, BANK], F32, name="gains_first", offset=OLD_AT, align_bytes=64)
        load_gains(gains_first[:], 0, 0, BANK)
        w2_sc.append(placed.tile([P, PASSES, (PACK - 1) * P // 4], I32, name="w2_sc1", offset=W2_LATE_AT, align_bytes=64))
        nc.vector.memset(w2_sc[1][:], 0)
        move_rows(w2_sc[1], staged[:, P // 4 :])

        def quantize(grouped, width, pool, name):
            codes = pool.tile([P, width], U32, name=name + "_c", align_bytes=64)
            scales = pool.tile([P, width], U8, name=name + "_s", align_bytes=64)
            nc.vector.quantize_mx(out=codes[:].bitcast(FP8X4), scales=scales[:], in_=grouped)
            return codes, scales

        w1_q = {}

        def prepare_w1(copy, raw, a, t0, t1, pool, **where):
            name = "w1_%d_%d" % (a, t0)
            grouped = pool.tile([P, (t1 - t0) * H], BF16, name=name + "_g", align_bytes=64, **where)
            copy(grouped[:].rearrange("p (t g e j) -> p g t j e", t=t1 - t0, e=2, j=PACK),
                 raw[:].rearrange("p j (g t e) -> p g t j e", t=PACK, e=2)[:, :, t0:t1, :, :])
            codes, scales = quantize(grouped[:], (t1 - t0) * P, keep, name)
            for t in range(t0, t1):
                w1_q[a, t] = (codes, scales, (t - t0) * P)

        prepare_w1(nc.scalar.copy, w1_raw0, 0, 0, 2, keep)
        prepare_w1(nc.scalar.copy, w1_raw0, 0, 2, 4, keep, tag="slot_bias")
        gains_rest = late.tile([P, 3 * BANK], F32, name="gains_rest", tag="slot_c", align_bytes=64)
        load_gains(gains_rest[:, :BANK], 0, BANK, S)
        load_gains(gains_rest[:, BANK:], 1, 0, S)

        h_tiles = {}
        w1_sums = {}
        w2_sums = {}

        def moving(u, a, first):
            cols = slice(u * BANK, (u + 1) * BANK)
            return dict(rhs=v_w[a][:, cols].bitcast(FP8X4), rhs_scale=v_sc[a][:, cols], start=(a == first), stop=(a != first))

        def multiply_w2(t, u):
            acc = psum.tile([P, BANK], F32, name="acc_w2", tag="bank_w2_%d" % u)
            codes, scales, i = w2_q[t]
            for a in range(PASSES):
                nc.tensor.matmul_mx(out=acc[:], lhsT=codes[:, a, i * P // 2 : (i + 1) * P // 2].bitcast(U8).bitcast(FP4X4),
                                    lhsT_scale=scales[:, a, i * P // 4 : (i + 1) * P // 4].bitcast(U8), **moving(u, a, 0))
            if (t, u) == (0, 1):
                second = placed.tile([P, BANK], F32, name="second_half", offset=0, align_bytes=64)
            else:
                second = keep.tile([P, BANK], F32, name="second", tag="second_%d" % ((2 * t + u) % AHEAD))
            nc.scalar.copy(second[:], acc[:])
            w2_sums[t, u] = second

        def multiply_w1(t, u):
            acc = psum.tile([P, BANK], F32, name="acc_w1", tag="bank_w1_%d" % ((2 * t + u) % AHEAD))
            first = 0 if (t, u) == (0, 0) else 1
            for a in (first, 1 - first):
                codes, scales, m0 = w1_q[a, t]
                nc.tensor.matmul_mx(out=acc[:], lhsT=codes[:, m0 : m0 + P].bitcast(FP8X4), lhsT_scale=scales[:, m0 : m0 + P],
                                    **moving(u, a, first))
            w1_sums[t, u] = acc

        def smaller(t, u):
            if u == 0:
                h_tiles[t] = ring.tile([P, S], F32, name="h", bufs=2)
            nc.vector.tensor_tensor(h_tiles[t][:, u * BANK : (u + 1) * BANK], w1_sums[t, u][:], w2_sums[t, u][:], ALU.min)

        def project(t, u):
            multiply_w2(t, u)
            multiply_w1(t, u)
            smaller(t, u)

        multiply_w2(0, 0)
        prepare_w1(nc.vector.tensor_copy, w1_raw1, 1, 0, 1, placed, offset=W1_URGENT_AT)
        multiply_w1(0, 0)
        smaller(0, 0)
        prepare_w2(nc.vector.tensor_copy, 1, PACK, W2_REST_AT)
        prepare_w1(nc.scalar.copy, w1_raw1, 1, 1, 2, keep, tag="slot_g")
        prepare_w1(nc.scalar.copy, w1_raw1, 1, 2, 4, placed, offset=BANK * 4)

        wf_raw = keep.tile([P, PACK, N], F32, name="wf_raw", tag="slot_a", align_bytes=64)
        for t in range(PACK):
            nc.sync.dma_start(wf_raw[:, t, :], planes(wf)[t])
        gains_hi = keep.tile([P, 2, S], F32, name="gains_hi", tag="slot_g", align_bytes=64)
        load_gains(gains_hi[:, 0, :], 2, 0, S)
        load_gains(gains_hi[:, 1, :], 3, 0, S)

        def scatter(t, j0, j1, gains):
            if (t, j0) == (0, 0):
                nc.vector.tensor_tensor(pages[0][:].indirect(scatter_list[:, j0 // 16 : j1 // 16]), h_tiles[t][:, j0:j1], gains, ALU.mult)
                return
            scaled = ring.tile([P, j1 - j0], F32, name="scaled", bufs=2)
            for c0 in range(0, j1 - j0, BANK):
                nc.gpsimd.tensor_tensor(scaled[:, c0 : c0 + BANK], h_tiles[t][:, j0 + c0 : j0 + c0 + BANK], gains[:, c0 : c0 + BANK], ALU.mult)
            nc.vector.tensor_copy(pages[t % 2][:].indirect(scatter_list[:, j0 // 16 : j1 // 16]), scaled[:])

        scatter(0, 0, BANK, gains_first[:])
        old_sb = placed.tile([P, PACK, T2], F32, name="old_sb", offset=OLD_AT, align_bytes=64)
        for cols in (slice(0, T2 // 2), slice(T2 // 2, T2)):
            for t in range(PACK):
                nc.sync.dma_start(old_sb[:, t, cols], planes(old)[t][:, :, cols])
        project(0, 1)
        project(1, 0)
        scatter(0, BANK, S, gains_rest[:, :BANK])
        pages.append(placed.tile([P, T2], F32, name="page1", offset=0, align_bytes=64))
        nc.gpsimd.memset(pages[1][:], 0.0)
        project(1, 1)
        project(2, 0)
        scatter(1, 0, S, gains_rest[:, BANK:])
        project(2, 1)
        project(3, 0)
        project(3, 1)
        bias = keep.tile([P, PACK], F32, name="bias", tag="slot_bias", align_bytes=64)
        nc.sync.dma_start(bias[:], bf.rearrange("(p m) -> p m", m=PACK))
        wf_g = keep.tile([P, PACK * N], BF16, name="wf_g", align_bytes=64)
        for q in range(4):
            cols = slice(QUAD * q, QUAD * (q + 1))
            nc.scalar.copy(wf_g[:].rearrange("p (m c j) -> p c m j", m=PACK, j=PACK)[:, cols],
                           wf_raw[:].rearrange("p j (c m) -> p c m j", m=PACK)[:, cols])
        page4 = keep.tile([P, PACK, T2], F32, name="page4", tag="slot_a", align_bytes=64)
        nc.scalar.copy(page4[:, 0, :], pages[0][:])
        scatter(2, 0, S, gains_hi[:, 0, :])
        nc.scalar.copy(page4[:, 1, :], pages[1][:])
        scatter(3, 0, S, gains_hi[:, 1, :])
        nc.scalar.copy(page4[:, 2, :], pages[0][:])
        wf_c = keep.tile([P, N], U32, name="wf_c", tag="slot_g", align_bytes=64)
        wf_s = keep.tile([P, N], U8, name="wf_s", align_bytes=64)
        nc.vector.quantize_mx(out=wf_c[:].bitcast(FP8X4), scales=wf_s[:], in_=wf_g[:])

        nc.sync.dma_start(page4[:, PACK - 1, LAST_PLANE_CUTS[-1] :], pages[1][:, LAST_PLANE_CUTS[-1] :])
        for c0, c1 in zip(LAST_PLANE_CUTS, LAST_PLANE_CUTS[1:]):
            nc.scalar.copy(page4[:, PACK - 1, c0:c1], pages[1][:, c0:c1])

        out_rows = out.rearrange("(p m) c -> p m c", m=PACK)
        chunks = len(CHUNKS)
        starts = [sum(CHUNKS[:c]) for c in range(chunks + 1)]
        z_tiles = {}

        def lower(c, c0, c1):
            if c0 == 0:
                z_tiles[c] = ring.tile([P, PACK * CHUNKS[c]], BF16, name="z", align_bytes=64)
            cols = slice(starts[c] + c0, starts[c] + c1)
            nc.vector.tensor_tensor(z_tiles[c][:, PACK * c0 : PACK * c1].rearrange("p (c i t) -> p c t i", i=2, t=PACK),
                                    page4[:, :, cols].rearrange("p t (c i) -> p c t i", i=2),
                                    old_sb[:, :, cols].rearrange("p t (c i) -> p c t i", i=2), ALU.min)

        bank_tags = [["bank_out_0", "bank_out_1", "bank_w2_0", "bank_w2_1"], ["bank_w1_%d" % m for m in range(AHEAD)]]

        def apply_filters(c):
            w = CHUNKS[c]
            cols = slice(starts[c], starts[c + 1])
            z_c, z_s = quantize(z_tiles[c][:], w, ring, "zq")
            res = late.tile([P, PACK, w], F32, name="res", bufs=8, align_bytes=64)
            for m in range(PACK):
                rows = slice(m * P, (m + 1) * P)
                acc = psum.tile([P, BANK], F32, name="acc", tag=bank_tags[c % 2][m])
                nc.tensor.matmul_mx(out=acc[:, :w], lhsT=wf_c[:, rows].bitcast(FP8X4), lhsT_scale=wf_s[:, rows],
                                    rhs=z_c[:].bitcast(FP8X4), rhs_scale=z_s[:], start=True, stop=True)
                if c == chunks - 1 and m % 2 == 1:
                    nc.vector.tensor_scalar(res[:, m, :], acc[:, :w], bias[:, m : m + 1], 0.0, ALU.add, ALU.max)
                else:
                    nc.scalar.activation(res[:, m, :], acc[:, :w], ACT.Relu, bias=bias[:, m : m + 1])
                if m % 2 == 1:
                    nc.sync.dma_start(out_rows[:, m - 1 : m + 1, cols], res[:, m - 1 : m + 1, :])

        lower(0, 0, CHUNKS[0])
        for c in range(chunks):
            if c + 1 < chunks:
                lower(c + 1, 0, min(LEAD, CHUNKS[c + 1]))
            apply_filters(c)
            if c + 1 < chunks and LEAD < CHUNKS[c + 1]:
                lower(c + 1, LEAD, CHUNKS[c + 1])
